import numpy as np, ml_dtypes
CORES = [10,34,74,98]
N = 4
import mx_ref
BF = ml_dtypes.bfloat16
def gcols(t, e):
    v = np.concatenate([t.reshape(8, 16, -1, 4), np.zeros((8, 16, 1, 4), BF)], axis=2)
    return np.ascontiguousarray(np.stack([v[g][:, e[g]] for g in range(8)])).reshape(128, -1)
def tile(rs):
    return np.stack(rs, axis=2).reshape(128, -1).astype(BF)
def pick(q, e):
    c = np.concatenate([q[0].reshape(128, -1, 4), np.zeros((128, 1, 4), np.uint8)], axis=1); s = np.concatenate([q[1], np.ones((16, 1), np.uint8)], axis=1)
    return (np.ascontiguousarray(c[:, e].reshape(128, -1)), np.ascontiguousarray(s[:, e]))
def join(*qs):
    return (np.concatenate([q[0] for q in qs], axis=1), np.concatenate([q[1] for q in qs], axis=1))
def put(q, e, v):
    c, s = q[0].reshape(128, -1, 4).copy(), q[1].copy(); c[:, e] = v[0].reshape(128, -1, 4); s[:, e] = v[1]
    return (c.reshape(128, -1), s)
def pk(c, s):
    return (np.ascontiguousarray(c), mx_ref.live(s))
def emit(q):
    return q[0], q[1]
def packed(v, rng):
    q = [mx_ref.quantize(np.ascontiguousarray(v[r])) for r in range(N)]
    return np.stack([a for a, b in q]), np.stack([mx_ref.plane(b, rng) for a, b in q])
def values_of_codes():
    e, c = np.zeros((128, 128, 4), np.float32), np.zeros((128, 2, 4), np.uint8)
    e[np.arange(128), np.arange(128), 0] = 1
    c[:127, :, 0] = np.arange(256).reshape(2, 128).T[:127]
    return mx_ref.matmul(mx_ref.quantize(e.reshape(128, 512).astype(BF)), (c.reshape(128, 8), np.full((16, 2), 127, np.uint8))).T.reshape(-1).astype(np.float64)
CODE_VALUE, SCALE_VALUE = values_of_codes(), 2.0 ** (np.arange(256) - 127.0)
def decode(q):
    return (CODE_VALUE[q[0]].reshape(16, 8, -1, 4) * SCALE_VALUE[q[1]][:, None, :, None] + 0.0).reshape(128, -1).astype(np.float32)
def f(rng, *shape):
    return mx_ref.flush((rng.standard_normal(shape, dtype=np.float32) * np.exp2(rng.integers(-2, 3, shape[:-1] + (1,)))).astype(BF))
def wide(rng, *shape, cols=0):
    v = rng.standard_normal(shape, dtype=np.float32) * np.exp2(rng.integers(-12, 13, shape)).astype(np.float32)
    if cols: v *= np.repeat(np.exp2(rng.integers(-cols, cols + 1, shape[:-2] + (1, shape[-1] // 4))) * (rng.random(shape[:-2] + (1, shape[-1] // 4)) > 0.0625), 4, axis=-1).astype(np.float32)
    return mx_ref.flush(v.astype(BF))
C, B, F, K, R = 288, 96, 3, 64, 3
def order(p):
    return np.argsort(-(p[::16] + np.float32(0.0)), axis=1, kind="stable")
def layer(w, q):
    return tile([mx_ref.matmul(pick(w, np.arange(128 * b, 128 * b + 128)), q) * np.float32(0.03125) for b in range(4)])
def numbers_of(rng):
    return {"x": np.array(f(rng, N, 128, 4 * C)), "u": np.array(f(rng, N, 128, 512)), "v": np.array(f(rng, N, 128, 512))}
def weights(rng, w):
    c, p = packed(w, rng)
    return {"wc": c, "ws": p}
def still(rng, q=-1):
    w = np.zeros((N, 128, 4, 128, 4), np.float32)
    i = np.arange(128)
    c = np.where(rng.permutation(N) % 2 == 0, 32.0, -32.0)
    for b in range(4): w[:, i, b, i, b] = c[:, None]
    if q >= 0:
        for b in range(4):
            w[:, 16 * q, b, 16 * q, :] = 0
            w[:, 16 * q, b, 16 * q, (b + 1) % 4] = 32
    return weights(rng, w.reshape(N, 128, 2048).astype(BF))
def signs(rng):
    return np.stack([rng.permutation(8) % 2 * 2.0 - 1.0 for r in range(N)])
def planned(rng, kind):
    b = rng.permutation(F)
    n = np.zeros(F, int)
    if kind == 0: n[:] = B // F
    if kind == 1: n[b[0]] = B
    if kind == 2: n[b[:2]] = B // 2
    if kind == 3:
        n[min(b[:2])] = B // 2 - 1
        n[max(b[:2])] = B // 2
        n[b[2]] = 1
    e = rng.permutation(np.concatenate([B * i + rng.permutation(B)[:n[i]] for i in range(F)]))
    return np.concatenate([e, rng.permutation(np.setdiff1d(np.arange(C), e))])
def level(rng):
    a, n, block, may = np.zeros((C, 4)), np.zeros(C, int), np.arange(C) // B, list(range(F))
    for t in range(R):
        least, more = (C - B) // (F + t), (C - B) % (F + t)
        e = [int(j) for j in rng.permutation(may)]
        w = np.concatenate([rng.permutation(np.flatnonzero(block == e[i]))[least + int(i < more):] for i in range(F + t)])
        a[w, n[w]] = R - t
        n[w] += 1
        block[w] = F + 2 * t
        b = min(e[more:])
        s = np.flatnonzero(block == b)
        n[s] += 1
        block[s] = F + 2 * t + 1
        may = [j for j in may if j != b] + [F + 2 * t, F + 2 * t + 1]
    return a
def setup_inputs(rng):
    return {**numbers_of(rng), **weights(rng, f(rng, N, 128, 2048))}
def setup_inputs_ties(rng):
    d = numbers_of(rng)
    e = rng.permutation(N)
    x = d["x"].reshape(N, 8, 16, C, 4)
    for r in range(N):
        k = np.zeros(C, int) if r == e[0] else rng.permutation(C) % 5 // 2
        a = x[r][:, :8, :3].copy()
        a[:, :, 2] = 0
        x[r][:, :8] = a[:, :, k]
        if r == e[1]: x[r][:, :, k == 2] = 0
    u = d["u"].reshape(N, 8, 16, 128, 4)
    u[:, :, 8:, ::16] = 0
    w = np.array(f(rng, N, 128, 2048)).reshape(N, 8, 16, 4, 8, 16, 4)
    w[:, :, 8:, :, :, :8] = 0
    return {"x": x.reshape(N, 128, 4 * C), "u": u.reshape(N, 128, 512), "v": d["v"], **weights(rng, w.reshape(N, 128, 2048))}
def setup_inputs_blocks(rng):
    d = numbers_of(rng)
    x = d["x"].astype(np.float32).reshape(N, 8, 16, C, 4)
    o = rng.permutation(N)
    s = np.zeros((N, 8, C), int)
    for r in range(N):
        k = rng.permutation(8) % 4 if o[r] > 1 else np.full(8, o[r])
        for g in range(8): s[r, g, planned(rng, k[g])] = (C - 1 - np.arange(C)) // 2
    b = ((s[:, :, :, None] >> np.arange(8)) & 1) * np.exp2(np.arange(8) - 23.0)
    x[:, :, 0] = 0
    x[:, :, 0, :, 0] = signs(rng)[:, :, None]
    x[:, :, 8] = b[:, :, :, :4]
    x[:, :, 9] = b[:, :, :, 4:]
    x[:, :, 10:] = rng.integers(4, 8, (N, 8, 6, C, 4)) * rng.choice([-1.0, 1.0], (N, 8, 6, C, 4)) * 2.0 ** -20
    u = d["u"].reshape(N, 128, 128, 4)
    k = np.where(rng.permutation(N) < N // 2, 2.0 ** -30, 1.0).astype(np.float32).astype(BF)
    u[:, :, ::16] = 0
    for h in range(0, 128, 16):
        u[:, h, h, 0] = k
        u[:, h + 8:h + 10, h] = k[:, None, None]
    return {"x": x.reshape(N, 128, 4 * C).astype(BF), "u": u.reshape(N, 128, 512), "v": d["v"], **still(rng)}
def setup_inputs_sizes(rng):
    d = numbers_of(rng)
    x = d["x"].astype(np.float32).reshape(N, 8, 16, C, 4)
    a = rng.integers(-7, 8, (N, 8, C)) * 2.0 ** -30
    r, g = np.nonzero(signs(rng) > 0)
    a[r, g, rng.integers(0, C, len(r))] = 2.0 ** 30 * rng.choice([-1.0, 1.0], len(r))
    x[:, :, :8] = 0
    x[:, :, 0, :, 0] = a
    q = int(rng.integers(8))
    x[:, q, 0] = level(rng) * 2.0 ** -30
    u = d["u"].reshape(N, 128, 128, 4)
    k = signs(rng) * np.where(rng.permutation(N) < N // 2, 2.0 ** -30, 1.0)[:, None]
    k[:, q] = np.abs(k[:, q])
    u[:, :, ::16] = 0
    for h in range(8): u[:, 16 * h, 16 * h, 0] = k[:, h].astype(np.float32).astype(BF)
    return {"x": x.reshape(N, 128, 4 * C).astype(BF), "u": u.reshape(N, 128, 512), "v": d["v"], **still(rng, q)}
def setup_inputs_huge(rng):
    d = numbers_of(rng)
    x = 2.0 ** 30 * (0.6 + 0.4 * rng.random((N, 128, C, 4)))
    c = np.stack([rng.permutation(C) % 2 * 2.0 - 1.0 for r in range(N)])
    c[rng.permutation(N) < N // 2] = 1
    x *= c[:, None, :, None]
    u = d["u"].reshape(N, 128, 128, 4)
    a = 2.0 ** 30 * (1 - 0.25 * rng.random((N, 128, 8, 4))) * signs(rng)[:, None, :, None]
    u[:, :, ::16] = a.astype(np.float32).astype(BF)
    return {"x": x.astype(np.float32).reshape(N, 128, 4 * C).astype(BF), "u": u.reshape(N, 128, 512), "v": d["v"], **still(rng)}
def setup_inputs_spread(rng):
    d = setup_inputs(rng)
    d["x"] = wide(rng, N, 128, 4 * C, cols=6)
    return d
def check_inputs(d):
    b = []
    for k in ("x", "u", "v"):
        a = np.abs(d[k].astype(np.float32))
        if not (np.isfinite(a).all() and ((a == 0) | (a >= 2.0 ** -30) & (a <= 2.0 ** 30)).all()): b.append("a value of " + k)
    return b
def reference(x, u, v, wc, ws):
    qu = [mx_ref.quantize(u[r]) for r in range(N)]
    lay = [pk(wc[r], ws[r]) for r in range(N)]
    now = [x[r] for r in range(N)]
    block = np.tile(np.arange(C) // B, (N, 8, 1))
    gone = np.zeros((N, 8, F + 2 * R), bool)
    for t in range(R):
        first, made, stay, kept, sent = [], [], [], [], []
        for r in range(N):
            q = mx_ref.quantize(now[r])
            o = order(mx_ref.matmul(qu[r], q))
            first.append(o[:, :B])
            made.append(layer(lay[r], mx_ref.quantize(gcols(now[r], o[:, :B]))))
            np.put_along_axis(block[r], o[:, :B], F + 2 * t, axis=1)
            e = np.full((8, K), -1)
            for g in range(8):
                n = np.bincount(block[r, g], minlength=F + 2 * R)
                n[gone[r, g]] = C + 1
                b = np.argmin(n[:F + 2 * t])
                gone[r, g, b] = True
                s = o[g][block[r, g, o[g]] == b]
                e[g, :len(s)] = s
                block[r, g, s] = F + 2 * t + 1
            stay.append(e)
            kept.append(gcols(decode(q).astype(BF), e))
            sent.append(mx_ref.quantize(kept[r]))
        for r in range(N):
            p = (r - 1) % N
            h = layer(lay[r], sent[p])
            e = np.tile(np.arange(C), (8, 1))
            np.put_along_axis(e, first[r], np.tile(C + np.arange(B), (8, 1)), axis=1)
            for g in range(8):
                k = np.flatnonzero(stay[r][g] >= 0)
                e[g, stay[r][g, k]] = C + B + k + np.where(stay[p][g, k] >= 0, 0, K)
            now[r] = gcols(np.concatenate([now[r], made[r], h, kept[r]], axis=1), e)
    y, ob = np.zeros((N, 128, C), np.float32), np.zeros((N, 8, C), np.float32)
    oc, osc = np.zeros((N, 128, 4 * C), np.uint8), np.zeros((N, 16, C), np.uint8)
    for r in range(N):
        q = mx_ref.quantize(now[r])
        y[r] = mx_ref.matmul(mx_ref.quantize(v[r]), q)
        ob[r] = block[r]
        oc[r], osc[r] = emit(q)
    return {"y": y, "ob": ob, "oc": oc, "osc": osc}

@@ -1,0 +1,443 @@
+from concourse.mybir import dt, AluOpType, AxisListType, ActivationFunctionType
+
+C, B, K, R = 288, 96, 64, 3
+NY, NH, ND = 288, 384, 448
+WW = 4 * (ND + C)
+S = 1.0 / 8192
+M = 1.5 * 2.0 ** 19
+BIG = 1.0e28
+CT = [0, 288, 512, 800, 672]
+CW = [288, 224, 160, 128, 128]
+ORDER = [17, 14, 16, 15, 13, 12, 11, 10, 9, 8, 7, 2, 1, 6, 5, 4, 3]
+ON_SCALAR = (17, 14)
+QUANT_AFTER = {13: (0, 288), 10: (288, 512), 6: (512, 704)}
+SP = 192
+
+F32, BF, I32, U16, Q4, U8 = "float32", "bfloat16", "int32", "uint16", "float8_e4m3fn_x4", "uint8"
+
+
+def _sb(n, d):
+    return ("sbuf", [128, n], d)
+
+
+SCRATCH = {
+    "w0": _sb(WW, BF), "w1": _sb(WW, BF), "xq": _sb(4 * C, Q4), "xs": _sb(4 * C, U8), "lq": _sb(R * C, Q4), "ls": _sb(R * C, U8),
+    "ut": _sb(512, BF), "uq": _sb(128, Q4), "us": _sb(128, U8), "uq2": _sb(128, Q4), "us2": _sb(128, U8),
+    "vt": _sb(512, BF), "vq": _sb(128, Q4), "vs": _sb(128, U8), "wq": _sb(512, Q4), "wp": _sb(512, U8),
+    "ones": _sb(128, BF), "ff": _sb(1040, BF), "eq": _sb(512, Q4), "es": _sb(512, U8),
+    "gj": _sb(128, F32), "b2": _sb(512, BF), "bq": _sb(128, Q4), "bs": _sb(128, U8),
+    "ct": _sb(4 * 928, BF), "cq": _sb(928, Q4), "cs": _sb(928, U8), "junk": _sb(2448, BF), "junk2": _sb(384, BF),
+    "tt": _sb(512, BF), "tq": _sb(128, Q4), "ts": _sb(128, U8),
+    "dp": _sb(4 * C + 16, BF), "st": _sb(512, BF), "sq": _sb(128, Q4), "ss": _sb(128, U8),
+    "n0": _sb(1, F32), "n1": _sb(1, F32), "n2": _sb(1, F32), "l0": _sb(16, U16), "l1": _sb(16, U16), "l2": _sb(16, U16),
+    "pi": _sb(2, I32), "ci": _sb(6, I32), "cf": _sb(6, F32), "cc": _sb(20, F32),
+    "oui": _sb(8, I32), "ou": _sb(8, U16), "i16": _sb(C, F32), "i4": _sb(C, F32), "it16": _sb(72, F32), "it4": _sb(72, F32),
+    "mx": _sb(C, F32), "hd": _sb(C, F32), "sd": _sb(C, BF), "d1": _sb(C, F32), "d4": _sb(C, F32),
+    "kk": _sb(18, F32), "thr": _sb(4, F32), "j4": _sb(4, F32), "e4": _sb(4, F32),
+    "pg": _sb(C, F32), "src": _sb(C, F32), "aa": _sb(C, F32), "hh": _sb(C, F32), "rs": _sb(18, F32),
+    "dseg": _sb(C, BF), "adj": _sb(18, F32), "ext": _sb(C, F32), "r16": _sb(18, U16), "zz": _sb(304, F32),
+    "iq": _sb(160, BF), "kd": _sb(160, F32), "kr": _sb(160, F32), "kt": _sb(64, F32), "mm": _sb(6, F32),
+    "ind": _sb(192, BF), "zero": _sb(192, BF), "pf": _sb(192, BF), "le": _sb(336, BF), "acc": _sb(4, F32), "v5": _sb(1, F32),
+    "o4": _sb(4, U16), "lp": _sb(K, F32), "lx": _sb(K, F32), "os16": _sb(16 * R, U16),
+    "tx": _sb(B, F32), "tr": _sb(24, F32), "tp": _sb(24, F32), "ot": _sb(24, U16),
+    "zc": _sb(C, BF), "zp": _sb(C, F32), "zx": _sb(C, F32), "th": _sb(1, F32),
+    "ea": _sb(72, F32), "en": _sb(72, F32), "eb": _sb(72, F32), "ec": _sb(72, F32), "ed": _sb(72, F32), "oe": _sb(72, U16),
+    "lab": _sb(192, F32), "ik": _sb(192, F32), "gl": _sb(C, F32), "ku": _sb(4, F32), "base": _sb(3, F32),
+    "yo": _sb(C, F32), "obo": _sb(C, F32),
+    "pp": ("psum", [128, 512], F32), "pc": ("psum", [128, 512], F32),
+    "pd0": ("psum", [128, 512], F32), "pd1": ("psum", [128, 512], F32), "pd2": ("psum", [128, 512], F32), "pd3": ("psum", [128, 512], F32),
+    "py0": ("psum", [128, 512], F32), "py1": ("psum", [128, 512], F32),
+}
+SEMAPHORES = ["qv", "qs", "qt", "qg", "sent", "lx", "lu", "lv", "lw", "lp", "so", "sc", "sy", "s0", "s1", "s2", "s3",
+              "an0", "an1", "an2", "ax0", "ax1", "ax2", "al0", "al1", "al2"]
+A, ACT = AluOpType, ActivationFunctionType
+
+
+def _meet(a, b):
+    if a[0] != b[0] or a[2] <= b[1] or b[2] <= a[1]:
+        return False
+    return not (a[3] == b[3] and a[3] > 1 and (a[1] - b[1]) % a[3] != 0)
+
+
+def rank_program(g, core, T, topo):
+    rank = T.rank_of(core)
+    if rank is None:
+        return
+    nxt = T.cores[(rank + 1) % len(T.cores)]
+    rid, pid = topo.addr(nxt)[:2]
+    lanes = topo.mask(core, nxt)
+    nl = len(topo.engines(core, nxt))
+    nin = len(topo.engines(T.cores[rank - 1], core))
+    eng = {"v": g.vector, "s": g.scalar, "t": g.tensor, "g": g, "y": g.sync}
+
+    ops = {q: [] for q in eng}
+    known = {q: {} for q in eng}
+    seen = {n: [] for n in SCRATCH}
+    count = {}
+    sends = []
+
+    def r(name, lo=0, hi=None, step=1):
+        return (name, lo, SCRATCH[name][1][1] if hi is None else hi, step)
+
+    def col(name, j):
+        return r(name, j, j + 1)
+
+    def ap(x):
+        if len(x) == 2:
+            return ap(x[0]).indirect(ap(x[1]))
+        return T[x[0]][:, x[1]:x[2]:x[3]] if x[3] > 1 else T[x[0]][:, x[1]:x[2]]
+
+    def val(x):
+        return ap(x) if isinstance(x, tuple) else x
+
+    def u8(x):
+        return ap(x).bitcast(dt.uint8)
+
+    def put(q, call, reads, writes, own=None, chain=False):
+        acc = []
+        for x, w in [(x, False) for x in reads if isinstance(x, tuple)] + [(x, True) for x in writes]:
+            acc += [(x[0], w), (x[1], False)] if len(x) == 2 else [(x, w)]
+        need = {}
+        for x, w in acc:
+            bank = SCRATCH[x[0]][0] == "psum"
+            for y, wy, s, i, clock in seen[x[0]]:
+                if chain and bank and s == q:
+                    continue
+                if (bank and s != q) or ((w or wy) and _meet(x, y)):
+                    if known[q].get(s, -1) < i and need.get(s, (-1, None))[0] < i:
+                        need[s] = (i, clock)
+        waits = []
+        for s, (i, clock) in sorted(need.items(), key=lambda e: -len(e[1][1])):
+            if known[q].get(s, -1) >= i:
+                continue
+            waits.append((s, i))
+            known[q][s] = i
+            for k2, i2 in clock.items():
+                if known[q].get(k2, -1) < i2:
+                    known[q][k2] = i2
+        me = (q, len(ops[q])) if own is None else (own, 0)
+        ops[q].append([call, waits, own])
+        for x, w in acc:
+            seen[x[0]].append((x, w, me[0], me[1], dict(known[q])))
+
+    def arrives(name, n, views):
+        count[name] = n
+        for x in views:
+            seen[x[0]].append((x, True, name, 0, {}))
+
+    def dma(q, sem, out, in_, reads, writes):
+        count[sem] = 16
+        put(q, lambda: eng[q].dma_start(out, in_), reads, writes, own=sem)
+
+    def send(out, in_, sem, reads):
+        sends.append(sem)
+        put("g", lambda: g.remote_dma(out, in_, T.sem[sem], T.sem.sent, pid, rid, lanes), reads, [], own="")
+
+    def ts(out, in0, s1, op0, s2=None, op1=None):
+        if op1 is None:
+            put("v", lambda: g.vector.tensor_scalar(ap(out), ap(in0), val(s1), None, op0), [in0, s1], [out])
+        else:
+            put("v", lambda: g.vector.tensor_scalar(ap(out), ap(in0), val(s1), val(s2), op0, op1), [in0, s1, s2], [out])
+
+    def tt(out, a, b, op):
+        put("v", lambda: g.vector.tensor_tensor(ap(out), ap(a), ap(b), op), [a, b], [out])
+
+    def cp(out, a):
+        put("v", lambda: g.vector.tensor_copy(ap(out), ap(a)), [a], [out])
+
+    def fill(out, c):
+        put("v", lambda: g.vector.memset(ap(out), c), [], [out])
+
+    def scan(out, d0, d1, init, op0, op1):
+        put("v", lambda: g.vector.tensor_tensor_scan(ap(out), ap(d0), ap(d1), val(init), op0, op1), [d0, d1, init], [out])
+
+    def red(out, a, op):
+        put("v", lambda: g.vector.tensor_reduce(ap(out), ap(a), AxisListType.X, op), [a], [out])
+
+    def quant(qn, sn, lo, hi, tile):
+        put("v", lambda: g.vector.quantize_mx(ap(r(qn, lo, hi)), ap(r(sn, lo, hi)), ap(tile)), [tile], [r(qn, lo, hi), r(sn, lo, hi)])
+
+    def act(out, a, func=ACT.Identity, bias=0.0, scale=1.0, acc=None):
+        if acc is None:
+            put("s", lambda: g.scalar.activation(ap(out), ap(a), func, bias=val(bias), scale=val(scale)), [a, bias, scale], [out])
+        else:
+            put("s", lambda: g.scalar.activation(ap(out), ap(a), func, bias=val(bias), scale=val(scale), accum_out=ap(acc)), [a, bias, scale], [out, acc])
+
+    def mm(bank, wn, ws_, w0, xn, xs_, lo, hi, start=True, stop=True):
+        a = [r(wn, w0, w0 + 128), r(ws_, w0, w0 + 128), r(xn, lo, hi), r(xs_, lo, hi)]
+        o = r(bank, 0, hi - lo)
+        put("t", lambda: g.tensor.matmul_mx(ap(o), ap(a[0]), ap(a[1]), ap(a[2]), ap(a[3]), start, stop), a, [o], chain=not start)
+
+    def iota(out, pattern, base, cm=0):
+        if SCRATCH[out[0]][2] == I32:
+            put("g", lambda: g.iota(ap(out), pattern, base, cm), [], [out])
+        else:
+            put("g", lambda: g.iota(ap(out), pattern, base, cm, allow_small_or_imprecise_dtypes=True), [], [out])
+
+    def ident(out):
+        put("g", lambda: g.affine_select(ap(out), T.ones[:, 0:128], [[-1, 128]], A.is_equal, 0.0, 0, 1), [r("ones")], [out])
+
+    for t in range(R):
+        arrives("an%d" % t, nin, [r("n%d" % t)])
+        arrives("al%d" % t, nin, [r("l%d" % t)])
+        arrives("ax%d" % t, 2 * nin, [r("lq", C * t, C * t + C), r("ls", C * t, C * t + C)])
+
+    x0 = r("w0", 0, 4 * C)
+    dma("y", "lx", ap(x0), T.x[:], [], [x0])
+    dma("s", "lu", T.ut[:], T.u[:], [], [r("ut")])
+    dma("y", "lw", u8(r("wq")), T.wc[:], [x0], [r("wq")])
+    dma("y", "lp", T.wp[:], T.ws[:], [], [r("wp")])
+    dma("y", "lv", T.vt[:], T.v[:], [], [r("vt")])
+
+    q_, qm1, h_, r_, q4, g_ = (col("cf", j) for j in range(6))
+    mq, z0, t0, ccs, ck, cl0, cl, ctl, cz0, cz, cth, t1, cz1, t2, t3, t4 = (col("cc", j) for j in range(16))
+    fill(r("st"), 0.0)
+    fill(r("ones"), 1.0)
+    fill(r("ff"), 0.0)
+    iota(r("pi"), [[15, 2]], 0, 1)
+    iota(r("oui"), [[16, 8]], 0)
+    iota(r("i16"), [[0, 18], [1, 16]], 0)
+    ident(r("ff", 2, 514, 4))
+    ident(r("ff", 523, 1035, 4))
+    iota(r("gj"), [[1, 8], [0, 16]], 0)
+    iota(r("it16"), [[16, 72]], 0)
+    iota(r("src"), [[B + 512, 3], [1, B]], -144)
+    iota(r("i4"), [[0, 72], [1, 4]], 0)
+
+    act(r("ct", 4 * 672, 4 * 800), r("st"), ACT.Copy)
+    act(r("ct", 4 * 848, 4 * 928), r("st", 0, 320), ACT.Copy)
+    ts(r("ci", 0, 2), r("pi"), 15, A.bitwise_and)
+    ts(col("ci", 2), col("pi", 0), 4, A.logical_shift_right, 1, A.bitwise_and)
+    ts(col("ci", 3), col("pi", 0), 2, A.logical_shift_right, 3, A.bitwise_and)
+    ts(col("ci", 4), col("pi", 0), 3, A.bitwise_and)
+    ts(col("ci", 5), col("pi", 0), 4, A.logical_shift_right)
+    cp(r("ou"), r("oui"))
+    cp(r("cf"), r("ci"))
+    for a in (240, 464, 624):
+        fill(r("ct", 4 * a, 4 * a + 192), 0.0)
+    ts(r("mx"), r("i16"), q_, A.is_equal, 0.5, A.subtract)
+    ts(r("d1"), r("i16"), qm1, A.not_equal, 1.0 - 1.0 / 128, A.subtract)
+    quant("cq", "cs", 672, 800, r("ct", 4 * 672, 4 * 800))
+    act(r("hd"), r("i16"), bias=-0.5 * BIG, scale=BIG)
+    act(r("mx"), r("mx"), scale=BIG)
+    act(r("gj"), r("gj"), ACT.Abs, bias=g_, scale=-1.0)
+    act(z0, q_, ACT.Relu, bias=1.0, scale=-1.0)
+    act(t0, q_, bias=-7680.0, scale=512.0)
+    act(t1, q_, bias=15.0, scale=-1.0)
+    act(t2, q_, bias=-131072.0, scale=-0.0625)
+    for b in range(4):
+        act(r("b2", b, 512, 4), r("gj"), ACT.Relu, bias=1.0, scale=-1.0)
+    for b, a in enumerate((2, 522, 0, 520)):
+        quant("eq", "es", 128 * b, 128 * b + 128, r("ff", a, a + 512))
+    fill(r("kd", 0, B), -1.0)
+    fill(r("kd", B, 160), 0.0)
+    fill(r("zz", C, 304), 1.0e6)
+    quant("uq", "us", 0, 128, r("ut"))
+    fill(col("rs", 0), 0.0)
+    put("v", lambda: g.vector.tensor_copy(T.uq2[:, 0:128].bitcast(dt.uint32), T.uq[:, 0:128].bitcast(dt.uint32).indirect(T.ou[:, 0:8])),
+        [r("uq"), r("ou")], [r("uq2")])
+    cp(r("us2"), (r("us"), r("ou")))
+    act(ccs, z0, bias=t0, scale=65024.0)
+    act(ck, z0, bias=t1, scale=-65024.0)
+    act(r("sd"), r("i16"), ACT.Sign)
+    act(r("d1"), r("d1"), scale=65536.0)
+    act(r("kk"), r("it16", 0, 18), bias=ck)
+    act(mq, q_, bias=M, scale=0.0625)
+    act(t3, q_, bias=B + 0.5)
+    act(t4, q_, scale=S)
+    act(col("kd", 96), h_, scale=131072.0)
+    act(col("kd", 112), h_, bias=131072.0, scale=-262144.0)
+    act(col("kd", 128), h_, bias=t2, scale=262144.0)
+    act(col("kd", 144), h_, bias=131072.0, scale=-262144.0)
+    act(r("src"), r("src"), scale=S)
+    act(r("iq", B, 160), r("st", 0, 64), ACT.Copy)
+    act(r("zero"), r("st", 0, 192), ACT.Copy)
+
+    def late_constants():
+        act(r("d4"), r("i4"), ACT.Abs, bias=r_, scale=-1.0)
+        act(r("thr"), r("it16", 0, 4), bias=t3)
+        act(cl0, q4, bias=4.0 * 144 - 3 * 32768.0)
+        act(r("d4"), r("d4"), ACT.Sign)
+        act(ctl, q4, bias=4.0 * 144)
+        act(cz0, q4, bias=4.0 * (NY - 1) * S - 3, scale=S)
+        act(r("d4"), r("d4"), bias=-7.0, scale=8.0)
+        act(cl, r_, bias=cl0, scale=32768.0)
+        act(cz1, q4, bias=(4.0 * (NY - 1) + 0.5) * S, scale=S)
+        act(cth, q4, bias=4.0 * (NH - 1 - M) * S, scale=S)
+        act(cz, r_, bias=cz0)
+        act(r("it4"), r("it16"), bias=t4, scale=S)
+        act(r("tt", 4 * B, 512), r("st", 0, 128), ACT.Copy)
+        act(r("dp", 4 * C, 4 * C + 16), r("st", 0, 16), ACT.Copy)
+        act(r("pg"), r("pg"), scale=S)
+
+    pd = ["pd0", "pd1", "pd2", "pd3"]
+    py = ["py0", "py1", "pp", "pc"]
+
+    def cview(m):
+        k = (18 - m) // 4
+        return r("ct", 4 * CT[k] + (18 - m) % 4, 4 * (CT[k] + 16 * m), 4)
+
+    for t in range(R):
+        w, wn = "w%d" % (t % 2), "w%d" % ((t + 1) % 2)
+        win = r(w)
+        more = t < R - 1
+        m1, m2 = col("mm", 2 * t), col("mm", 2 * t + 1)
+        xa, xb = C * t, C * t + C
+        quant("xq", "xs", xa, xb, r(w, 0, 4 * C))
+        mm("pp", "uq2", "us2", 0, "xq", "xs", xa, xb)
+        mm("py0", "uq2", "us2", 0, "xq", "xs", xa, xb)
+        send(u8(r("lq", xa, xb)), u8(r("xq", xa, xb)), "ax%d" % t, [r("xq", xa, xb)])
+        send(ap(r("ls", xa, xb)), ap(r("xs", xa, xb)), "ax%d" % t, [r("xs", xa, xb)])
+        if t == 0:
+            iota(r("j4"), [[1, 4]], 3)
+            iota(r("zc", 0, B), [[1, B]], 1)
+            iota(r("pg"), [[1, C]], -144)
+            quant("bq", "bs", 0, 128, r("b2"))
+            ts(col("ku", 0), q_, 2.5, A.is_gt, 65536.0 - B, A.mult)
+            fill(r("le", 160, 336, 168), -128.0)
+            ts(col("base", 0), col("ku", 0), float(B), A.add, mq, A.add)
+        else:
+            tt(r("src", 128, C), (r("gl"), r("r16", 8, 18)), r("pg", 128, C), A.add)
+        for b in range(4):
+            mm(pd[b], "eq", "es", 128 * b, "xq", "xs", xa, xb)
+        dv = r("ct", 0, 4 * C, 4)
+        for a, b in ((SP, C), (0, SP)):
+            tt(r("aa", a, b), r("pp", a, b), r("mx", a, b), A.min)
+        for a, b in ((SP, C), (0, SP)):
+            scan(r("hh", a, b), r("hd", a, b), r("aa", a, b), -BIG, A.min, A.max)
+        jo = 0
+        for m in ORDER:
+            jv = r("junk", jo, jo + 16 * m)
+            jo += 16 * m
+            if m in ON_SCALAR:
+                act(jv, r("py0", 0, 16 * m), ACT.Sign, bias=col("hh", 16 * m + 15), scale=-1.0)
+                act(cview(m), jv, ACT.Relu, acc=col("rs", m))
+            else:
+                ts(cview(m), r("pp", 0, 16 * m), col("hh", 16 * m + 15), A.is_lt)
+                act(jv, cview(m), acc=col("rs", m))
+            if m == 16:
+                tt(dv, r("hh"), r("pp", 0, C), A.is_ge)
+            if m in QUANT_AFTER:
+                a, b = QUANT_AFTER[m]
+                quant("cq", "cs", a, b, r("ct", 4 * a, 4 * b))
+        scan(r("dseg"), r("sd"), dv, 0.0, A.mult, A.add)
+        quant("cq", "cs", 800, 928, r("ct", 4 * 800, 4 * 928))
+        for k in (0, 1, 2, 4, 3):
+            mm("pc", "bq", "bs", 0, "cq", "cs", CT[k], CT[k] + CW[k], start=(k == 0), stop=(k == 3))
+        if t == 0:
+            late_constants()
+        for b in range(4):
+            act(r(w, 4 * ND + b, WW, 4), r(pd[b], 0, C), ACT.Copy)
+        for b in range(4):
+            mm(pd[b], "eq", "es", 128 * b, "lq", "ls", xa, xb)
+        tt(r("adj"), r("kk"), r("dseg", 15, C, 16), A.subtract)
+        tt(r("d1", 15, C, 16), r("adj"), r("rs"), A.subtract)
+        scan(r("ext"), r("pc", 0, C), r("d1"), -65024.0, A.max, A.add)
+        ts(r("r16"), r("ext", 15, C, 16), ccs, A.add)
+        cp((r("zz", 0, C), r("r16")), r("src"))
+        ts(r("iq", 0, B), r("zz", 0, B), M, A.add, mq, A.not_equal)
+        scan(r("kr"), r("iq"), r("kd"), col("base", t), A.add, A.add)
+        put("v", lambda: g.vector.transpose(T.kt[:, 0:64], T.kr[:, B:160]), [r("kr", B, 160)], [r("kt")])
+        red(m2, r("kt", 32, 64), A.min)
+        red(m1, r("kt", 0, 32), A.min)
+        send(T["n%d" % t][:, 0:1], ap(m2), "an%d" % t, [m2])
+        ts(r("ind"), r("zz", B, C), m2, A.add, m1, A.is_equal)
+        ts(r("v5"), m1, m2, A.subtract)
+        scan(r("pf"), r("ind"), r("zero"), float(B), A.add, A.add)
+        for k in (0, 1):
+            act(r("junk2", 192 * k, 192 * k + 192), r("pf"), ACT.Sign, bias=col("thr", k), scale=-1.0, acc=col("acc", k))
+        for k in (2, 3):
+            ts(r("le", 168 * (k - 2), 168 * (k - 2) + 160), r("pf", 32, 192), col("thr", k), A.is_lt, 2.0, A.mult)
+        for k in (2, 3):
+            red(col("acc", k), r("le", 168 * (k - 2), 168 * (k - 2) + 161), A.add)
+        ts(r("o4"), r("acc"), 192.0, A.add, 0.5, A.mult)
+        ts(r("lp"), (r("zz", B, C + 1), r("o4")), r("v5"), A.subtract, 144.0 * S, A.min)
+        scan(r("lx"), r("d4", 0, K), r("lp"), 0.0, A.add, A.max)
+        ol = r("os16", 16 * t, 16 * t + 16)
+        ts(ol, r("lx", 3, K, 4), 32768.0, A.mult, cl, A.add)
+        send(T["l%d" % t][:, 0:16], ap(ol), "al%d" % t, [ol])
+        for b in range(2):
+            act(r("dp", b, 4 * C, 4), r(pd[b], 0, C), ACT.Copy)
+        scan(r("tx"), r("d4", 0, B), r("zz", 0, B), 0.0, A.add, A.max)
+        tt(r("zc", B, C), r("ind"), r("pf"), A.mult)
+        ts(r("tr"), r("tx", 3, B, 4), M, A.add, M, A.subtract)
+        ts(r("lab"), r("zz", B, C), M, A.add, M, A.subtract)
+        tt(r("tp"), r("tx", 3, B, 4), r("tr"), A.subtract)
+        fill(r("gl", 0, B), (3 + 2 * t) / 16)
+        ts(r("ot"), r("tp"), 32768.0, A.mult, ctl, A.add)
+        act(r("zp"), (r("zc"), r("r16")), bias=cz, scale=4.0 * S)
+        act(r("tt", 0, 4 * B), (win, r("ot")), ACT.Copy)
+        for b in range(2, 4):
+            act(r("dp", b, 4 * C, 4), r(pd[b], 0, C), ACT.Copy)
+        ts(r("ik"), r("ind"), (4 + 2 * t) / 16, A.mult)
+        if t == 0:
+            ts(r("e4"), r("j4"), q_, A.is_equal)
+        if more:
+            ts(col("ku", 1), col("kr", B - 1), m1, A.is_equal, 65536.0, A.mult)
+        tt(r("gl", B, C), r("lab"), r("ik"), A.max)
+        scan(r("zx"), r("d4"), r("zp"), 0.0, A.add, A.max)
+        x = r("zx", 3, C, 4)
+        if more:
+            ts(col("ku", 2), m2, M + 65536.0, A.subtract, col("e4", 2 * t + 1), A.mult)
+            ts(col("ku", 3), col("e4", 2 * t), B - 65536.0, A.mult, col("kr", B - 1), A.add)
+        ts(r("en"), x, cz1, A.is_gt, 4.0 * ND * S, A.mult)
+        quant("tq", "ts", 0, 128, r("tt"))
+        for b in range(4):
+            mm(py[b], "wq", "wp", 128 * b, "tq", "ts", 0, 128)
+        for b in range(4):
+            act(r(w, 4 * NY + b, 4 * NH, 4), r(py[b], 0, B), scale=0.03125)
+        ts(r("th"), r("n%d" % t), 4.0 * S, A.mult, cth, A.add)
+        tt(r("ec"), r("en"), r("it4"), A.add)
+        ts(r("ea"), x, r("th"), A.is_gt)
+        if more:
+            ts(col("base", t + 1), col("ku", 3), col("ku", 2), A.add, col("ku", 1), A.add)
+        tt(r("eb"), r("ea"), x, A.add)
+        if not more:
+            quant("vq", "vs", 0, 128, r("vt"))
+        tt(r("ed"), r("ec"), r("eb"), A.min)
+        ts(r("oe"), r("ed"), 8192.0, A.mult)
+        cp(r("st", 0, 128), (r("dp"), r("l%d" % t, 0, 8)))
+        act(r("st", 128, 256), (r("dp"), r("l%d" % t, 8, 16)), ACT.Copy)
+        quant("sq", "ss", 0, 128, r("st"))
+        for b in (0, 2, 1, 3):
+            mm(pd[b], "wq", "wp", 128 * b, "sq", "ss", 0, 128)
+        if more:
+            tt(r("src", 0, 128), (r("gl"), r("r16", 0, 8)), r("pg", 0, 128), A.add)
+        for b in (0, 2, 1, 3):
+            o = r(w, 4 * NH + b, 4 * ND, 4)
+            if b < 2:
+                ts(o, r(pd[b], 0, K), 0.03125, A.mult)
+            else:
+                act(o, r(pd[b], 0, K), scale=0.03125)
+        cp(r(wn, 0, 576), (win, r("oe", 0, 36)))
+        act(r(wn, 576, 1152), (win, r("oe", 36, 72)), ACT.Copy)
+
+    xa, xb = R * C, R * C + C
+    act(r("obo"), (r("gl"), r("r16")), scale=16.0)
+    quant("xq", "xs", xa, xb, r("w%d" % (R % 2), 0, 4 * C))
+    mm("pp", "vq", "vs", 0, "xq", "xs", xa, xa + C // 2)
+    mm("pc", "vq", "vs", 0, "xq", "xs", xa + C // 2, xb)
+    dma("y", "sc", T.oc[:], u8(r("xq", xa, xb)), [r("xq", xa, xb)], [])
+    for k in range(4):
+        dma("y", "s%d" % k, T.osc[4 * k:4 * k + 4, :], T.xs[32 * k:32 * k + 4, xa:xb], [r("xs", xa, xb)], [])
+    dma("y", "so", T.ob[:], T.obo[0:128:16, :], [r("obo")], [])
+    act(r("yo", 0, C // 2), r("pp", 0, C // 2), ACT.Copy)
+    cp(r("yo", C // 2, C), r("pc", 0, C // 2))
+    dma("s", "sy", T.y[:], T.yo[:], [r("yo")], [])
+
+    marked = {q: sorted({i for p in ops for o in ops[p] for s, i in o[1] if s == q}) for q in eng}
+    for q in eng:
+        for i, (call, waits, own) in enumerate(ops[q]):
+            for s, j in waits:
+                if s in eng:
+                    eng[q].wait_ge(T.sem["q" + s], marked[s].index(j) + 1)
+                else:
+                    eng[q].wait_ge(T.sem[s], count[s])
+            ins = call()
+            if own:
+                ins.then_inc(T.sem[own], 16)
+            elif own is None and i in marked[q]:
+                ins.then_inc(T.sem["q" + q], 1)
+    g.wait_ge(T.sem.sent, nl * len(sends))
+    for s in ("so", "sc", "sy", "s0", "s1", "s2", "s3"):
+        g.sync.wait_ge(T.sem[s], 16)

@@ -2,54 +2,36 @@ from concourse.mybir import dt, AluOpType, AxisListType, ActivationFunctionType
 
 C, B, K, R = 288, 96, 64, 3
 NY, NH, ND = 288, 384, 448
-WW = 4 * (ND + C)
+WW = 4 * (ND + C) + 16
 S = 1.0 / 8192
 M = 1.5 * 2.0 ** 19
 BIG = 1.0e28
 CT = [0, 288, 512, 800, 672]
 CW = [288, 224, 160, 128, 128]
-ORDER = [17, 14, 16, 15, 13, 12, 11, 10, 9, 8, 7, 2, 1, 6, 5, 4, 3]
+ORDER = [16, 15, 13, 12, 11, 10, 9, 8, 7, 2, 1, 6, 5, 4, 3]
 ON_SCALAR = (17, 14)
 QUANT_AFTER = {13: (0, 288), 10: (288, 512), 6: (512, 704)}
 SP = 192
+KT = [64, 48, 40]
+LO = [128, 192, 240]
 
 F32, BF, I32, U16, Q4, U8 = "float32", "bfloat16", "int32", "uint16", "float8_e4m3fn_x4", "uint8"
-
-
-def _sb(n, d):
-    return ("sbuf", [128, n], d)
-
-
-SCRATCH = {
-    "w0": _sb(WW, BF), "w1": _sb(WW, BF), "xq": _sb(4 * C, Q4), "xs": _sb(4 * C, U8), "lq": _sb(R * C, Q4), "ls": _sb(R * C, U8),
-    "ut": _sb(512, BF), "uq": _sb(128, Q4), "us": _sb(128, U8), "uq2": _sb(128, Q4), "us2": _sb(128, U8),
-    "vt": _sb(512, BF), "vq": _sb(128, Q4), "vs": _sb(128, U8), "wq": _sb(512, Q4), "wp": _sb(512, U8),
-    "ones": _sb(128, BF), "ff": _sb(1040, BF), "eq": _sb(512, Q4), "es": _sb(512, U8),
-    "gj": _sb(128, F32), "b2": _sb(512, BF), "bq": _sb(128, Q4), "bs": _sb(128, U8),
-    "ct": _sb(4 * 928, BF), "cq": _sb(928, Q4), "cs": _sb(928, U8), "junk": _sb(2448, BF), "junk2": _sb(384, BF),
-    "tt": _sb(512, BF), "tq": _sb(128, Q4), "ts": _sb(128, U8),
-    "dp": _sb(4 * C + 16, BF), "st": _sb(512, BF), "sq": _sb(128, Q4), "ss": _sb(128, U8),
-    "n0": _sb(1, F32), "n1": _sb(1, F32), "n2": _sb(1, F32), "l0": _sb(16, U16), "l1": _sb(16, U16), "l2": _sb(16, U16),
-    "pi": _sb(2, I32), "ci": _sb(6, I32), "cf": _sb(6, F32), "cc": _sb(20, F32),
-    "oui": _sb(8, I32), "ou": _sb(8, U16), "i16": _sb(C, F32), "i4": _sb(C, F32), "it16": _sb(72, F32), "it4": _sb(72, F32),
-    "mx": _sb(C, F32), "hd": _sb(C, F32), "sd": _sb(C, BF), "d1": _sb(C, F32), "d4": _sb(C, F32),
-    "kk": _sb(18, F32), "thr": _sb(4, F32), "j4": _sb(4, F32), "e4": _sb(4, F32),
-    "pg": _sb(C, F32), "src": _sb(C, F32), "aa": _sb(C, F32), "hh": _sb(C, F32), "rs": _sb(18, F32),
-    "dseg": _sb(C, BF), "adj": _sb(18, F32), "ext": _sb(C, F32), "r16": _sb(18, U16), "zz": _sb(304, F32),
-    "iq": _sb(160, BF), "kd": _sb(160, F32), "kr": _sb(160, F32), "kt": _sb(64, F32), "mm": _sb(6, F32),
-    "ind": _sb(192, BF), "zero": _sb(192, BF), "pf": _sb(192, BF), "le": _sb(336, BF), "acc": _sb(4, F32), "v5": _sb(1, F32),
-    "o4": _sb(4, U16), "lp": _sb(K, F32), "lx": _sb(K, F32), "os16": _sb(16 * R, U16),
-    "tx": _sb(B, F32), "tr": _sb(24, F32), "tp": _sb(24, F32), "ot": _sb(24, U16),
-    "zc": _sb(C, BF), "zp": _sb(C, F32), "zx": _sb(C, F32), "th": _sb(1, F32),
-    "ea": _sb(72, F32), "en": _sb(72, F32), "eb": _sb(72, F32), "ec": _sb(72, F32), "ed": _sb(72, F32), "oe": _sb(72, U16),
-    "lab": _sb(192, F32), "ik": _sb(192, F32), "gl": _sb(C, F32), "ku": _sb(4, F32), "base": _sb(3, F32),
-    "yo": _sb(C, F32), "obo": _sb(C, F32),
-    "pp": ("psum", [128, 512], F32), "pc": ("psum", [128, 512], F32),
-    "pd0": ("psum", [128, 512], F32), "pd1": ("psum", [128, 512], F32), "pd2": ("psum", [128, 512], F32), "pd3": ("psum", [128, 512], F32),
-    "py0": ("psum", [128, 512], F32), "py1": ("psum", [128, 512], F32),
+SIZES = {
+    BF: dict(w0=WW, w1=WW, ut=512, vt=512, ones=128, ff=1040, b2=512, ct=4 * 928, junk=2448, junk2=384, tt=512, st=512, sd=C,
+             dseg=C, iq=160, ind=192, zero=192, pf=192, le=336, zc=C),
+    Q4: dict(xq=4 * C, lq=128 + R * K, uq=128, uq2=128, vq=128, wq=512, eq=512, bq=128, cq=928, tq=128, sq=128 * R),
+    U8: dict(xs=4 * C, ls=128 + R * K, us=128, us2=128, vs=128, wp=512, es=512, bs=128, cs=928, ts=128, ss=128 * R),
+    I32: dict(pi=2, ci=6, oui=8),
+    U16: dict(ou=8, r16=18, o4=4, os16=16, ot=24, oe=72),
+    F32: dict(n0=1, n1=1, n2=1, gj=128, cf=6, cc=20, i16=C, i4=C, it16=72, it4=72, mx=C, hd=C, d1=C, d4=C, kk=18, thr=4, j4=4,
+              e4=4, pg=C, src=C, aa=C, hh=C, rs=18, adj=18, ext=C, zz=304, kd=160, kr=160, kt=64, mm=6, acc=4, v5=1, lp=K, lx=K,
+              tx=B, tr=24, tp=24, zp=C, zx=C, th=1, ea=72, en=72, eb=72, ec=72, ed=72, lab=192, ik=192, gl=C, ku=4, base=3,
+              yo=C, obo=C),
 }
+SCRATCH = {n: ("sbuf", [128, k], d) for d in SIZES for n, k in SIZES[d].items()}
+SCRATCH.update({n: ("psum", [128, 512], F32) for n in ("pp", "pc", "pd0", "pd1", "pd2", "pd3", "py0", "py1")})
 SEMAPHORES = ["qv", "qs", "qt", "qg", "sent", "lx", "lu", "lv", "lw", "lp", "so", "sc", "sy", "s0", "s1", "s2", "s3",
-              "an0", "an1", "an2", "ax0", "ax1", "ax2", "al0", "al1", "al2"]
+              "an0", "an1", "an2", "ax0", "ax1", "ax2"]
 A, ACT = AluOpType, ActivationFunctionType
 
 
@@ -179,8 +161,7 @@ def rank_program(g, core, T, topo):
 
     for t in range(R):
         arrives("an%d" % t, nin, [r("n%d" % t)])
-        arrives("al%d" % t, nin, [r("l%d" % t)])
-        arrives("ax%d" % t, 2 * nin, [r("lq", C * t, C * t + C), r("ls", C * t, C * t + C)])
+        arrives("ax%d" % t, 2 * nin, [r("lq", LO[t], LO[t] + KT[t]), r("ls", LO[t], LO[t] + KT[t])])
 
     x0 = r("w0", 0, 4 * C)
     dma("y", "lx", ap(x0), T.x[:], [], [x0])
@@ -203,6 +184,9 @@ def rank_program(g, core, T, topo):
     iota(r("it16"), [[16, 72]], 0)
     iota(r("src"), [[B + 512, 3], [1, B]], -144)
     iota(r("i4"), [[0, 72], [1, 4]], 0)
+    iota(r("j4"), [[1, 4]], 3)
+    iota(r("zc", 0, B), [[1, B]], 1)
+    iota(r("pg"), [[1, C]], -144)
 
     act(r("ct", 4 * 672, 4 * 800), r("st"), ACT.Copy)
     act(r("ct", 4 * 848, 4 * 928), r("st", 0, 320), ACT.Copy)
@@ -229,9 +213,6 @@ def rank_program(g, core, T, topo):
         act(r("b2", b, 512, 4), r("gj"), ACT.Relu, bias=1.0, scale=-1.0)
     for b, a in enumerate((2, 522, 0, 520)):
         quant("eq", "es", 128 * b, 128 * b + 128, r("ff", a, a + 512))
-    fill(r("kd", 0, B), -1.0)
-    fill(r("kd", B, 160), 0.0)
-    fill(r("zz", C, 304), 1.0e6)
     quant("uq", "us", 0, 128, r("ut"))
     fill(col("rs", 0), 0.0)
     put("v", lambda: g.vector.tensor_copy(T.uq2[:, 0:128].bitcast(dt.uint32), T.uq[:, 0:128].bitcast(dt.uint32).indirect(T.ou[:, 0:8])),
@@ -241,34 +222,38 @@ def rank_program(g, core, T, topo):
     act(ck, z0, bias=t1, scale=-65024.0)
     act(r("sd"), r("i16"), ACT.Sign)
     act(r("d1"), r("d1"), scale=65536.0)
-    act(r("kk"), r("it16", 0, 18), bias=ck)
     act(mq, q_, bias=M, scale=0.0625)
-    act(t3, q_, bias=B + 0.5)
-    act(t4, q_, scale=S)
-    act(col("kd", 96), h_, scale=131072.0)
-    act(col("kd", 112), h_, bias=131072.0, scale=-262144.0)
-    act(col("kd", 128), h_, bias=t2, scale=262144.0)
-    act(col("kd", 144), h_, bias=131072.0, scale=-262144.0)
+    act(r("kk"), r("it16", 0, 18), bias=ck)
     act(r("src"), r("src"), scale=S)
-    act(r("iq", B, 160), r("st", 0, 64), ACT.Copy)
-    act(r("zero"), r("st", 0, 192), ACT.Copy)
 
     def late_constants():
+        act(r("kd", 0, B), r("st", 256, 352), bias=-1.0)
+        act(r("kd", B, 160), r("st", 256, 320), ACT.Copy)
+        act(r("iq", B, 160), r("st", 256, 320), ACT.Copy)
+        act(r("zz", C, 304), r("st", 256, 272), bias=1.0e6)
+        act(col("kd", 96), h_, scale=131072.0)
+        act(col("kd", 112), h_, bias=131072.0, scale=-262144.0)
+        act(col("kd", 128), h_, bias=t2, scale=262144.0)
+        act(col("kd", 144), h_, bias=131072.0, scale=-262144.0)
         act(r("d4"), r("i4"), ACT.Abs, bias=r_, scale=-1.0)
-        act(r("thr"), r("it16", 0, 4), bias=t3)
-        act(cl0, q4, bias=4.0 * 144 - 3 * 32768.0)
+        act(t3, q_, bias=B + 0.5)
+        act(r("zero"), r("st", 256, 448), ACT.Copy)
         act(r("d4"), r("d4"), ACT.Sign)
-        act(ctl, q4, bias=4.0 * 144)
-        act(cz0, q4, bias=4.0 * (NY - 1) * S - 3, scale=S)
+        act(r("thr"), r("it16", 0, 4), bias=t3)
+        act(cl0, q4, bias=4.0 * (144 + ND) - 3 * 32768.0)
         act(r("d4"), r("d4"), bias=-7.0, scale=8.0)
         act(cl, r_, bias=cl0, scale=32768.0)
+
+    def last_constants():
+        act(ctl, q4, bias=4.0 * 144)
+        act(cz0, q4, bias=4.0 * (NY - 1) * S - 3, scale=S)
+        act(t4, q_, scale=S)
         act(cz1, q4, bias=(4.0 * (NY - 1) + 0.5) * S, scale=S)
-        act(cth, q4, bias=4.0 * (NH - 1 - M) * S, scale=S)
         act(cz, r_, bias=cz0)
+        act(cth, q4, bias=4.0 * (NH - 1 - M) * S, scale=S)
         act(r("it4"), r("it16"), bias=t4, scale=S)
-        act(r("tt", 4 * B, 512), r("st", 0, 128), ACT.Copy)
-        act(r("dp", 4 * C, 4 * C + 16), r("st", 0, 16), ACT.Copy)
-        act(r("pg"), r("pg"), scale=S)
+        act(r("tt", 4 * B, 512), r("st", 256, 384), ACT.Copy)
+        act(r("w1", WW - 16, WW), r("st", 256, 272), ACT.Copy)
 
     pd = ["pd0", "pd1", "pd2", "pd3"]
     py = ["py0", "py1", "pp", "pc"]
@@ -277,21 +262,22 @@ def rank_program(g, core, T, topo):
         k = (18 - m) // 4
         return r("ct", 4 * CT[k] + (18 - m) % 4, 4 * (CT[k] + 16 * m), 4)
 
+    def jview(m):
+        return r("junk", 8 * m * (m - 1), 8 * m * (m + 1))
+
     for t in range(R):
         w, wn = "w%d" % (t % 2), "w%d" % ((t + 1) % 2)
         win = r(w)
         more = t < R - 1
         m1, m2 = col("mm", 2 * t), col("mm", 2 * t + 1)
         xa, xb = C * t, C * t + C
+        kt, lo = KT[t], LO[t]
+        n4 = (kt + 15) // 16
+        h4 = 2 * n4
         quant("xq", "xs", xa, xb, r(w, 0, 4 * C))
         mm("pp", "uq2", "us2", 0, "xq", "xs", xa, xb)
         mm("py0", "uq2", "us2", 0, "xq", "xs", xa, xb)
-        send(u8(r("lq", xa, xb)), u8(r("xq", xa, xb)), "ax%d" % t, [r("xq", xa, xb)])
-        send(ap(r("ls", xa, xb)), ap(r("xs", xa, xb)), "ax%d" % t, [r("xs", xa, xb)])
         if t == 0:
-            iota(r("j4"), [[1, 4]], 3)
-            iota(r("zc", 0, B), [[1, B]], 1)
-            iota(r("pg"), [[1, C]], -144)
             quant("bq", "bs", 0, 128, r("b2"))
             ts(col("ku", 0), q_, 2.5, A.is_gt, 65536.0 - B, A.mult)
             fill(r("le", 160, 336, 168), -128.0)
@@ -305,16 +291,13 @@ def rank_program(g, core, T, topo):
             tt(r("aa", a, b), r("pp", a, b), r("mx", a, b), A.min)
         for a, b in ((SP, C), (0, SP)):
             scan(r("hh", a, b), r("hd", a, b), r("aa", a, b), -BIG, A.min, A.max)
-        jo = 0
+        for m in ON_SCALAR:
+            act(jview(m), r("py0", 0, 16 * m), ACT.Sign, bias=col("hh", 16 * m + 15), scale=-1.0)
+        for m in ON_SCALAR:
+            act(cview(m), jview(m), ACT.Relu, acc=col("rs", m))
         for m in ORDER:
-            jv = r("junk", jo, jo + 16 * m)
-            jo += 16 * m
-            if m in ON_SCALAR:
-                act(jv, r("py0", 0, 16 * m), ACT.Sign, bias=col("hh", 16 * m + 15), scale=-1.0)
-                act(cview(m), jv, ACT.Relu, acc=col("rs", m))
-            else:
-                ts(cview(m), r("pp", 0, 16 * m), col("hh", 16 * m + 15), A.is_lt)
-                act(jv, cview(m), acc=col("rs", m))
+            ts(cview(m), r("pp", 0, 16 * m), col("hh", 16 * m + 15), A.is_lt)
+            act(jview(m), cview(m), acc=col("rs", m))
             if m == 16:
                 tt(dv, r("hh"), r("pp", 0, C), A.is_ge)
             if m in QUANT_AFTER:
@@ -327,9 +310,7 @@ def rank_program(g, core, T, topo):
         if t == 0:
             late_constants()
         for b in range(4):
-            act(r(w, 4 * ND + b, WW, 4), r(pd[b], 0, C), ACT.Copy)
-        for b in range(4):
-            mm(pd[b], "eq", "es", 128 * b, "lq", "ls", xa, xb)
+            act(r(w, 4 * ND + b, WW - 16, 4), r(pd[b], 0, C), ACT.Copy)
         tt(r("adj"), r("kk"), r("dseg", 15, C, 16), A.subtract)
         tt(r("d1", 15, C, 16), r("adj"), r("rs"), A.subtract)
         scan(r("ext"), r("pc", 0, C), r("d1"), -65024.0, A.max, A.add)
@@ -346,19 +327,26 @@ def rank_program(g, core, T, topo):
         scan(r("pf"), r("ind"), r("zero"), float(B), A.add, A.add)
         for k in (0, 1):
             act(r("junk2", 192 * k, 192 * k + 192), r("pf"), ACT.Sign, bias=col("thr", k), scale=-1.0, acc=col("acc", k))
-        for k in (2, 3):
+        for k in range(2, n4):
             ts(r("le", 168 * (k - 2), 168 * (k - 2) + 160), r("pf", 32, 192), col("thr", k), A.is_lt, 2.0, A.mult)
-        for k in (2, 3):
+        for k in range(2, n4):
             red(col("acc", k), r("le", 168 * (k - 2), 168 * (k - 2) + 161), A.add)
-        ts(r("o4"), r("acc"), 192.0, A.add, 0.5, A.mult)
-        ts(r("lp"), (r("zz", B, C + 1), r("o4")), r("v5"), A.subtract, 144.0 * S, A.min)
-        scan(r("lx"), r("d4", 0, K), r("lp"), 0.0, A.add, A.max)
-        ol = r("os16", 16 * t, 16 * t + 16)
-        ts(ol, r("lx", 3, K, 4), 32768.0, A.mult, cl, A.add)
-        send(T["l%d" % t][:, 0:16], ap(ol), "al%d" % t, [ol])
-        for b in range(2):
-            act(r("dp", b, 4 * C, 4), r(pd[b], 0, C), ACT.Copy)
-        scan(r("tx"), r("d4", 0, B), r("zz", 0, B), 0.0, A.add, A.max)
+        if t == 0:
+            act(r("w0", WW - 16, WW), r("st", 256, 272), ACT.Copy)
+        else:
+            scan(r("tx"), r("d4", 0, B), r("zz", 0, B), 0.0, A.add, A.max)
+        ts(r("o4", 0, n4), r("acc", 0, n4), 192.0, A.add, 0.5, A.mult)
+        ts(r("lp", 0, 16 * n4), (r("zz", B, C + 1), r("o4", 0, n4)), r("v5"), A.subtract, 144.0 * S, A.min)
+        scan(r("lx", 0, kt), r("d4", 0, kt), r("lp", 0, kt), 0.0, A.add, A.max)
+        ts(r("os16", 0, kt // 4), r("lx", 3, kt, 4), 32768.0, A.mult, cl, A.add)
+        cp(r("st", 0, 16 * h4), (win, r("os16", 0, h4)))
+        act(r("st", 16 * h4, 4 * kt), (win, r("os16", h4, kt // 4)), ACT.Copy)
+        quant("sq", "ss", 128 * t, 128 * t + 128, r("st"))
+        send(u8(r("lq", lo, lo + kt)), u8(r("sq", 128 * t, 128 * t + kt)), "ax%d" % t, [r("sq", 128 * t, 128 * t + kt)])
+        send(ap(r("ls", lo, lo + kt)), ap(r("ss", 128 * t, 128 * t + kt)), "ax%d" % t, [r("ss", 128 * t, 128 * t + kt)])
+        if t == 0:
+            last_constants()
+            scan(r("tx"), r("d4", 0, B), r("zz", 0, B), 0.0, A.add, A.max)
         tt(r("zc", B, C), r("ind"), r("pf"), A.mult)
         ts(r("tr"), r("tx", 3, B, 4), M, A.add, M, A.subtract)
         ts(r("lab"), r("zz", B, C), M, A.add, M, A.subtract)
@@ -367,60 +355,57 @@ def rank_program(g, core, T, topo):
         ts(r("ot"), r("tp"), 32768.0, A.mult, ctl, A.add)
         act(r("zp"), (r("zc"), r("r16")), bias=cz, scale=4.0 * S)
         act(r("tt", 0, 4 * B), (win, r("ot")), ACT.Copy)
-        for b in range(2, 4):
-            act(r("dp", b, 4 * C, 4), r(pd[b], 0, C), ACT.Copy)
-        ts(r("ik"), r("ind"), (4 + 2 * t) / 16, A.mult)
+        act(r("ik"), r("ind"), scale=(4 + 2 * t) / 16)
         if t == 0:
+            act(r("pg"), r("pg"), scale=S)
             ts(r("e4"), r("j4"), q_, A.is_equal)
+            quant("lq", "ls", 0, 128, r("st"))
+        ts(r("th"), r("n%d" % t), 4.0 * S, A.mult, cth, A.add)
         if more:
             ts(col("ku", 1), col("kr", B - 1), m1, A.is_equal, 65536.0, A.mult)
-        tt(r("gl", B, C), r("lab"), r("ik"), A.max)
         scan(r("zx"), r("d4"), r("zp"), 0.0, A.add, A.max)
         x = r("zx", 3, C, 4)
         if more:
             ts(col("ku", 2), m2, M + 65536.0, A.subtract, col("e4", 2 * t + 1), A.mult)
-            ts(col("ku", 3), col("e4", 2 * t), B - 65536.0, A.mult, col("kr", B - 1), A.add)
         ts(r("en"), x, cz1, A.is_gt, 4.0 * ND * S, A.mult)
+        ts(r("ea"), x, r("th"), A.is_gt)
         quant("tq", "ts", 0, 128, r("tt"))
         for b in range(4):
             mm(py[b], "wq", "wp", 128 * b, "tq", "ts", 0, 128)
         for b in range(4):
             act(r(w, 4 * NY + b, 4 * NH, 4), r(py[b], 0, B), scale=0.03125)
-        ts(r("th"), r("n%d" % t), 4.0 * S, A.mult, cth, A.add)
         tt(r("ec"), r("en"), r("it4"), A.add)
-        ts(r("ea"), x, r("th"), A.is_gt)
+        tt(r("eb"), r("ea"), x, A.add)
+        if more:
+            ts(col("ku", 3), col("e4", 2 * t), B - 65536.0, A.mult, col("kr", B - 1), A.add)
+        tt(r("ed"), r("ec"), r("eb"), A.min)
+        tt(r("gl", B, C), r("lab"), r("ik"), A.max)
+        ts(r("oe"), r("ed"), 8192.0, A.mult)
         if more:
             ts(col("base", t + 1), col("ku", 3), col("ku", 2), A.add, col("ku", 1), A.add)
-        tt(r("eb"), r("ea"), x, A.add)
-        if not more:
-            quant("vq", "vs", 0, 128, r("vt"))
-        tt(r("ed"), r("ec"), r("eb"), A.min)
-        ts(r("oe"), r("ed"), 8192.0, A.mult)
-        cp(r("st", 0, 128), (r("dp"), r("l%d" % t, 0, 8)))
-        act(r("st", 128, 256), (r("dp"), r("l%d" % t, 8, 16)), ACT.Copy)
-        quant("sq", "ss", 0, 128, r("st"))
-        for b in (0, 2, 1, 3):
-            mm(pd[b], "wq", "wp", 128 * b, "sq", "ss", 0, 128)
-        if more:
             tt(r("src", 0, 128), (r("gl"), r("r16", 0, 8)), r("pg", 0, 128), A.add)
+        else:
+            quant("vq", "vs", 0, 128, r("vt"))
+            act(r("obo"), (r("gl"), r("r16")), scale=16.0)
+            dma("y", "so", T.ob[:], T.obo[0:128:16, :], [r("obo")], [])
         for b in (0, 2, 1, 3):
-            o = r(w, 4 * NH + b, 4 * ND, 4)
+            mm(pd[b], "wq", "wp", 128 * b, "lq", "ls", lo + kt - 128, lo + kt)
+        for b in (0, 2, 1, 3):
+            o = r(w, 4 * NH + b, 4 * (NH + kt), 4)
             if b < 2:
-                ts(o, r(pd[b], 0, K), 0.03125, A.mult)
+                ts(o, r(pd[b], 128 - kt, 128), 0.03125, A.mult)
             else:
-                act(o, r(pd[b], 0, K), scale=0.03125)
+                act(o, r(pd[b], 128 - kt, 128), scale=0.03125)
         cp(r(wn, 0, 576), (win, r("oe", 0, 36)))
         act(r(wn, 576, 1152), (win, r("oe", 36, 72)), ACT.Copy)
 
     xa, xb = R * C, R * C + C
-    act(r("obo"), (r("gl"), r("r16")), scale=16.0)
     quant("xq", "xs", xa, xb, r("w%d" % (R % 2), 0, 4 * C))
     mm("pp", "vq", "vs", 0, "xq", "xs", xa, xa + C // 2)
     mm("pc", "vq", "vs", 0, "xq", "xs", xa + C // 2, xb)
     dma("y", "sc", T.oc[:], u8(r("xq", xa, xb)), [r("xq", xa, xb)], [])
     for k in range(4):
         dma("y", "s%d" % k, T.osc[4 * k:4 * k + 4, :], T.xs[32 * k:32 * k + 4, xa:xb], [r("xs", xa, xb)], [])
-    dma("y", "so", T.ob[:], T.obo[0:128:16, :], [r("obo")], [])
     act(r("yo", 0, C // 2), r("pp", 0, C // 2), ACT.Copy)
     cp(r("yo", C // 2, C), r("pc", 0, C // 2))
     dma("s", "sy", T.y[:], T.yo[:], [r("yo")], [])

@@ -1,36 +1,38 @@
 from concourse.mybir import dt, AluOpType, AxisListType, ActivationFunctionType
 
 C, B, K, R = 288, 96, 64, 3
-NY, NH, ND = 288, 384, 448
-WW = 4 * (ND + C) + 16
-S = 1.0 / 8192
-M = 1.5 * 2.0 ** 19
+HF = C // 2
+NY, NH, NS = 288, 384, 448
+WW = 4 * (NS + 128)
+U, EPS = 2.0 ** -8, 2.0 ** -17
+S = 2.0 ** -12
+MLO, MHI = 1.5 * 2.0 ** 15, 1.5 * 2.0 ** 23
+GONE = 512.0
 BIG = 1.0e28
-CT = [0, 288, 512, 800, 672]
+CT = [0, 288, 512, 672, 768]
 CW = [288, 224, 160, 128, 128]
-ORDER = [16, 15, 13, 12, 11, 10, 9, 8, 7, 2, 1, 6, 5, 4, 3]
+ORDER = [16, 15, 13, 12, 11, 10, 9, 8, 7, 6, 5, 4, 3, 2, 1]
 ON_SCALAR = (17, 14)
-QUANT_AFTER = {13: (0, 288), 10: (288, 512), 6: (512, 704)}
-SP = 192
+QUANT_AFTER = {13: (0, 288), 10: (288, 512), 6: (512, 672)}
 KT = [64, 48, 40]
 LO = [128, 192, 240]
 
 F32, BF, I32, U16, Q4, U8 = "float32", "bfloat16", "int32", "uint16", "float8_e4m3fn_x4", "uint8"
 SIZES = {
-    BF: dict(w0=WW, w1=WW, ut=512, vt=512, ones=128, ff=1040, b2=512, ct=4 * 928, junk=2448, junk2=384, tt=512, st=512, sd=C,
-             dseg=C, iq=160, ind=192, zero=192, pf=192, le=336, zc=C),
-    Q4: dict(xq=4 * C, lq=128 + R * K, uq=128, uq2=128, vq=128, wq=512, eq=512, bq=128, cq=928, tq=128, sq=128 * R),
-    U8: dict(xs=4 * C, ls=128 + R * K, us=128, us2=128, vs=128, wp=512, es=512, bs=128, cs=928, ts=128, ss=128 * R),
+    BF: dict(w0=WW, w1=WW, dd=4 * C + 4, ut=512, vt=512, ones=128, ff=1040, b2=512, ct=4 * 896, junk=2448, junk2=384, tt=512, zer=512,
+             sd=C, dseg=C, ind=192, in2=192, pf=192, le=320, rl=320, lc=320, zc=C),
+    Q4: dict(xq=4 * C, lq=128 + R * K, uq=128, uq2=128, vq=128, wq=512, eq=512, bq=128, cq=896, tq=128, sq=128 * R),
+    U8: dict(xs=4 * C, ls=128 + R * K, us=128, us2=128, vs=128, wp=512, es=512, bs=128, cs=896, ts=128, ss=128 * R),
     I32: dict(pi=2, ci=6, oui=8),
     U16: dict(ou=8, r16=18, o4=4, os16=16, ot=24, oe=72),
-    F32: dict(n0=1, n1=1, n2=1, gj=128, cf=6, cc=20, i16=C, i4=C, it16=72, it4=72, mx=C, hd=C, d1=C, d4=C, kk=18, thr=4, j4=4,
-              e4=4, pg=C, src=C, aa=C, hh=C, rs=18, adj=18, ext=C, zz=304, kd=160, kr=160, kt=64, mm=6, acc=4, v5=1, lp=K, lx=K,
-              tx=B, tr=24, tp=24, zp=C, zx=C, th=1, ea=72, en=72, eb=72, ec=72, ed=72, lab=192, ik=192, gl=C, ku=4, base=3,
-              yo=C, obo=C),
+    F32: dict(n0=1, n1=1, n2=1, gj=128, ga=128, cf=6, cc=24, i16=C, i4=C, it16=72, it4=72, mx=C, hd=C, d1=C, d4=C, kk=18, thr=4, jl=10,
+              ju=10, e9=10, fl=10, flm=10, flu=10, pg=C, src0=C, src1=C, aa=C, hh=C, rs=18, adj=18, ext=C, zz=C + 64, kd=256, kr=256,
+              kt=64, kb=64, ke=32, mm=6, acc=2, lz=192, lp=K, lx=K, tx=B, tr=24, tp=24, zp=C, zx=C, th=1, ea=72, eb=72, ec=72,
+              da=B, dl=C, ku=1, base=3, yo=C, oba=C, obo=C),
 }
 SCRATCH = {n: ("sbuf", [128, k], d) for d in SIZES for n, k in SIZES[d].items()}
 SCRATCH.update({n: ("psum", [128, 512], F32) for n in ("pp", "pc", "pd0", "pd1", "pd2", "pd3", "py0", "py1")})
-SEMAPHORES = ["qv", "qs", "qt", "qg", "sent", "lx", "lu", "lv", "lw", "lp", "so", "sc", "sy", "s0", "s1", "s2", "s3",
+SEMAPHORES = ["qv", "qs", "qt", "qg", "sent", "lx", "ly", "lu", "lv", "lw", "lp", "so", "sc", "sy", "s0", "s1", "s2", "s3",
               "an0", "an1", "an2", "ax0", "ax1", "ax2"]
 A, ACT = AluOpType, ActivationFunctionType
 
@@ -163,97 +165,80 @@ def rank_program(g, core, T, topo):
         arrives("an%d" % t, nin, [r("n%d" % t)])
         arrives("ax%d" % t, 2 * nin, [r("lq", LO[t], LO[t] + KT[t]), r("ls", LO[t], LO[t] + KT[t])])
 
-    x0 = r("w0", 0, 4 * C)
-    dma("y", "lx", ap(x0), T.x[:], [], [x0])
+    xhi, xlo = r("w0", 2 * C, 4 * C), r("w0", 0, 2 * C)
+    dma("y", "lx", ap(xhi), T.x[:, 2 * C:4 * C], [], [xhi])
     dma("s", "lu", T.ut[:], T.u[:], [], [r("ut")])
-    dma("y", "lw", u8(r("wq")), T.wc[:], [x0], [r("wq")])
+    dma("y", "ly", ap(xlo), T.x[:, 0:2 * C], [], [xlo])
+    dma("y", "lw", u8(r("wq")), T.wc[:], [xlo], [r("wq")])
     dma("y", "lp", T.wp[:], T.ws[:], [], [r("wp")])
     dma("y", "lv", T.vt[:], T.v[:], [], [r("vt")])
 
     q_, qm1, h_, r_, q4, g_ = (col("cf", j) for j in range(6))
-    mq, z0, t0, ccs, ck, cl0, cl, ctl, cz0, cz, cth, t1, cz1, t2, t3, t4 = (col("cc", j) for j in range(16))
-    fill(r("st"), 0.0)
+    mq, z0, t0, ccs, ck, cl0, cl, ctl, cz0, cz, cth, t1, cu, c1, t3, t4, dv_, e2, fv, dl_, eg, b1, b2_ = (col("cc", j) for j in range(23))
+    zer = r("zer")
     fill(r("ones"), 1.0)
-    fill(r("ff"), 0.0)
+    fill(r("ff", 0, 520), 0.0)
     iota(r("pi"), [[15, 2]], 0, 1)
-    iota(r("oui"), [[16, 8]], 0)
     iota(r("i16"), [[0, 18], [1, 16]], 0)
+    iota(r("oui"), [[16, 8]], 0)
+    iota(r("gj"), [[1, 8], [0, 16]], 0)
+    act(r("ff", 520, 1040), r("ff", 0, 520), ACT.Copy)
+    fill(zer, 0.0)
     ident(r("ff", 2, 514, 4))
     ident(r("ff", 523, 1035, 4))
-    iota(r("gj"), [[1, 8], [0, 16]], 0)
     iota(r("it16"), [[16, 72]], 0)
-    iota(r("src"), [[B + 512, 3], [1, B]], -144)
-    iota(r("i4"), [[0, 72], [1, 4]], 0)
-    iota(r("j4"), [[1, 4]], 3)
-    iota(r("zc", 0, B), [[1, B]], 1)
+    iota(r("jl"), [[1, 10]], 0)
     iota(r("pg"), [[1, C]], -144)
+    iota(r("i4"), [[0, 72], [1, 4]], 0)
+    iota(r("zc", 0, B), [[1, B]], 1)
+    iota(r("kd", 0, 192), [[0, 192]], 0)
+    iota(r("zz", C, C + 64), [[0, 64]], 0)
+    iota(r("rl"), [[0, 320]], 1)
+    iota(r("rl", 7, 176, 168), [[0, 2]], 0)
+    iota(r("le", 0, 8), [[0, 8]], 32)
+    iota(r("le", 168, 176), [[0, 8]], 48)
+    iota(r("dd", 0, 4), [[0, 4]], 0)
+    iota(r("w0", 4 * (NS + K), WW), [[0, 256]], 0)
+    iota(r("tt", 4 * B, 512), [[0, 128]], 0)
+    iota(r("w1", 4 * (NS + KT[1]), WW), [[0, WW - 4 * (NS + KT[1])]], 0)
 
-    act(r("ct", 4 * 672, 4 * 800), r("st"), ACT.Copy)
-    act(r("ct", 4 * 848, 4 * 928), r("st", 0, 320), ACT.Copy)
     ts(r("ci", 0, 2), r("pi"), 15, A.bitwise_and)
     ts(col("ci", 2), col("pi", 0), 4, A.logical_shift_right, 1, A.bitwise_and)
     ts(col("ci", 3), col("pi", 0), 2, A.logical_shift_right, 3, A.bitwise_and)
     ts(col("ci", 4), col("pi", 0), 3, A.bitwise_and)
     ts(col("ci", 5), col("pi", 0), 4, A.logical_shift_right)
-    cp(r("ou"), r("oui"))
-    cp(r("cf"), r("ci"))
-    for a in (240, 464, 624):
+    for a in (240, 464):
         fill(r("ct", 4 * a, 4 * a + 192), 0.0)
-    ts(r("mx"), r("i16"), q_, A.is_equal, 0.5, A.subtract)
-    ts(r("d1"), r("i16"), qm1, A.not_equal, 1.0 - 1.0 / 128, A.subtract)
-    quant("cq", "cs", 672, 800, r("ct", 4 * 672, 4 * 800))
+    cp(r("cf"), r("ci"))
+    cp(r("ou"), r("oui"))
+    fill(r("ct", 4 * 624, 4 * 624 + 192), 0.0)
+    ts(r("mx"), r("i16"), q_, A.not_equal, -BIG, A.mult)
     act(r("hd"), r("i16"), bias=-0.5 * BIG, scale=BIG)
-    act(r("mx"), r("mx"), scale=BIG)
-    act(r("gj"), r("gj"), ACT.Abs, bias=g_, scale=-1.0)
+    act(r("ct", 4 * 768, 4 * 896), zer, ACT.Copy)
+    act(r("ct", 4 * 720, 4 * 768), r("zer", 0, 192), ACT.Copy)
+    act(r("ga"), r("gj"), ACT.Abs, bias=g_, scale=-1.0)
     act(z0, q_, ACT.Relu, bias=1.0, scale=-1.0)
     act(t0, q_, bias=-7680.0, scale=512.0)
-    act(t1, q_, bias=15.0, scale=-1.0)
-    act(t2, q_, bias=-131072.0, scale=-0.0625)
     for b in range(4):
-        act(r("b2", b, 512, 4), r("gj"), ACT.Relu, bias=1.0, scale=-1.0)
-    for b, a in enumerate((2, 522, 0, 520)):
-        quant("eq", "es", 128 * b, 128 * b + 128, r("ff", a, a + 512))
+        act(r("b2", b, 512, 4), r("ga"), ACT.Relu, bias=1.0, scale=-1.0)
     quant("uq", "us", 0, 128, r("ut"))
     fill(col("rs", 0), 0.0)
     put("v", lambda: g.vector.tensor_copy(T.uq2[:, 0:128].bitcast(dt.uint32), T.uq[:, 0:128].bitcast(dt.uint32).indirect(T.ou[:, 0:8])),
         [r("uq"), r("ou")], [r("uq2")])
     cp(r("us2"), (r("us"), r("ou")))
+    act(t1, q_, bias=15.0, scale=-1.0)
     act(ccs, z0, bias=t0, scale=65024.0)
+    act(r("ju"), r("jl"), scale=U)
     act(ck, z0, bias=t1, scale=-65024.0)
     act(r("sd"), r("i16"), ACT.Sign)
-    act(r("d1"), r("d1"), scale=65536.0)
-    act(mq, q_, bias=M, scale=0.0625)
+    act(mq, q_, bias=MLO, scale=0.0625)
+    act(cu, q_, bias=15 * U, scale=-U)
     act(r("kk"), r("it16", 0, 18), bias=ck)
-    act(r("src"), r("src"), scale=S)
 
-    def late_constants():
-        act(r("kd", 0, B), r("st", 256, 352), bias=-1.0)
-        act(r("kd", B, 160), r("st", 256, 320), ACT.Copy)
-        act(r("iq", B, 160), r("st", 256, 320), ACT.Copy)
-        act(r("zz", C, 304), r("st", 256, 272), bias=1.0e6)
-        act(col("kd", 96), h_, scale=131072.0)
-        act(col("kd", 112), h_, bias=131072.0, scale=-262144.0)
-        act(col("kd", 128), h_, bias=t2, scale=262144.0)
-        act(col("kd", 144), h_, bias=131072.0, scale=-262144.0)
-        act(r("d4"), r("i4"), ACT.Abs, bias=r_, scale=-1.0)
-        act(t3, q_, bias=B + 0.5)
-        act(r("zero"), r("st", 256, 448), ACT.Copy)
-        act(r("d4"), r("d4"), ACT.Sign)
-        act(r("thr"), r("it16", 0, 4), bias=t3)
-        act(cl0, q4, bias=4.0 * (144 + ND) - 3 * 32768.0)
-        act(r("d4"), r("d4"), bias=-7.0, scale=8.0)
-        act(cl, r_, bias=cl0, scale=32768.0)
-
-    def last_constants():
-        act(ctl, q4, bias=4.0 * 144)
-        act(cz0, q4, bias=4.0 * (NY - 1) * S - 3, scale=S)
-        act(t4, q_, scale=S)
-        act(cz1, q4, bias=(4.0 * (NY - 1) + 0.5) * S, scale=S)
-        act(cz, r_, bias=cz0)
-        act(cth, q4, bias=4.0 * (NH - 1 - M) * S, scale=S)
-        act(r("it4"), r("it16"), bias=t4, scale=S)
-        act(r("tt", 4 * B, 512), r("st", 256, 384), ACT.Copy)
-        act(r("w1", WW - 16, WW), r("st", 256, 272), ACT.Copy)
+    def tile_e(b):
+        a = (2, 522, 0, 520)[b]
+        quant("eq", "es", 128 * b, 128 * b + 128, r("ff", a, a + 512))
+        mm("pd%d" % b, "eq", "es", 128 * b, "xq", "xs", 0, C)
 
     pd = ["pd0", "pd1", "pd2", "pd3"]
     py = ["py0", "py1", "pp", "pc"]
@@ -267,29 +252,29 @@ def rank_program(g, core, T, topo):
 
     for t in range(R):
         w, wn = "w%d" % (t % 2), "w%d" % ((t + 1) % 2)
-        win = r(w)
-        more = t < R - 1
+        src, srn = "src%d" % (t % 2), "src%d" % ((t + 1) % 2)
+        more, first = t < R - 1, t == 0
         m1, m2 = col("mm", 2 * t), col("mm", 2 * t + 1)
         xa, xb = C * t, C * t + C
         kt, lo = KT[t], LO[t]
         n4 = (kt + 15) // 16
         h4 = 2 * n4
-        quant("xq", "xs", xa, xb, r(w, 0, 4 * C))
+        quant("xq", "xs", xa + HF, xb, r(w, 4 * HF, 4 * C))
+        quant("xq", "xs", xa, xa + HF, r(w, 0, 4 * HF))
+        mm("py1", "uq2", "us2", 0, "xq", "xs", xa + HF, xb)
         mm("pp", "uq2", "us2", 0, "xq", "xs", xa, xb)
         mm("py0", "uq2", "us2", 0, "xq", "xs", xa, xb)
-        if t == 0:
-            quant("bq", "bs", 0, 128, r("b2"))
-            ts(col("ku", 0), q_, 2.5, A.is_gt, 65536.0 - B, A.mult)
-            fill(r("le", 160, 336, 168), -128.0)
-            ts(col("base", 0), col("ku", 0), float(B), A.add, mq, A.add)
+        if first:
+            quant("cq", "cs", 768, 896, r("ct", 4 * 768, 4 * 896))
         else:
-            tt(r("src", 128, C), (r("gl"), r("r16", 8, 18)), r("pg", 128, C), A.add)
-        for b in range(4):
-            mm(pd[b], "eq", "es", 128 * b, "xq", "xs", xa, xb)
+            for b in range(4):
+                mm(pd[b], "eq", "es", 128 * b, "xq", "xs", xa, xb)
         dv = r("ct", 0, 4 * C, 4)
-        for a, b in ((SP, C), (0, SP)):
-            tt(r("aa", a, b), r("pp", a, b), r("mx", a, b), A.min)
-        for a, b in ((SP, C), (0, SP)):
+        tt(r("aa", HF, C), r("py1", 0, HF), r("mx", HF, C), A.add)
+        if first:
+            quant("bq", "bs", 0, 128, r("b2"))
+        tt(r("aa", 0, HF), r("pp", 0, HF), r("mx", 0, HF), A.add)
+        for a, b in ((HF, C), (0, HF)):
             scan(r("hh", a, b), r("hd", a, b), r("aa", a, b), -BIG, A.min, A.max)
         for m in ON_SCALAR:
             act(jview(m), r("py0", 0, 16 * m), ACT.Sign, bias=col("hh", 16 * m + 15), scale=-1.0)
@@ -298,96 +283,158 @@ def rank_program(g, core, T, topo):
         for m in ORDER:
             ts(cview(m), r("pp", 0, 16 * m), col("hh", 16 * m + 15), A.is_lt)
             act(jview(m), cview(m), acc=col("rs", m))
-            if m == 16:
+            if m == ORDER[0]:
                 tt(dv, r("hh"), r("pp", 0, C), A.is_ge)
             if m in QUANT_AFTER:
                 a, b = QUANT_AFTER[m]
                 quant("cq", "cs", a, b, r("ct", 4 * a, 4 * b))
-        scan(r("dseg"), r("sd"), dv, 0.0, A.mult, A.add)
-        quant("cq", "cs", 800, 928, r("ct", 4 * 800, 4 * 928))
-        for k in (0, 1, 2, 4, 3):
-            mm("pc", "bq", "bs", 0, "cq", "cs", CT[k], CT[k] + CW[k], start=(k == 0), stop=(k == 3))
-        if t == 0:
-            late_constants()
-        for b in range(4):
-            act(r(w, 4 * ND + b, WW - 16, 4), r(pd[b], 0, C), ACT.Copy)
-        tt(r("adj"), r("kk"), r("dseg", 15, C, 16), A.subtract)
-        tt(r("d1", 15, C, 16), r("adj"), r("rs"), A.subtract)
-        scan(r("ext"), r("pc", 0, C), r("d1"), -65024.0, A.max, A.add)
-        ts(r("r16"), r("ext", 15, C, 16), ccs, A.add)
-        cp((r("zz", 0, C), r("r16")), r("src"))
-        ts(r("iq", 0, B), r("zz", 0, B), M, A.add, mq, A.not_equal)
-        scan(r("kr"), r("iq"), r("kd"), col("base", t), A.add, A.add)
-        put("v", lambda: g.vector.transpose(T.kt[:, 0:64], T.kr[:, B:160]), [r("kr", B, 160)], [r("kt")])
+            if first and m == ORDER[1]:
+                ts(r("d1"), r("i16"), qm1, A.not_equal, 1.0 - 1.0 / 128, A.subtract)
+                ts(r("e9"), r("jl"), q_, A.is_equal)
+            if first and m == ORDER[3]:
+                act(r("d1"), r("d1"), scale=65536.0)
+                tt(r("fl"), r("e9"), r("ju"), A.add)
+            if m == 13:
+                scan(r("dseg"), r("sd"), dv, 0.0, A.mult, A.add)
+            if m == 10:
+                tt(r("adj"), r("kk"), r("dseg", 15, C, 16), A.subtract)
+        for k in (0, 1, 2):
+            mm("pc", "bq", "bs", 0, "cq", "cs", CT[k], CT[k] + CW[k], start=(k == 0), stop=(k == 2))
+            mm("py1", "bq", "bs", 0, "cq", "cs", CT[k], CT[k] + 128, start=(k == 0), stop=False)
+        if first:
+            for b in (1, 2, 0):
+                act(r(src, B * b, B * b + B), r("pg", B * b, B * b + B), bias=col("fl", b), scale=EPS)
+            act(col("zz", C), col("zer", 0), bias=-MHI)
+        else:
+            for b in range(4):
+                act(r("dd", 4 + b, 4 + 4 * C, 4), r(pd[b], 0, C), ACT.Copy)
+        tt(r("d1", B + 15, C, 16), r("adj", 6, 18), r("rs", 6, 18), A.subtract)
+        quant("cq", "cs", 672, 800, r("ct", 4 * 672, 4 * 800))
+        for k in (3, 4):
+            mm("py1", "bq", "bs", 0, "cq", "cs", CT[k], CT[k] + 128, start=False, stop=(k == 4))
+        scan(r("ext", B, C), r("pc", B, C), r("d1", B, C), -65024.0, A.max, A.add)
+        if first:
+            ts(r("kb", 32, 64), r("gj", 0, 32), h_, A.not_equal, 4096.0, A.mult)
+            ts(r("ke"), r("i16", 0, 32), q_, A.not_equal, cu, A.mult)
+        ts(r("r16", 6, 18), r("ext", B + 15, C, 16), ccs, A.add)
+        tt(r("d1", 15, B, 16), r("adj", 0, 6), r("rs", 0, 6), A.subtract)
+        if first:
+            tt(r("kb", 0, 32), r("kb", 32, 64), r("ke"), A.add)
+        scan(r("ext", 0, B), r("py1", 0, B), r("d1", 0, B), -65024.0, A.max, A.add)
+        cp((r("zz", 0, C), r("r16", 6, 18)), r(src, B, C))
+        ts(r("r16", 0, 6), r("ext", 15, B, 16), ccs, A.add)
+        if first:
+            ts(col("kd", 192), col("kb", 0), mq, A.add)
+            tt(r("kd", 193, 256), r("kb", 1, 64), r("kb", 0, 63), A.subtract)
+            act(r("d4"), r("i4"), ACT.Abs, bias=r_, scale=-1.0)
+            act(col("ku", 0), q_, ACT.Sign, bias=-2.5)
+            act(t3, q_, bias=B + 0.5)
+            act(r("d4"), r("d4"), ACT.Sign)
+            act(col("base", 0), col("ku", 0), bias=MHI + GONE / 2, scale=GONE / 2)
+            act(r("thr"), r("it16", 0, 4), bias=t3)
+            act(r("d4"), r("d4"), bias=-14.0, scale=16.0)
+        cp((r("zz", 0, C), r("r16", 0, 6)), r(src, 0, B))
+        if first:
+            tile_e(0)
+        act(r("lz"), r("zz", B, C), ACT.Relu, bias=15 * U, scale=-1.0)
+        scan(r("kr"), r("zz", B, C + 64), r("kd"), col("base", t), A.add, A.add)
+        scan(r("tx"), r("d4", 0, B), r("zz", 0, B), 0.0, A.add, A.max)
+        put("v", lambda: g.vector.transpose(T.kt[:, 0:64], T.kr[:, 192:256]), [r("kr", 192, 256)], [r("kt")])
+        ts(r("tr"), r("tx", 3, B, 4), MLO, A.add, MLO, A.subtract)
+        if first:
+            tile_e(1)
+            act(ctl, q4, bias=4.0 * 144)
+            act(c1, cu, bias=1.0, scale=-1.0)
+            act(cl0, q4, bias=4.0 * 145 - 15 * U * 2.0 ** 19 - 3 * 2.0 ** 20)
+            for b in range(2):
+                act(r("dd", 4 + b, 4 + 4 * C, 4), r(pd[b], 0, C), ACT.Copy)
         red(m2, r("kt", 32, 64), A.min)
         red(m1, r("kt", 0, 32), A.min)
         send(T["n%d" % t][:, 0:1], ap(m2), "an%d" % t, [m2])
-        ts(r("ind"), r("zz", B, C), m2, A.add, m1, A.is_equal)
-        ts(r("v5"), m1, m2, A.subtract)
-        scan(r("pf"), r("ind"), r("zero"), float(B), A.add, A.add)
+        tt(r("tp"), r("tx", 3, B, 4), r("tr"), A.subtract)
+        ts(r("ind"), r("lz"), m2, A.add, m1, A.is_equal)
+        ts(dv_, m1, m2, A.subtract)
+        ts(r("ot"), r("tp"), 2.0 ** 19, A.mult, ctl, A.add)
+        act(r("in2"), r("ind"), bias=-512.0, scale=1024.0)
+        scan(r("pf"), r("ind"), r("zer", 0, 192), float(B), A.add, A.add)
+        if first:
+            tile_e(2)
+        ts(e2, dv_, 0.0, A.is_equal, c1, A.mult)
         for k in (0, 1):
             act(r("junk2", 192 * k, 192 * k + 192), r("pf"), ACT.Sign, bias=col("thr", k), scale=-1.0, acc=col("acc", k))
         for k in range(2, n4):
-            ts(r("le", 168 * (k - 2), 168 * (k - 2) + 160), r("pf", 32, 192), col("thr", k), A.is_lt, 2.0, A.mult)
-        for k in range(2, n4):
-            red(col("acc", k), r("le", 168 * (k - 2), 168 * (k - 2) + 161), A.add)
-        if t == 0:
-            act(r("w0", WW - 16, WW), r("st", 256, 272), ACT.Copy)
+            ts(r("le", 168 * (k - 2) + 8, 168 * (k - 2) + 200 - 16 * k), r("pf", 16 * k, 192), col("thr", k), A.is_lt)
+        ts(fv, e2, dv_, A.subtract)
+        scan(r("zc", B, C), r("pf"), r("in2"), 0.0, A.max, A.min)
+        if first:
+            tile_e(3)
+        le_end = 168 if n4 == 3 else 320
+        scan(r("lc", 7, le_end), r("rl", 7, le_end), r("le", 7, le_end), 0.0, A.mult, A.add)
+        if first:
+            act(cl, r_, bias=cl0, scale=2.0 ** 20)
+            for b in range(2, 4):
+                act(r("dd", 4 + b, 4 + 4 * C, 4), r(pd[b], 0, C), ACT.Copy)
+            act(cz0, q4, bias=4.0 * (NY - 1) * S - 6, scale=S)
+            act(t4, q_, scale=S)
+            act(cth, q4, bias=(4.0 * (NH - 0.5) - 4 * MLO) * S, scale=S)
+            act(cz, r_, bias=cz0, scale=2.0)
+            quant("lq", "ls", 0, 128, zer)
         else:
-            scan(r("tx"), r("d4", 0, B), r("zz", 0, B), 0.0, A.add, A.max)
-        ts(r("o4", 0, n4), r("acc", 0, n4), 192.0, A.add, 0.5, A.mult)
-        ts(r("lp", 0, 16 * n4), (r("zz", B, C + 1), r("o4", 0, n4)), r("v5"), A.subtract, 144.0 * S, A.min)
+            act(r("tt", 0, 4 * B), (r(w, 0, 4 * C), r("ot")), ACT.Copy)
+            act(r("zp"), (r("zc"), r("r16")), bias=cz, scale=4.0 * S)
+        cp(r("o4", 2, n4), r("lc", 167, le_end, 152))
+        ts(r("o4", 0, 2), r("acc"), 192.0, A.add, 0.5, A.mult)
+        ts(r("lp", 0, 16 * n4), (r("zz", B, C + 1), r("o4", 0, n4)), fv, A.subtract, 15 * U - 145 * EPS, A.max)
+        if first:
+            ts(r("flm"), r("fl"), MLO, A.add)
+            ts(r("flu"), r("fl"), 15 * U, A.subtract)
         scan(r("lx", 0, kt), r("d4", 0, kt), r("lp", 0, kt), 0.0, A.add, A.max)
-        ts(r("os16", 0, kt // 4), r("lx", 3, kt, 4), 32768.0, A.mult, cl, A.add)
-        cp(r("st", 0, 16 * h4), (win, r("os16", 0, h4)))
-        act(r("st", 16 * h4, 4 * kt), (win, r("os16", h4, kt // 4)), ACT.Copy)
-        quant("sq", "ss", 128 * t, 128 * t + 128, r("st"))
+        ts(r("os16", 0, kt // 4), r("lx", 3, kt, 4), 2.0 ** 19, A.mult, cl, A.add)
+
+        def layer_t():
+            quant("tq", "ts", 0, 128, r("tt"))
+            for b in range(4):
+                mm(py[b], "wq", "wp", 128 * b, "tq", "ts", 0, 128)
+
+        if not first:
+            layer_t()
+        cp(r(w, 4 * NS, 4 * NS + 16 * h4), (r("dd"), r("os16", 0, h4)))
+        act(r(w, 4 * NS + 16 * h4, 4 * (NS + kt)), (r("dd"), r("os16", h4, kt // 4)), ACT.Copy)
+        quant("sq", "ss", 128 * t, 128 * t + 128, r(w, 4 * NS, 4 * NS + 512))
         send(u8(r("lq", lo, lo + kt)), u8(r("sq", 128 * t, 128 * t + kt)), "ax%d" % t, [r("sq", 128 * t, 128 * t + kt)])
         send(ap(r("ls", lo, lo + kt)), ap(r("ss", 128 * t, 128 * t + kt)), "ax%d" % t, [r("ss", 128 * t, 128 * t + kt)])
-        if t == 0:
-            last_constants()
-            scan(r("tx"), r("d4", 0, B), r("zz", 0, B), 0.0, A.add, A.max)
-        tt(r("zc", B, C), r("ind"), r("pf"), A.mult)
-        ts(r("tr"), r("tx", 3, B, 4), M, A.add, M, A.subtract)
-        ts(r("lab"), r("zz", B, C), M, A.add, M, A.subtract)
-        tt(r("tp"), r("tx", 3, B, 4), r("tr"), A.subtract)
-        fill(r("gl", 0, B), (3 + 2 * t) / 16)
-        ts(r("ot"), r("tp"), 32768.0, A.mult, ctl, A.add)
-        act(r("zp"), (r("zc"), r("r16")), bias=cz, scale=4.0 * S)
-        act(r("tt", 0, 4 * B), (win, r("ot")), ACT.Copy)
-        act(r("ik"), r("ind"), scale=(4 + 2 * t) / 16)
-        if t == 0:
-            act(r("pg"), r("pg"), scale=S)
-            ts(r("e4"), r("j4"), q_, A.is_equal)
-            quant("lq", "ls", 0, 128, r("st"))
-        ts(r("th"), r("n%d" % t), 4.0 * S, A.mult, cth, A.add)
-        if more:
-            ts(col("ku", 1), col("kr", B - 1), m1, A.is_equal, 65536.0, A.mult)
+        if first:
+            act(r("zp"), (r("zc"), r("r16")), bias=cz, scale=4.0 * S)
+            act(r("it4"), r("it16"), bias=t4, scale=S)
+            act(r("tt", 0, 4 * B), (r(w, 0, 4 * C), r("ot")), ACT.Copy)
         scan(r("zx"), r("d4"), r("zp"), 0.0, A.add, A.max)
+        ts(r("th"), r("n%d" % t), 4.0 * S, A.mult, cth, A.add)
+        act(dl_, fv, bias=col("flu", 4 + 2 * t), scale=-1.0)
+        act(r("da"), r("zz", 0, B), bias=col("flm", 3 + 2 * t), scale=-1.0)
         x = r("zx", 3, C, 4)
-        if more:
-            ts(col("ku", 2), m2, M + 65536.0, A.subtract, col("e4", 2 * t + 1), A.mult)
-        ts(r("en"), x, cz1, A.is_gt, 4.0 * ND * S, A.mult)
-        ts(r("ea"), x, r("th"), A.is_gt)
-        quant("tq", "ts", 0, 128, r("tt"))
-        for b in range(4):
-            mm(py[b], "wq", "wp", 128 * b, "tq", "ts", 0, 128)
+        tt(r("ec"), x, r("it4"), A.max)
+        ts(r("ea"), x, r("th"), A.is_gt, 4.0 * K * S, A.mult)
+        if first:
+            layer_t()
+        if not more:
+            quant("vq", "vs", 0, 128, r("vt"))
+        tt(r("eb"), r("ea"), r("ec"), A.add)
+        act(r("dl", B, C), r("ind"), scale=dl_)
+        act(r("dl", 0, B), r("da"), bias=-MLO)
         for b in range(4):
             act(r(w, 4 * NY + b, 4 * NH, 4), r(py[b], 0, B), scale=0.03125)
-        tt(r("ec"), r("en"), r("it4"), A.add)
-        tt(r("eb"), r("ea"), x, A.add)
+        tt(r(srn, 0, 128), (r("dl"), r("r16", 0, 8)), r(src, 0, 128), A.add)
+        ts(r("oe"), r("eb"), 1 / S, A.mult)
+        tt(r(srn, 128, C), (r("dl"), r("r16", 8, 18)), r(src, 128, C), A.add)
         if more:
-            ts(col("ku", 3), col("e4", 2 * t), B - 65536.0, A.mult, col("kr", B - 1), A.add)
-        tt(r("ed"), r("ec"), r("eb"), A.min)
-        tt(r("gl", B, C), r("lab"), r("ik"), A.max)
-        ts(r("oe"), r("ed"), 8192.0, A.mult)
-        if more:
-            ts(col("base", t + 1), col("ku", 3), col("ku", 2), A.add, col("ku", 1), A.add)
-            tt(r("src", 0, 128), (r("gl"), r("r16", 0, 8)), r("pg", 0, 128), A.add)
+            act(b1, col("e9", 3 + 2 * t), bias=col("base", t), scale=-GONE)
+            act(eg, dv_, ACT.Relu, bias=GONE, scale=-GONE / U)
+            act(b2_, col("e9", 4 + 2 * t), bias=b1, scale=-GONE)
+            act(col("base", t + 1), eg, bias=b2_)
         else:
-            quant("vq", "vs", 0, 128, r("vt"))
-            act(r("obo"), (r("gl"), r("r16")), scale=16.0)
-            dma("y", "so", T.ob[:], T.obo[0:128:16, :], [r("obo")], [])
+            act(r("oba"), r(srn), bias=MHI, scale=1 / U)
+            act(r("obo"), r("oba"), bias=-MHI)
+            dma("y", "so", T.ob[:], T.obo[15:128:16, :], [r("obo")], [])
         for b in (0, 2, 1, 3):
             mm(pd[b], "wq", "wp", 128 * b, "lq", "ls", lo + kt - 128, lo + kt)
         for b in (0, 2, 1, 3):
@@ -396,18 +443,21 @@ def rank_program(g, core, T, topo):
                 ts(o, r(pd[b], 128 - kt, 128), 0.03125, A.mult)
             else:
                 act(o, r(pd[b], 128 - kt, 128), scale=0.03125)
-        cp(r(wn, 0, 576), (win, r("oe", 0, 36)))
-        act(r(wn, 576, 1152), (win, r("oe", 36, 72)), ACT.Copy)
+        win = r(w, 0, 4 * (NS + K))
+        cp(r(wn, 4 * HF, 4 * C), (win, r("oe", 36, 72)))
+        act(r(wn, 0, 4 * HF), (win, r("oe", 0, 36)), ACT.Copy)
 
     xa, xb = R * C, R * C + C
-    quant("xq", "xs", xa, xb, r("w%d" % (R % 2), 0, 4 * C))
-    mm("pp", "vq", "vs", 0, "xq", "xs", xa, xa + C // 2)
-    mm("pc", "vq", "vs", 0, "xq", "xs", xa + C // 2, xb)
+    w = "w%d" % (R % 2)
+    quant("xq", "xs", xa + HF, xb, r(w, 4 * HF, 4 * C))
+    quant("xq", "xs", xa, xa + HF, r(w, 0, 4 * HF))
+    mm("pc", "vq", "vs", 0, "xq", "xs", xa + HF, xb)
+    mm("pp", "vq", "vs", 0, "xq", "xs", xa, xa + HF)
     dma("y", "sc", T.oc[:], u8(r("xq", xa, xb)), [r("xq", xa, xb)], [])
     for k in range(4):
         dma("y", "s%d" % k, T.osc[4 * k:4 * k + 4, :], T.xs[32 * k:32 * k + 4, xa:xb], [r("xs", xa, xb)], [])
-    act(r("yo", 0, C // 2), r("pp", 0, C // 2), ACT.Copy)
-    cp(r("yo", C // 2, C), r("pc", 0, C // 2))
+    act(r("yo", HF, C), r("pc", 0, HF), ACT.Copy)
+    cp(r("yo", 0, HF), r("pp", 0, HF))
     dma("s", "sy", T.y[:], T.yo[:], [r("yo")], [])
 
     marked = {q: sorted({i for p in ops for o in ops[p] for s, i in o[1] if s == q}) for q in eng}

@@ -2,38 +2,37 @@ from concourse.mybir import dt, AluOpType, AxisListType, ActivationFunctionType
 
 C, B, K, R = 288, 96, 64, 3
 HF = C // 2
-NY, NH, NS = 288, 384, 448
-WW = 4 * (NS + 128)
+NY, NH, ND = 288, 384, 448
+WW = 4 * (ND + C)
 U, EPS = 2.0 ** -8, 2.0 ** -17
 S = 2.0 ** -12
 MLO, MHI = 1.5 * 2.0 ** 15, 1.5 * 2.0 ** 23
 GONE = 512.0
-BIG = 1.0e28
+BIG = 2.0 ** 93
 CT = [0, 288, 512, 672, 768]
 CW = [288, 224, 160, 128, 128]
 ORDER = [16, 15, 13, 12, 11, 10, 9, 8, 7, 6, 5, 4, 3, 2, 1]
 ON_SCALAR = (17, 14)
 QUANT_AFTER = {13: (0, 288), 10: (288, 512), 6: (512, 672)}
 KT = [64, 48, 40]
-LO = [128, 192, 240]
 
 F32, BF, I32, U16, Q4, U8 = "float32", "bfloat16", "int32", "uint16", "float8_e4m3fn_x4", "uint8"
 SIZES = {
-    BF: dict(w0=WW, w1=WW, dd=4 * C + 4, ut=512, vt=512, ones=128, ff=1040, b2=512, ct=4 * 896, junk=2448, junk2=384, tt=512, zer=512,
-             sd=C, dseg=C, ind=192, in2=192, pf=192, le=320, rl=320, lc=320, zc=C),
-    Q4: dict(xq=4 * C, lq=128 + R * K, uq=128, uq2=128, vq=128, wq=512, eq=512, bq=128, cq=896, tq=128, sq=128 * R),
-    U8: dict(xs=4 * C, ls=128 + R * K, us=128, us2=128, vs=128, wp=512, es=512, bs=128, cs=896, ts=128, ss=128 * R),
+    BF: dict(w0=WW, w1=WW, dd=4 * C, ds=4 * 208, ut=512, vt=512, ones=128, ff=1040, b2=512, ct=4 * 896, junk=2448, junk2=384, tt=512,
+             st=512, zer=192, sd=C, dseg=C, ind=192, in2=192, pf=192, le=320, rl=320, lc=320, zc=C),
+    Q4: dict(xq=4 * C, lq=R * C, uq=128, uq2=128, vq=128, wq=512, eq=512, bq=128, cq=896, tq=128, sq=128),
+    U8: dict(xs=4 * C, ls=R * C, us=128, us2=128, vs=128, wp=512, es=512, bs=128, cs=896, ts=128, ss=128),
     I32: dict(pi=2, ci=6, oui=8),
-    U16: dict(ou=8, r16=18, o4=4, os16=16, ot=24, oe=72),
-    F32: dict(n0=1, n1=1, n2=1, gj=128, ga=128, cf=6, cc=24, i16=C, i4=C, it16=72, it4=72, mx=C, hd=C, d1=C, d4=C, kk=18, thr=4, jl=10,
-              ju=10, e9=10, fl=10, flm=10, flu=10, pg=C, src0=C, src1=C, aa=C, hh=C, rs=18, adj=18, ext=C, zz=C + 64, kd=256, kr=256,
-              kt=64, kb=64, ke=32, mm=6, acc=2, lz=192, lp=K, lx=K, tx=B, tr=24, tp=24, zp=C, zx=C, th=1, ea=72, eb=72, ec=72,
-              da=B, dl=C, ku=1, base=3, yo=C, oba=C, obo=C),
+    U16: dict(ou=8, r16=18, o4=8 * R, op=8 * R, os16=16 * R, ol=16 * R, ot=24, oe=72),
+    F32: dict(n0=1, n1=1, n2=1, gj=128, ga=128, cf=6, cc=24, i16=C, i4=C, it16=72, it4=72, itd=72, ed=72, mx=C, hd=C, d1=C, d4=C, kk=18,
+              thr=4, jl=10, ju=10, e9=10, fl=10, flm=10, flu=10, pg=C, src0=C, src1=C, aa=C, hh=C, rs=18, adj=18, ext=C, zz=C + 64,
+              kd=256, kr=256, kt=64, kb=64, ke=32, mm=64 * R, acc=2, lz=192, d16=192, ex=192, er=12, ep=12, tx=B, tr=24, tp=24, zp=C,
+              zx=C, th=1, ea=72, eb=72, ec=72, da=B, dl=C, kz=64, base=4, yo=C, oba=C, obo=C),
 }
 SCRATCH = {n: ("sbuf", [128, k], d) for d in SIZES for n, k in SIZES[d].items()}
 SCRATCH.update({n: ("psum", [128, 512], F32) for n in ("pp", "pc", "pd0", "pd1", "pd2", "pd3", "py0", "py1")})
-SEMAPHORES = ["qv", "qs", "qt", "qg", "sent", "lx", "ly", "lu", "lv", "lw", "lp", "so", "sc", "sy", "s0", "s1", "s2", "s3",
-              "an0", "an1", "an2", "ax0", "ax1", "ax2"]
+SEMAPHORES = ["qv", "qs", "qt", "qg", "sent", "lx", "ly", "lu", "lv", "lw", "lp", "so", "sc", "sy", "sz", "s0", "s1", "s2", "s3",
+              "an0", "an1", "an2", "ax0", "ax1", "ax2", "al0", "al1", "al2", "ap0", "ap1", "ap2"]
 A, ACT = AluOpType, ActivationFunctionType
 
 
@@ -135,9 +134,6 @@ def rank_program(g, core, T, topo):
     def scan(out, d0, d1, init, op0, op1):
         put("v", lambda: g.vector.tensor_tensor_scan(ap(out), ap(d0), ap(d1), val(init), op0, op1), [d0, d1, init], [out])
 
-    def red(out, a, op):
-        put("v", lambda: g.vector.tensor_reduce(ap(out), ap(a), AxisListType.X, op), [a], [out])
-
     def quant(qn, sn, lo, hi, tile):
         put("v", lambda: g.vector.quantize_mx(ap(r(qn, lo, hi)), ap(r(sn, lo, hi)), ap(tile)), [tile], [r(qn, lo, hi), r(sn, lo, hi)])
 
@@ -163,7 +159,9 @@ def rank_program(g, core, T, topo):
 
     for t in range(R):
         arrives("an%d" % t, nin, [r("n%d" % t)])
-        arrives("ax%d" % t, 2 * nin, [r("lq", LO[t], LO[t] + KT[t]), r("ls", LO[t], LO[t] + KT[t])])
+        arrives("ax%d" % t, 2 * nin, [r("lq", C * t, C * t + C), r("ls", C * t, C * t + C)])
+        arrives("al%d" % t, nin, [r("ol", 16 * t, 16 * t + 16)])
+        arrives("ap%d" % t, nin, [r("op", 8 * t, 8 * t + 8)])
 
     xhi, xlo = r("w0", 2 * C, 4 * C), r("w0", 0, 2 * C)
     dma("y", "lx", ap(xhi), T.x[:, 2 * C:4 * C], [], [xhi])
@@ -174,7 +172,7 @@ def rank_program(g, core, T, topo):
     dma("y", "lv", T.vt[:], T.v[:], [], [r("vt")])
 
     q_, qm1, h_, r_, q4, g_ = (col("cf", j) for j in range(6))
-    mq, z0, t0, ccs, ck, cl0, cl, ctl, cz0, cz, cth, t1, cu, c1, t3, t4, dv_, e2, fv, dl_, eg, b1, b2_ = (col("cc", j) for j in range(23))
+    mq, z0, t0, ccs, ck, ku, ctl, cz0, cz, cth, t1, cu, c1, t3, t4, dv_, e2, fv, dl_, eg, b1, b2_ = (col("cc", j) for j in range(22))
     zer = r("zer")
     fill(r("ones"), 1.0)
     fill(r("ff", 0, 520), 0.0)
@@ -183,65 +181,80 @@ def rank_program(g, core, T, topo):
     iota(r("oui"), [[16, 8]], 0)
     iota(r("gj"), [[1, 8], [0, 16]], 0)
     act(r("ff", 520, 1040), r("ff", 0, 520), ACT.Copy)
-    fill(zer, 0.0)
     ident(r("ff", 2, 514, 4))
     ident(r("ff", 523, 1035, 4))
     iota(r("it16"), [[16, 72]], 0)
     iota(r("jl"), [[1, 10]], 0)
-    iota(r("pg"), [[1, C]], -144)
-    iota(r("i4"), [[0, 72], [1, 4]], 0)
-    iota(r("zc", 0, B), [[1, B]], 1)
-    iota(r("kd", 0, 192), [[0, 192]], 0)
-    iota(r("zz", C, C + 64), [[0, 64]], 0)
-    iota(r("rl"), [[0, 320]], 1)
-    iota(r("rl", 7, 176, 168), [[0, 2]], 0)
-    iota(r("le", 0, 8), [[0, 8]], 32)
-    iota(r("le", 168, 176), [[0, 8]], 48)
-    iota(r("dd", 0, 4), [[0, 4]], 0)
-    iota(r("w0", 4 * (NS + K), WW), [[0, 256]], 0)
-    iota(r("tt", 4 * B, 512), [[0, 128]], 0)
-    iota(r("w1", 4 * (NS + KT[1]), WW), [[0, WW - 4 * (NS + KT[1])]], 0)
+    iota(r("ct", 4 * 464, 4 * 512), [[0, 192]], 0)
+
+    def late_rows():
+        iota(r("sd"), [[0, 18], [1, 16]], 0)
+        iota(r("ct", 4 * 624, 4 * 672), [[0, 192]], 0)
+        iota(r("ct", 4 * 720, 4 * 896), [[0, 704]], 0)
+        iota(r("pg"), [[1, C]], -144)
+        iota(r("i4"), [[0, 72], [1, 4]], 0)
+        iota(r("zz", C + 1, C + 64), [[0, 63]], 0)
+        iota(r("kd", 0, 192), [[0, 192]], 0)
+        iota(r("kz"), [[0, 2], [-30000, 32]], 70000)
+        iota(zer, [[0, 192]], 0)
+        iota(r("ds", 192, 4 * 208, 208), [[0, 4]], 0)
+        iota(r("zc", 0, B), [[1, B]], 1)
+        iota(r("rl"), [[0, 320]], 1)
+        iota(r("le", 0, 8), [[0, 8]], 32)
+        iota(r("le", 168, 176), [[0, 8]], 48)
+        iota(r("rl", 7, 176, 168), [[0, 2]], 0)
+        iota(r("tt", 4 * B, 512), [[0, 128]], 0)
+        iota(r("st", 4 * K, 512), [[0, 256]], 0)
+
+    def tile_e(b):
+        a = (2, 522, 0, 520)[b]
+        quant("eq", "es", 128 * b, 128 * b + 128, r("ff", a, a + 512))
 
     ts(r("ci", 0, 2), r("pi"), 15, A.bitwise_and)
     ts(col("ci", 2), col("pi", 0), 4, A.logical_shift_right, 1, A.bitwise_and)
     ts(col("ci", 3), col("pi", 0), 2, A.logical_shift_right, 3, A.bitwise_and)
     ts(col("ci", 4), col("pi", 0), 3, A.bitwise_and)
     ts(col("ci", 5), col("pi", 0), 4, A.logical_shift_right)
-    for a in (240, 464):
-        fill(r("ct", 4 * a, 4 * a + 192), 0.0)
+    fill(r("ct", 4 * 240, 4 * 288), 0.0)
     cp(r("cf"), r("ci"))
+    ts(ctl, q4, 4.0 * 144, A.add)
+    ts(t3, q_, B + 0.5, A.add)
+    ts(cz0, q4, S, A.mult, 4.0 * (NY - 1) * S - 6, A.add)
     cp(r("ou"), r("oui"))
-    fill(r("ct", 4 * 624, 4 * 624 + 192), 0.0)
     ts(r("mx"), r("i16"), q_, A.not_equal, -BIG, A.mult)
     act(r("hd"), r("i16"), bias=-0.5 * BIG, scale=BIG)
-    act(r("ct", 4 * 768, 4 * 896), zer, ACT.Copy)
-    act(r("ct", 4 * 720, 4 * 768), r("zer", 0, 192), ACT.Copy)
     act(r("ga"), r("gj"), ACT.Abs, bias=g_, scale=-1.0)
     act(z0, q_, ACT.Relu, bias=1.0, scale=-1.0)
     act(t0, q_, bias=-7680.0, scale=512.0)
-    for b in range(4):
-        act(r("b2", b, 512, 4), r("ga"), ACT.Relu, bias=1.0, scale=-1.0)
-    quant("uq", "us", 0, 128, r("ut"))
+    act(r("b2", 0, 512, 4), r("ga"), ACT.Relu, bias=1.0, scale=-1.0)
     fill(col("rs", 0), 0.0)
+    quant("uq", "us", 0, 128, r("ut"))
+    ts(c1, q_, U, A.mult, 1 - 15 * U, A.add)
+    ts(cth, q4, S, A.mult, (4.0 * (NH - 0.5) - 4 * MLO) * S, A.add)
+    ts(t4, q_, S, A.mult)
+    ts(cz, r_, 2.0, A.mult, cz0, A.add)
     put("v", lambda: g.vector.tensor_copy(T.uq2[:, 0:128].bitcast(dt.uint32), T.uq[:, 0:128].bitcast(dt.uint32).indirect(T.ou[:, 0:8])),
         [r("uq"), r("ou")], [r("uq2")])
-    cp(r("us2"), (r("us"), r("ou")))
+    put("s", lambda: g.scalar.activation(T.us2[:, 0:128], T.us[:, 0:128].indirect(T.ou[:, 0:8]), ACT.Copy), [r("us"), r("ou")], [r("us2")])
+    tile_e(0)
+    for b in range(1, 4):
+        act(r("b2", b, 512, 4), r("ga"), ACT.Relu, bias=1.0, scale=-1.0)
     act(t1, q_, bias=15.0, scale=-1.0)
     act(ccs, z0, bias=t0, scale=65024.0)
     act(r("ju"), r("jl"), scale=U)
     act(ck, z0, bias=t1, scale=-65024.0)
-    act(r("sd"), r("i16"), ACT.Sign)
+    act(r("d16"), r("mx", 0, 192), bias=-34.0, scale=-36.0 / BIG)
+    act(ku, q_, ACT.Sign, bias=-2.5)
     act(mq, q_, bias=MLO, scale=0.0625)
     act(cu, q_, bias=15 * U, scale=-U)
     act(r("kk"), r("it16", 0, 18), bias=ck)
-
-    def tile_e(b):
-        a = (2, 522, 0, 520)[b]
-        quant("eq", "es", 128 * b, 128 * b + 128, r("ff", a, a + 512))
-        mm("pd%d" % b, "eq", "es", 128 * b, "xq", "xs", 0, C)
+    act(col("base", 0), ku, bias=MHI + GONE / 2, scale=GONE / 2)
 
     pd = ["pd0", "pd1", "pd2", "pd3"]
     py = ["py0", "py1", "pp", "pc"]
+
+    def relabel(t, a, b):
+        tt(r("src%d" % ((t + 1) % 2), a, b), (r("dl"), r("r16", a // 16, b // 16)), r("src%d" % (t % 2), a, b), A.add)
 
     def cview(m):
         k = (18 - m) // 4
@@ -252,30 +265,60 @@ def rank_program(g, core, T, topo):
 
     for t in range(R):
         w, wn = "w%d" % (t % 2), "w%d" % ((t + 1) % 2)
-        src, srn = "src%d" % (t % 2), "src%d" % ((t + 1) % 2)
+        src = "src%d" % (t % 2)
         more, first = t < R - 1, t == 0
-        m1, m2 = col("mm", 2 * t), col("mm", 2 * t + 1)
+        m1, m2 = col("mm", 64 * t + 31), col("mm", 64 * t + 63)
         xa, xb = C * t, C * t + C
-        kt, lo = KT[t], LO[t]
+        kt, la, lb = KT[t], 16 * t, 8 * t
         n4 = (kt + 15) // 16
-        h4 = 2 * n4
+
+        def own_d(b, product=False, bank=None):
+            bank = bank or pd[b]
+            if product:
+                mm(bank, "eq", "es", 128 * b, "xq", "xs", xa, xb)
+            act(r(w, 4 * ND + b, WW, 4), r(bank, 0, C), ACT.Copy)
+
+        def far_d(b):
+            mm(pd[b], "eq", "es", 128 * b, "lq", "ls", xa, xb)
+            act(r("dd", C * b, C * b + C), r(pd[b], 0, C), ACT.Copy)
+
+        def sort_d(b, call):
+            call(r("ds", 208 * b, 208 * b + 192), (r("dd", C * b, C * b + C), r("ol", la, la + 12)))
+
+        def pick_s(b, call):
+            call(r("st", b, 64 * n4, 4), (r("ds", 208 * b, 208 * b + 193), r("op", lb, lb + n4)))
+
         quant("xq", "xs", xa + HF, xb, r(w, 4 * HF, 4 * C))
+        if first:
+            ts(r("d1"), r("i16"), qm1, A.not_equal, 1.0 - 1.0 / 128, A.subtract)
+            ts(r("e9"), r("jl"), q_, A.is_equal)
+            act(r("d1"), r("d1"), scale=65536.0)
         quant("xq", "xs", xa, xa + HF, r(w, 0, 4 * HF))
+        send(u8(r("lq", xa, xb)), u8(r("xq", xa, xb)), "ax%d" % t, [r("xq", xa, xb)])
+        send(ap(r("ls", xa, xb)), ap(r("xs", xa, xb)), "ax%d" % t, [r("xs", xa, xb)])
+        if first:
+            late_rows()
         mm("py1", "uq2", "us2", 0, "xq", "xs", xa + HF, xb)
         mm("pp", "uq2", "us2", 0, "xq", "xs", xa, xb)
         mm("py0", "uq2", "us2", 0, "xq", "xs", xa, xb)
-        if first:
-            quant("cq", "cs", 768, 896, r("ct", 4 * 768, 4 * 896))
-        else:
+        if not first:
             for b in range(4):
                 mm(pd[b], "eq", "es", 128 * b, "xq", "xs", xa, xb)
+        if not first:
+            relabel(t - 1, 128, C)
         dv = r("ct", 0, 4 * C, 4)
         tt(r("aa", HF, C), r("py1", 0, HF), r("mx", HF, C), A.add)
         if first:
-            quant("bq", "bs", 0, 128, r("b2"))
+            tile_e(1)
+            scan(r("hh", HF, C), r("hd", HF, C), r("aa", HF, C), -BIG, A.min, A.max)
         tt(r("aa", 0, HF), r("pp", 0, HF), r("mx", 0, HF), A.add)
-        for a, b in ((HF, C), (0, HF)):
-            scan(r("hh", a, b), r("hd", a, b), r("aa", a, b), -BIG, A.min, A.max)
+        if first:
+            quant("bq", "bs", 0, 128, r("b2"))
+        else:
+            scan(r("hh", HF, C), r("hd", HF, C), r("aa", HF, C), -BIG, A.min, A.max)
+        if t == 1:
+            relabel(0, 0, 128)
+        scan(r("hh", 0, HF), r("hd", 0, HF), r("aa", 0, HF), -BIG, A.min, A.max)
         for m in ON_SCALAR:
             act(jview(m), r("py0", 0, 16 * m), ACT.Sign, bias=col("hh", 16 * m + 15), scale=-1.0)
         for m in ON_SCALAR:
@@ -288,14 +331,14 @@ def rank_program(g, core, T, topo):
             if m in QUANT_AFTER:
                 a, b = QUANT_AFTER[m]
                 quant("cq", "cs", a, b, r("ct", 4 * a, 4 * b))
-            if first and m == ORDER[1]:
-                ts(r("d1"), r("i16"), qm1, A.not_equal, 1.0 - 1.0 / 128, A.subtract)
-                ts(r("e9"), r("jl"), q_, A.is_equal)
+            if first and m == 3:
+                tile_e(2)
+            if first and m == 8:
+                quant("cq", "cs", 768, 896, r("ct", 4 * 768, 4 * 896))
             if first and m == ORDER[3]:
-                act(r("d1"), r("d1"), scale=65536.0)
                 tt(r("fl"), r("e9"), r("ju"), A.add)
             if m == 13:
-                scan(r("dseg"), r("sd"), dv, 0.0, A.mult, A.add)
+                scan(r("dseg"), r("sd"), dv, 0.0, A.min, A.add)
             if m == 10:
                 tt(r("adj"), r("kk"), r("dseg", 15, C, 16), A.subtract)
         for k in (0, 1, 2):
@@ -304,20 +347,24 @@ def rank_program(g, core, T, topo):
         if first:
             for b in (1, 2, 0):
                 act(r(src, B * b, B * b + B), r("pg", B * b, B * b + B), bias=col("fl", b), scale=EPS)
-            act(col("zz", C), col("zer", 0), bias=-MHI)
+            act(col("zz", C), q_, bias=-MHI, scale=0.0)
+            act(r("thr"), r("it16", 0, 4), bias=t3)
         else:
             for b in range(4):
-                act(r("dd", 4 + b, 4 + 4 * C, 4), r(pd[b], 0, C), ACT.Copy)
+                own_d(b)
         tt(r("d1", B + 15, C, 16), r("adj", 6, 18), r("rs", 6, 18), A.subtract)
         quant("cq", "cs", 672, 800, r("ct", 4 * 672, 4 * 800))
         for k in (3, 4):
             mm("py1", "bq", "bs", 0, "cq", "cs", CT[k], CT[k] + 128, start=False, stop=(k == 4))
+        if not first:
+            for b in range(2):
+                far_d(b)
         scan(r("ext", B, C), r("pc", B, C), r("d1", B, C), -65024.0, A.max, A.add)
         if first:
             ts(r("kb", 32, 64), r("gj", 0, 32), h_, A.not_equal, 4096.0, A.mult)
             ts(r("ke"), r("i16", 0, 32), q_, A.not_equal, cu, A.mult)
-        ts(r("r16", 6, 18), r("ext", B + 15, C, 16), ccs, A.add)
         tt(r("d1", 15, B, 16), r("adj", 0, 6), r("rs", 0, 6), A.subtract)
+        ts(r("r16", 6, 18), r("ext", B + 15, C, 16), ccs, A.add)
         if first:
             tt(r("kb", 0, 32), r("kb", 32, 64), r("ke"), A.add)
         scan(r("ext", 0, B), r("py1", 0, B), r("d1", 0, B), -65024.0, A.max, A.add)
@@ -327,138 +374,126 @@ def rank_program(g, core, T, topo):
             ts(col("kd", 192), col("kb", 0), mq, A.add)
             tt(r("kd", 193, 256), r("kb", 1, 64), r("kb", 0, 63), A.subtract)
             act(r("d4"), r("i4"), ACT.Abs, bias=r_, scale=-1.0)
-            act(col("ku", 0), q_, ACT.Sign, bias=-2.5)
-            act(t3, q_, bias=B + 0.5)
+            own_d(0, True)
             act(r("d4"), r("d4"), ACT.Sign)
-            act(col("base", 0), col("ku", 0), bias=MHI + GONE / 2, scale=GONE / 2)
-            act(r("thr"), r("it16", 0, 4), bias=t3)
+            own_d(1, True)
             act(r("d4"), r("d4"), bias=-14.0, scale=16.0)
+            own_d(2, True)
         cp((r("zz", 0, C), r("r16", 0, 6)), r(src, 0, B))
         if first:
-            tile_e(0)
+            tile_e(3)
         act(r("lz"), r("zz", B, C), ACT.Relu, bias=15 * U, scale=-1.0)
+        if first:
+            act(r("it4"), r("it16"), bias=t4, scale=S)
         scan(r("kr"), r("zz", B, C + 64), r("kd"), col("base", t), A.add, A.add)
-        scan(r("tx"), r("d4", 0, B), r("zz", 0, B), 0.0, A.add, A.max)
+        scan(r("ex"), r("d16"), r("zz", B, C), 0.0, A.add, A.max)
         put("v", lambda: g.vector.transpose(T.kt[:, 0:64], T.kr[:, 192:256]), [r("kr", 192, 256)], [r("kt")])
-        ts(r("tr"), r("tx", 3, B, 4), MLO, A.add, MLO, A.subtract)
-        if first:
-            tile_e(1)
-            act(ctl, q4, bias=4.0 * 144)
-            act(c1, cu, bias=1.0, scale=-1.0)
-            act(cl0, q4, bias=4.0 * 145 - 15 * U * 2.0 ** 19 - 3 * 2.0 ** 20)
-            for b in range(2):
-                act(r("dd", 4 + b, 4 + 4 * C, 4), r(pd[b], 0, C), ACT.Copy)
-        red(m2, r("kt", 32, 64), A.min)
-        red(m1, r("kt", 0, 32), A.min)
+        ts(r("er"), r("ex", 15, 192, 16), MLO, A.add, MLO, A.subtract)
+        for b in range(0 if first else 2, 4):
+            far_d(b)
+        if not first:
+            act(r("da"), r("zz", 0, B), bias=col("flm", 3 + 2 * t), scale=-1.0)
+            act(r("dl", 0, B), r("da"), bias=-MLO)
+        scan(r("mm", 64 * t, 64 * t + 64), r("kz"), r("kt"), 0.0, A.max, A.min)
         send(T["n%d" % t][:, 0:1], ap(m2), "an%d" % t, [m2])
-        tt(r("tp"), r("tx", 3, B, 4), r("tr"), A.subtract)
+        tt(r("ep"), r("ex", 15, 192, 16), r("er"), A.subtract)
+        scan(r("tx"), r("d4", 0, B), r("zz", 0, B), 0.0, A.add, A.max)
         ts(r("ind"), r("lz"), m2, A.add, m1, A.is_equal)
-        ts(dv_, m1, m2, A.subtract)
-        ts(r("ot"), r("tp"), 2.0 ** 19, A.mult, ctl, A.add)
-        act(r("in2"), r("ind"), bias=-512.0, scale=1024.0)
-        scan(r("pf"), r("ind"), r("zer", 0, 192), float(B), A.add, A.add)
-        if first:
-            tile_e(2)
-        ts(e2, dv_, 0.0, A.is_equal, c1, A.mult)
+        ts(r("os16", la, la + 12), r("ep"), 1 / EPS, A.mult, 144.0, A.add)
+        send(ap(r("ol", la, la + 12)), ap(r("os16", la, la + 12)), "al%d" % t, [r("os16", la, la + 12)])
+        ts(r("tr"), r("tx", 3, B, 4), MLO, A.add, MLO, A.subtract)
+        scan(r("pf"), r("ind"), zer, float(B), A.add, A.add)
+        ts(r("in2"), r("ind"), 1024.0, A.mult, 512.0, A.subtract)
         for k in (0, 1):
             act(r("junk2", 192 * k, 192 * k + 192), r("pf"), ACT.Sign, bias=col("thr", k), scale=-1.0, acc=col("acc", k))
         for k in range(2, n4):
             ts(r("le", 168 * (k - 2) + 8, 168 * (k - 2) + 200 - 16 * k), r("pf", 16 * k, 192), col("thr", k), A.is_lt)
-        ts(fv, e2, dv_, A.subtract)
+        tt(r("tp"), r("tx", 3, B, 4), r("tr"), A.subtract)
         scan(r("zc", B, C), r("pf"), r("in2"), 0.0, A.max, A.min)
-        if first:
-            tile_e(3)
         le_end = 168 if n4 == 3 else 320
         scan(r("lc", 7, le_end), r("rl", 7, le_end), r("le", 7, le_end), 0.0, A.mult, A.add)
-        if first:
-            act(cl, r_, bias=cl0, scale=2.0 ** 20)
-            for b in range(2, 4):
-                act(r("dd", 4 + b, 4 + 4 * C, 4), r(pd[b], 0, C), ACT.Copy)
-            act(cz0, q4, bias=4.0 * (NY - 1) * S - 6, scale=S)
-            act(t4, q_, scale=S)
-            act(cth, q4, bias=(4.0 * (NH - 0.5) - 4 * MLO) * S, scale=S)
-            act(cz, r_, bias=cz0, scale=2.0)
-            quant("lq", "ls", 0, 128, zer)
-        else:
-            act(r("tt", 0, 4 * B), (r(w, 0, 4 * C), r("ot")), ACT.Copy)
-            act(r("zp"), (r("zc"), r("r16")), bias=cz, scale=4.0 * S)
-        cp(r("o4", 2, n4), r("lc", 167, le_end, 152))
-        ts(r("o4", 0, 2), r("acc"), 192.0, A.add, 0.5, A.mult)
-        ts(r("lp", 0, 16 * n4), (r("zz", B, C + 1), r("o4", 0, n4)), fv, A.subtract, 15 * U - 145 * EPS, A.max)
+        ts(r("ot"), r("tp"), 2.0 ** 19, A.mult, ctl, A.add)
+        ts(dv_, m1, m2, A.subtract)
+        act(r("zp"), (r("zc"), r("r16")), bias=cz, scale=4.0 * S)
+        act(r("tt", 0, 4 * B), (r(w, 0, 4 * C), r("ot")), ACT.Copy)
+        cp(r("o4", lb + 2, lb + n4), r("lc", 167, le_end, 152))
+        ts(r("o4", lb, lb + 2), r("acc"), 192.0, A.add, 0.5, A.mult)
+        send(ap(r("op", lb, lb + n4)), ap(r("o4", lb, lb + n4)), "ap%d" % t, [r("o4", lb, lb + n4)])
+        ts(e2, dv_, 0.0, A.is_equal, c1, A.mult)
         if first:
             ts(r("flm"), r("fl"), MLO, A.add)
             ts(r("flu"), r("fl"), 15 * U, A.subtract)
-        scan(r("lx", 0, kt), r("d4", 0, kt), r("lp", 0, kt), 0.0, A.add, A.max)
-        ts(r("os16", 0, kt // 4), r("lx", 3, kt, 4), 2.0 ** 19, A.mult, cl, A.add)
-
-        def layer_t():
-            quant("tq", "ts", 0, 128, r("tt"))
-            for b in range(4):
-                mm(py[b], "wq", "wp", 128 * b, "tq", "ts", 0, 128)
-
-        if not first:
-            layer_t()
-        cp(r(w, 4 * NS, 4 * NS + 16 * h4), (r("dd"), r("os16", 0, h4)))
-        act(r(w, 4 * NS + 16 * h4, 4 * (NS + kt)), (r("dd"), r("os16", h4, kt // 4)), ACT.Copy)
-        quant("sq", "ss", 128 * t, 128 * t + 128, r(w, 4 * NS, 4 * NS + 512))
-        send(u8(r("lq", lo, lo + kt)), u8(r("sq", 128 * t, 128 * t + kt)), "ax%d" % t, [r("sq", 128 * t, 128 * t + kt)])
-        send(ap(r("ls", lo, lo + kt)), ap(r("ss", 128 * t, 128 * t + kt)), "ax%d" % t, [r("ss", 128 * t, 128 * t + kt)])
-        if first:
-            act(r("zp"), (r("zc"), r("r16")), bias=cz, scale=4.0 * S)
-            act(r("it4"), r("it16"), bias=t4, scale=S)
-            act(r("tt", 0, 4 * B), (r(w, 0, 4 * C), r("ot")), ACT.Copy)
-        scan(r("zx"), r("d4"), r("zp"), 0.0, A.add, A.max)
-        ts(r("th"), r("n%d" % t), 4.0 * S, A.mult, cth, A.add)
-        act(dl_, fv, bias=col("flu", 4 + 2 * t), scale=-1.0)
-        act(r("da"), r("zz", 0, B), bias=col("flm", 3 + 2 * t), scale=-1.0)
-        x = r("zx", 3, C, 4)
-        tt(r("ec"), x, r("it4"), A.max)
-        ts(r("ea"), x, r("th"), A.is_gt, 4.0 * K * S, A.mult)
-        if first:
-            layer_t()
+            ts(r("itd"), r("it4"), 4.0 * ND * S, A.add)
         if not more:
             quant("vq", "vs", 0, 128, r("vt"))
+        ts(fv, e2, dv_, A.subtract)
+        scan(r("zx"), r("d4"), r("zp"), 0.0, A.add, A.max)
+        ts(dl_, fv, -1.0, A.mult, col("flu", 4 + 2 * t), A.add)
+        ts(r("th"), r("n%d" % t), 4.0 * S, A.mult, cth, A.add)
+        if first:
+            own_d(3, True, "py0")
+        for b in (2, 3) if first else (1, 2, 3):
+            sort_d(b, act)
+        x = r("zx", 3, C, 4)
+        tt(r("ec"), x, r("it4"), A.max)
+        ts(r("ea"), x, r("th"), A.is_gt)
+        quant("tq", "ts", 0, 128, r("tt"))
+        for b in range(4):
+            mm(py[b], "wq", "wp", 128 * b, "tq", "ts", 0, 128)
+        sort_d(0, cp)
+        if first:
+            sort_d(1, cp)
         tt(r("eb"), r("ea"), r("ec"), A.add)
-        act(r("dl", B, C), r("ind"), scale=dl_)
-        act(r("dl", 0, B), r("da"), bias=-MLO)
+        for b in (0, 1):
+            pick_s(b, cp)
+            pick_s(b + 2, act)
+        tt(r("ed"), r("eb"), r("itd"), A.min)
+        quant("sq", "ss", 0, 128, r("st"))
+        if not first:
+            act(r("dl", B, C), r("ind"), scale=dl_)
         for b in range(4):
             act(r(w, 4 * NY + b, 4 * NH, 4), r(py[b], 0, B), scale=0.03125)
-        tt(r(srn, 0, 128), (r("dl"), r("r16", 0, 8)), r(src, 0, 128), A.add)
-        ts(r("oe"), r("eb"), 1 / S, A.mult)
-        tt(r(srn, 128, C), (r("dl"), r("r16", 8, 18)), r(src, 128, C), A.add)
+        if first:
+            act(r("dl", B, C), r("ind"), scale=dl_)
+            act(r("da"), r("zz", 0, B), bias=col("flm", 3 + 2 * t), scale=-1.0)
+        ts(r("oe"), r("ed"), 1 / S, A.mult)
+        if not first:
+            relabel(t, 0, 128)
+        for b in (0, 2, 1, 3):
+            mm(pd[b], "wq", "wp", 128 * b, "sq", "ss", 0, 128)
+        for b in (0, 2, 1, 3):
+            o = r(w, 4 * NH + b, 4 * (NH + kt), 4)
+            if b < 2:
+                ts(o, r(pd[b], 0, kt), 0.03125, A.mult)
+            else:
+                act(o, r(pd[b], 0, kt), scale=0.03125)
+        cp(r(wn, 4 * HF, 4 * C), (r(w), r("oe", 36, 72)))
+        act(r(wn, 0, 4 * HF), (r(w), r("oe", 0, 36)), ACT.Copy)
+        if first:
+            act(r("dl", 0, B), r("da"), bias=-MLO)
         if more:
             act(b1, col("e9", 3 + 2 * t), bias=col("base", t), scale=-GONE)
             act(eg, dv_, ACT.Relu, bias=GONE, scale=-GONE / U)
             act(b2_, col("e9", 4 + 2 * t), bias=b1, scale=-GONE)
             act(col("base", t + 1), eg, bias=b2_)
-        else:
-            act(r("oba"), r(srn), bias=MHI, scale=1 / U)
-            act(r("obo"), r("oba"), bias=-MHI)
-            dma("y", "so", T.ob[:], T.obo[15:128:16, :], [r("obo")], [])
-        for b in (0, 2, 1, 3):
-            mm(pd[b], "wq", "wp", 128 * b, "lq", "ls", lo + kt - 128, lo + kt)
-        for b in (0, 2, 1, 3):
-            o = r(w, 4 * NH + b, 4 * (NH + kt), 4)
-            if b < 2:
-                ts(o, r(pd[b], 128 - kt, 128), 0.03125, A.mult)
-            else:
-                act(o, r(pd[b], 128 - kt, 128), scale=0.03125)
-        win = r(w, 0, 4 * (NS + K))
-        cp(r(wn, 4 * HF, 4 * C), (win, r("oe", 36, 72)))
-        act(r(wn, 0, 4 * HF), (win, r("oe", 0, 36)), ACT.Copy)
 
     xa, xb = R * C, R * C + C
     w = "w%d" % (R % 2)
     quant("xq", "xs", xa + HF, xb, r(w, 4 * HF, 4 * C))
     quant("xq", "xs", xa, xa + HF, r(w, 0, 4 * HF))
+    relabel(R - 1, 128, C)
+    act(r("oba"), r("src%d" % (R % 2)), bias=MHI, scale=1 / U)
+    act(r("obo"), r("oba"), bias=-MHI)
     mm("pc", "vq", "vs", 0, "xq", "xs", xa + HF, xb)
     mm("pp", "vq", "vs", 0, "xq", "xs", xa, xa + HF)
     dma("y", "sc", T.oc[:], u8(r("xq", xa, xb)), [r("xq", xa, xb)], [])
+    cp(r("yo", HF, C), r("pc", 0, HF))
+    cp(r("yo", 0, HF), r("pp", 0, HF))
     for k in range(4):
         dma("y", "s%d" % k, T.osc[4 * k:4 * k + 4, :], T.xs[32 * k:32 * k + 4, xa:xb], [r("xs", xa, xb)], [])
-    act(r("yo", HF, C), r("pc", 0, HF), ACT.Copy)
-    cp(r("yo", 0, HF), r("pp", 0, HF))
-    dma("s", "sy", T.y[:], T.yo[:], [r("yo")], [])
+    dma("y", "sz", T.y[:, HF:C], T.yo[:, HF:C], [r("yo", HF, C)], [])
+    dma("y", "sy", T.y[:, 0:HF], T.yo[:, 0:HF], [r("yo", 0, HF)], [])
+    dma("s", "so", T.ob[:], T.obo[15:128:16, :], [r("obo")], [])
 
     marked = {q: sorted({i for p in ops for o in ops[p] for s, i in o[1] if s == q}) for q in eng}
     for q in eng:
@@ -474,5 +509,5 @@ def rank_program(g, core, T, topo):
             elif own is None and i in marked[q]:
                 ins.then_inc(T.sem["q" + q], 1)
     g.wait_ge(T.sem.sent, nl * len(sends))
-    for s in ("so", "sc", "sy", "s0", "s1", "s2", "s3"):
+    for s in ("so", "sc", "sy", "sz", "s0", "s1", "s2", "s3"):
         g.sync.wait_ge(T.sem[s], 16)

@@ -1,7 +1,7 @@
 from concourse.mybir import dt, AluOpType, AxisListType, ActivationFunctionType
 
 C, B, K, R = 288, 96, 64, 3
-HF = C // 2
+HF = 160
 NY, NH, ND = 288, 384, 448
 WW = 4 * (ND + C)
 U, EPS = 2.0 ** -8, 2.0 ** -17
@@ -11,22 +11,22 @@ GONE = 512.0
 BIG = 2.0 ** 93
 CT = [0, 288, 512, 672, 768]
 CW = [288, 224, 160, 128, 128]
-ORDER = [16, 15, 13, 12, 11, 10, 9, 8, 7, 6, 5, 4, 3, 2, 1]
-ON_SCALAR = (17, 14)
-QUANT_AFTER = {13: (0, 288), 10: (288, 512), 6: (512, 672)}
+ORDER = [16, 15, 13, 12, 11, 9, 8, 7, 6, 5, 4, 3, 2, 1]
+ON_SCALAR = (17, 14, 10)
+QUANT_AFTER = {12: (0, 288), 8: (288, 512), 4: (512, 672)}
 KT = [64, 48, 40]
 
 F32, BF, I32, U16, Q4, U8 = "float32", "bfloat16", "int32", "uint16", "float8_e4m3fn_x4", "uint8"
 SIZES = {
     BF: dict(w0=WW, w1=WW, dd=4 * C, ds=4 * 208, ut=512, vt=512, ones=128, ff=1040, b2=512, ct=4 * 896, junk=2448, junk2=384, tt=512,
-             st=512, zer=192, sd=C, dseg=C, ind=192, in2=192, pf=192, le=320, rl=320, lc=320, zc=C),
+             st=512, zer=192, lz=192, sd=C, dseg=C, ind=192, in2=192, pf=192, le=386, rl=386, lc=386, zc=C),
     Q4: dict(xq=4 * C, lq=R * C, uq=128, uq2=128, vq=128, wq=512, eq=512, bq=128, cq=896, tq=128, sq=128),
     U8: dict(xs=4 * C, ls=R * C, us=128, us2=128, vs=128, wp=512, es=512, bs=128, cs=896, ts=128, ss=128),
     I32: dict(pi=2, ci=6, oui=8),
     U16: dict(ou=8, r16=18, o4=8 * R, op=8 * R, os16=16 * R, ol=16 * R, ot=24, oe=72),
     F32: dict(n0=1, n1=1, n2=1, gj=128, ga=128, cf=6, cc=24, i16=C, i4=C, it16=72, it4=72, itd=72, ed=72, mx=C, hd=C, d1=C, d4=C, kk=18,
-              thr=4, jl=10, ju=10, e9=10, fl=10, flm=10, flu=10, pg=C, src0=C, src1=C, aa=C, hh=C, rs=18, adj=18, ext=C, zz=C + 64,
-              kd=256, kr=256, kt=64, kb=64, ke=32, mm=64 * R, acc=2, lz=192, d16=192, ex=192, er=12, ep=12, tx=B, tr=24, tp=24, zp=C,
+              thr=8, jl=10, ju=10, e9=10, fl=10, flm=10, flu=10, pg=C, src0=C, src1=C, aa=C, hh=C, rs=18, adj=18, ext=C, zz=C + 64,
+              kd=160, kr=160, kt=64, kb=64, ke=32, mm=64 * R, acc=2, d16=192, ex=192, er=12, ep=12, tx=B, tr=24, tp=24, zp=C,
               zx=C, th=1, ea=72, eb=72, ec=72, da=B, dl=C, kz=64, base=4, yo=C, oba=C, obo=C),
 }
 SCRATCH = {n: ("sbuf", [128, k], d) for d in SIZES for n, k in SIZES[d].items()}
@@ -163,17 +163,17 @@ def rank_program(g, core, T, topo):
         arrives("al%d" % t, nin, [r("ol", 16 * t, 16 * t + 16)])
         arrives("ap%d" % t, nin, [r("op", 8 * t, 8 * t + 8)])
 
-    xhi, xlo = r("w0", 2 * C, 4 * C), r("w0", 0, 2 * C)
-    dma("y", "lx", ap(xhi), T.x[:, 2 * C:4 * C], [], [xhi])
+    xhi, xlo = r("w0", 4 * HF, 4 * C), r("w0", 0, 4 * HF)
+    dma("y", "lx", ap(xhi), T.x[:, 4 * HF:4 * C], [], [xhi])
     dma("s", "lu", T.ut[:], T.u[:], [], [r("ut")])
-    dma("y", "ly", ap(xlo), T.x[:, 0:2 * C], [], [xlo])
+    dma("y", "ly", ap(xlo), T.x[:, 0:4 * HF], [], [xlo])
     dma("y", "lw", u8(r("wq")), T.wc[:], [xlo], [r("wq")])
     dma("y", "lp", T.wp[:], T.ws[:], [], [r("wp")])
     dma("y", "lv", T.vt[:], T.v[:], [], [r("vt")])
 
     q_, qm1, h_, r_, q4, g_ = (col("cf", j) for j in range(6))
-    mq, z0, t0, ccs, ck, ku, ctl, cz0, cz, cth, t1, cu, c1, t3, t4, dv_, e2, fv, dl_, eg, b1, b2_ = (col("cc", j) for j in range(22))
-    zer = r("zer")
+    mq, z0, t0, ccs, ck, ku, ctl, cz0, cz, cth, t1, cu, c1, t3, t4, dv_, e2, fv, dl_, eg, b1, b2_, sx = (col("cc", j) for j in range(23))
+    zer, zwr, zun = r("zer"), r("zz", 64, 64 + B), r("zz", 64 + B, 64 + C)
     fill(r("ones"), 1.0)
     fill(r("ff", 0, 520), 0.0)
     iota(r("pi"), [[15, 2]], 0, 1)
@@ -193,16 +193,13 @@ def rank_program(g, core, T, topo):
         iota(r("ct", 4 * 720, 4 * 896), [[0, 704]], 0)
         iota(r("pg"), [[1, C]], -144)
         iota(r("i4"), [[0, 72], [1, 4]], 0)
-        iota(r("zz", C + 1, C + 64), [[0, 63]], 0)
-        iota(r("kd", 0, 192), [[0, 192]], 0)
-        iota(r("kz"), [[0, 2], [-30000, 32]], 70000)
+        iota(r("zz", 0, 63), [[0, 63]], 0)
+        iota(r("kd", 0, B), [[0, B]], 0)
+        iota(r("kz"), [[0, 2], [30000, 32]], -70000)
         iota(zer, [[0, 192]], 0)
         iota(r("ds", 192, 4 * 208, 208), [[0, 4]], 0)
         iota(r("zc", 0, B), [[1, B]], 1)
-        iota(r("rl"), [[0, 320]], 1)
-        iota(r("le", 0, 8), [[0, 8]], 32)
-        iota(r("le", 168, 176), [[0, 8]], 48)
-        iota(r("rl", 7, 176, 168), [[0, 2]], 0)
+        iota(r("le", 192, 194), [[0, 2]], 0)
         iota(r("tt", 4 * B, 512), [[0, 128]], 0)
         iota(r("st", 4 * K, 512), [[0, 256]], 0)
 
@@ -217,6 +214,7 @@ def rank_program(g, core, T, topo):
     ts(col("ci", 5), col("pi", 0), 4, A.logical_shift_right)
     fill(r("ct", 4 * 240, 4 * 288), 0.0)
     cp(r("cf"), r("ci"))
+    fill(r("rl"), -1.0 / 256)
     ts(ctl, q4, 4.0 * 144, A.add)
     ts(t3, q_, B + 0.5, A.add)
     ts(cz0, q4, S, A.mult, 4.0 * (NY - 1) * S - 6, A.add)
@@ -245,10 +243,10 @@ def rank_program(g, core, T, topo):
     act(ck, z0, bias=t1, scale=-65024.0)
     act(r("d16"), r("mx", 0, 192), bias=-34.0, scale=-36.0 / BIG)
     act(ku, q_, ACT.Sign, bias=-2.5)
-    act(mq, q_, bias=MLO, scale=0.0625)
+    act(mq, q_, bias=-MLO, scale=-0.0625)
     act(cu, q_, bias=15 * U, scale=-U)
     act(r("kk"), r("it16", 0, 18), bias=ck)
-    act(col("base", 0), ku, bias=MHI + GONE / 2, scale=GONE / 2)
+    act(col("base", 0), ku, bias=-MHI - (GONE + B) / 2, scale=-(GONE - B) / 2)
 
     pd = ["pd0", "pd1", "pd2", "pd3"]
     py = ["py0", "py1", "pp", "pc"]
@@ -307,18 +305,11 @@ def rank_program(g, core, T, topo):
         if not first:
             relabel(t - 1, 128, C)
         dv = r("ct", 0, 4 * C, 4)
-        tt(r("aa", HF, C), r("py1", 0, HF), r("mx", HF, C), A.add)
+        tt(r("aa", HF, C), r("py1", 0, C - HF), r("mx", HF, C), A.add)
         if first:
             tile_e(1)
-            scan(r("hh", HF, C), r("hd", HF, C), r("aa", HF, C), -BIG, A.min, A.max)
+        scan(r("hh", HF, C), r("hd", HF, C), r("aa", HF, C), -BIG, A.min, A.max)
         tt(r("aa", 0, HF), r("pp", 0, HF), r("mx", 0, HF), A.add)
-        if first:
-            quant("bq", "bs", 0, 128, r("b2"))
-        else:
-            scan(r("hh", HF, C), r("hd", HF, C), r("aa", HF, C), -BIG, A.min, A.max)
-        if t == 1:
-            relabel(0, 0, 128)
-        scan(r("hh", 0, HF), r("hd", 0, HF), r("aa", 0, HF), -BIG, A.min, A.max)
         for m in ON_SCALAR:
             act(jview(m), r("py0", 0, 16 * m), ACT.Sign, bias=col("hh", 16 * m + 15), scale=-1.0)
         for m in ON_SCALAR:
@@ -326,20 +317,22 @@ def rank_program(g, core, T, topo):
         for m in ORDER:
             ts(cview(m), r("pp", 0, 16 * m), col("hh", 16 * m + 15), A.is_lt)
             act(jview(m), cview(m), acc=col("rs", m))
-            if m == ORDER[0]:
+            if m == 16:
+                scan(r("hh", 0, HF), r("hd", 0, HF), r("aa", 0, HF), -BIG, A.min, A.max)
+            if first and m == 13:
+                quant("bq", "bs", 0, 128, r("b2"))
+            if m == 15:
                 tt(dv, r("hh"), r("pp", 0, C), A.is_ge)
             if m in QUANT_AFTER:
                 a, b = QUANT_AFTER[m]
                 quant("cq", "cs", a, b, r("ct", 4 * a, 4 * b))
-            if first and m == 3:
-                tile_e(2)
             if first and m == 8:
                 quant("cq", "cs", 768, 896, r("ct", 4 * 768, 4 * 896))
             if first and m == ORDER[3]:
                 tt(r("fl"), r("e9"), r("ju"), A.add)
-            if m == 13:
+            if m == 11:
                 scan(r("dseg"), r("sd"), dv, 0.0, A.min, A.add)
-            if m == 10:
+            if m == 8:
                 tt(r("adj"), r("kk"), r("dseg", 15, C, 16), A.subtract)
         for k in (0, 1, 2):
             mm("pc", "bq", "bs", 0, "cq", "cs", CT[k], CT[k] + CW[k], start=(k == 0), stop=(k == 2))
@@ -347,12 +340,14 @@ def rank_program(g, core, T, topo):
         if first:
             for b in (1, 2, 0):
                 act(r(src, B * b, B * b + B), r("pg", B * b, B * b + B), bias=col("fl", b), scale=EPS)
-            act(col("zz", C), q_, bias=-MHI, scale=0.0)
-            act(r("thr"), r("it16", 0, 4), bias=t3)
+            act(col("zz", 63), q_, bias=MHI, scale=0.0)
+            act(r("thr", 0, 4), r("it16", 0, 4), bias=t3)
         else:
             for b in range(4):
                 own_d(b)
         tt(r("d1", B + 15, C, 16), r("adj", 6, 18), r("rs", 6, 18), A.subtract)
+        if first:
+            tile_e(2)
         quant("cq", "cs", 672, 800, r("ct", 4 * 672, 4 * 800))
         for k in (3, 4):
             mm("py1", "bq", "bs", 0, "cq", "cs", CT[k], CT[k] + 128, start=False, stop=(k == 4))
@@ -361,104 +356,103 @@ def rank_program(g, core, T, topo):
                 far_d(b)
         scan(r("ext", B, C), r("pc", B, C), r("d1", B, C), -65024.0, A.max, A.add)
         if first:
-            ts(r("kb", 32, 64), r("gj", 0, 32), h_, A.not_equal, 4096.0, A.mult)
+            ts(r("kb", 32, 64), r("gj", 0, 32), h_, A.not_equal, -4096.0, A.mult)
             ts(r("ke"), r("i16", 0, 32), q_, A.not_equal, cu, A.mult)
         tt(r("d1", 15, B, 16), r("adj", 0, 6), r("rs", 0, 6), A.subtract)
         ts(r("r16", 6, 18), r("ext", B + 15, C, 16), ccs, A.add)
         if first:
             tt(r("kb", 0, 32), r("kb", 32, 64), r("ke"), A.add)
+            ts(r("flm"), r("fl"), MLO, A.add)
         scan(r("ext", 0, B), r("py1", 0, B), r("d1", 0, B), -65024.0, A.max, A.add)
-        cp((r("zz", 0, C), r("r16", 6, 18)), r(src, B, C))
+        cp((r("zz", 64, 64 + C), r("r16", 6, 18)), r(src, B, C))
         ts(r("r16", 0, 6), r("ext", 15, B, 16), ccs, A.add)
         if first:
-            ts(col("kd", 192), col("kb", 0), mq, A.add)
-            tt(r("kd", 193, 256), r("kb", 1, 64), r("kb", 0, 63), A.subtract)
+            ts(col("kd", B), col("kb", 0), mq, A.add)
+            tt(r("kd", B + 1, 160), r("kb", 1, 64), r("kb", 0, 63), A.subtract)
             act(r("d4"), r("i4"), ACT.Abs, bias=r_, scale=-1.0)
             own_d(0, True)
             act(r("d4"), r("d4"), ACT.Sign)
             own_d(1, True)
             act(r("d4"), r("d4"), bias=-14.0, scale=16.0)
             own_d(2, True)
-        cp((r("zz", 0, C), r("r16", 0, 6)), r(src, 0, B))
+        cp((r("zz", 64, 64 + C), r("r16", 0, 6)), r(src, 0, B))
         if first:
             tile_e(3)
-        act(r("lz"), r("zz", B, C), ACT.Relu, bias=15 * U, scale=-1.0)
+        act(r("lz"), zun, ACT.Relu, bias=15 * U, scale=-1.0)
         if first:
             act(r("it4"), r("it16"), bias=t4, scale=S)
-        scan(r("kr"), r("zz", B, C + 64), r("kd"), col("base", t), A.add, A.add)
-        scan(r("ex"), r("d16"), r("zz", B, C), 0.0, A.add, A.max)
-        put("v", lambda: g.vector.transpose(T.kt[:, 0:64], T.kr[:, 192:256]), [r("kr", 192, 256)], [r("kt")])
+            act(r("thr", 4, 8), r("thr", 0, 4), bias=B - 0.5, scale=-1.0)
+        put("v", lambda t=t: g.vector.tensor_tensor_scan(T.kr[:, 0:160], T.zz[:, 159::-1], T.kd[:, 0:160], T.base[:, t:t + 1], A.add, A.add),
+            [r("zz", 0, 160), r("kd"), col("base", t)], [r("kr")])
+        scan(r("ex"), r("d16"), zun, 0.0, A.add, A.max)
+        put("v", lambda: g.vector.transpose(T.kt[:, 0:64], T.kr[:, B:160]), [r("kr", B, 160)], [r("kt")])
+        scan(r("tx"), r("d4", 0, B), zwr, 0.0, A.add, A.max)
         ts(r("er"), r("ex", 15, 192, 16), MLO, A.add, MLO, A.subtract)
-        for b in range(0 if first else 2, 4):
+        act(r("da"), zwr, bias=col("flm", 3 + 2 * t), scale=-1.0)
+        for b in range(0 if first else 2, 3):
             far_d(b)
-        if not first:
-            act(r("da"), r("zz", 0, B), bias=col("flm", 3 + 2 * t), scale=-1.0)
-            act(r("dl", 0, B), r("da"), bias=-MLO)
-        scan(r("mm", 64 * t, 64 * t + 64), r("kz"), r("kt"), 0.0, A.max, A.min)
+        act(r("dl", 0, B), r("da"), bias=-MLO)
+        far_d(3)
+        if first:
+            mm("pd3", "eq", "es", 384, "xq", "xs", xa, xb)
+        scan(r("mm", 64 * t, 64 * t + 64), r("kz"), r("kt"), 0.0, A.min, A.max)
         send(T["n%d" % t][:, 0:1], ap(m2), "an%d" % t, [m2])
+        ts(r("tr"), r("tx", 3, B, 4), MLO, A.add, MLO, A.subtract)
         tt(r("ep"), r("ex", 15, 192, 16), r("er"), A.subtract)
-        scan(r("tx"), r("d4", 0, B), r("zz", 0, B), 0.0, A.add, A.max)
         ts(r("ind"), r("lz"), m2, A.add, m1, A.is_equal)
+        tt(r("tp"), r("tx", 3, B, 4), r("tr"), A.subtract)
         ts(r("os16", la, la + 12), r("ep"), 1 / EPS, A.mult, 144.0, A.add)
         send(ap(r("ol", la, la + 12)), ap(r("os16", la, la + 12)), "al%d" % t, [r("os16", la, la + 12)])
-        ts(r("tr"), r("tx", 3, B, 4), MLO, A.add, MLO, A.subtract)
         scan(r("pf"), r("ind"), zer, float(B), A.add, A.add)
-        ts(r("in2"), r("ind"), 1024.0, A.mult, 512.0, A.subtract)
-        for k in (0, 1):
+        ns = n4 - 2
+        for k, a in ((ns, 194), (ns + 1, 0)):
+            scan(r("le", a, a + 192), r("ind"), zer, col("thr", 4 + k), A.add, A.min)
+        for k in range(ns):
             act(r("junk2", 192 * k, 192 * k + 192), r("pf"), ACT.Sign, bias=col("thr", k), scale=-1.0, acc=col("acc", k))
-        for k in range(2, n4):
-            ts(r("le", 168 * (k - 2) + 8, 168 * (k - 2) + 200 - 16 * k), r("pf", 16 * k, 192), col("thr", k), A.is_lt)
-        tt(r("tp"), r("tx", 3, B, 4), r("tr"), A.subtract)
-        scan(r("zc", B, C), r("pf"), r("in2"), 0.0, A.max, A.min)
-        le_end = 168 if n4 == 3 else 320
-        scan(r("lc", 7, le_end), r("rl", 7, le_end), r("le", 7, le_end), 0.0, A.mult, A.add)
         ts(r("ot"), r("tp"), 2.0 ** 19, A.mult, ctl, A.add)
+        ts(r("in2"), r("ind"), 1024.0, A.mult, 512.0, A.subtract)
+        put("v", lambda: g.vector.tensor_tensor_scan(T.lc[:, 0:386], T.rl[:, 0:386], T.le[:, 385::-1], 0.0, A.add, A.max),
+            [r("rl"), r("le")], [r("lc")])
+        scan(r("zc", B, C), r("pf"), r("in2"), 0.0, A.max, A.min)
         ts(dv_, m1, m2, A.subtract)
-        act(r("zp"), (r("zc"), r("r16")), bias=cz, scale=4.0 * S)
-        act(r("tt", 0, 4 * B), (r(w, 0, 4 * C), r("ot")), ACT.Copy)
-        cp(r("o4", lb + 2, lb + n4), r("lc", 167, le_end, 152))
-        ts(r("o4", lb, lb + 2), r("acc"), 192.0, A.add, 0.5, A.mult)
+        ts(r("o4", lb, lb + ns), r("acc", 0, ns), 192.0, A.add, 0.5, A.mult)
+        ts(r("o4", lb + ns, lb + n4), r("lc", 191, 386, 194), -256.0, A.mult)
         send(ap(r("op", lb, lb + n4)), ap(r("o4", lb, lb + n4)), "ap%d" % t, [r("o4", lb, lb + n4)])
+        act(r("tt", 2 * B, 4 * B), (r(w, 0, 4 * C), r("ot", 12, 24)))
+        act(r("zp"), (r("zc"), r("r16")), bias=cz, scale=4.0 * S)
         ts(e2, dv_, 0.0, A.is_equal, c1, A.mult)
+        cp(r("tt", 0, 2 * B), (r(w, 0, 4 * C), r("ot", 0, 12)))
         if first:
-            ts(r("flm"), r("fl"), MLO, A.add)
             ts(r("flu"), r("fl"), 15 * U, A.subtract)
             ts(r("itd"), r("it4"), 4.0 * ND * S, A.add)
         if not more:
             quant("vq", "vs", 0, 128, r("vt"))
         ts(fv, e2, dv_, A.subtract)
-        scan(r("zx"), r("d4"), r("zp"), 0.0, A.add, A.max)
-        ts(dl_, fv, -1.0, A.mult, col("flu", 4 + 2 * t), A.add)
-        ts(r("th"), r("n%d" % t), 4.0 * S, A.mult, cth, A.add)
-        if first:
-            own_d(3, True, "py0")
-        for b in (2, 3) if first else (1, 2, 3):
-            sort_d(b, act)
-        x = r("zx", 3, C, 4)
-        tt(r("ec"), x, r("it4"), A.max)
-        ts(r("ea"), x, r("th"), A.is_gt)
         quant("tq", "ts", 0, 128, r("tt"))
         for b in range(4):
             mm(py[b], "wq", "wp", 128 * b, "tq", "ts", 0, 128)
-        sort_d(0, cp)
+        ts(dl_, fv, -1.0, A.mult, col("flu", 4 + 2 * t), A.add)
+        scan(r("zx"), r("d4"), r("zp"), 0.0, A.add, A.max)
         if first:
-            sort_d(1, cp)
-        tt(r("eb"), r("ea"), r("ec"), A.add)
+            own_d(3)
+        for b in range(1, 4):
+            sort_d(b, act)
+        ts(r("th"), r("n%d" % t), -4.0 * S, A.mult, cth, A.add)
+        sort_d(0, cp)
+        x = r("zx", 3, C, 4)
+        tt(r("ec"), x, r("it4"), A.max)
+        ts(r("ea"), x, r("th"), A.is_gt)
         for b in (0, 1):
             pick_s(b, cp)
             pick_s(b + 2, act)
-        tt(r("ed"), r("eb"), r("itd"), A.min)
+        tt(r("eb"), r("ea"), r("ec"), A.add)
         quant("sq", "ss", 0, 128, r("st"))
-        if not first:
-            act(r("dl", B, C), r("ind"), scale=dl_)
+        act(r("dl", B, C), r("ind"), scale=dl_)
         for b in range(4):
             act(r(w, 4 * NY + b, 4 * NH, 4), r(py[b], 0, B), scale=0.03125)
-        if first:
-            act(r("dl", B, C), r("ind"), scale=dl_)
-            act(r("da"), r("zz", 0, B), bias=col("flm", 3 + 2 * t), scale=-1.0)
+        tt(r("ed"), r("eb"), r("itd"), A.min)
+        relabel(t, 0, 128)
         ts(r("oe"), r("ed"), 1 / S, A.mult)
-        if not first:
-            relabel(t, 0, 128)
         for b in (0, 2, 1, 3):
             mm(pd[b], "wq", "wp", 128 * b, "sq", "ss", 0, 128)
         for b in (0, 2, 1, 3):
@@ -467,33 +461,33 @@ def rank_program(g, core, T, topo):
                 ts(o, r(pd[b], 0, kt), 0.03125, A.mult)
             else:
                 act(o, r(pd[b], 0, kt), scale=0.03125)
-        cp(r(wn, 4 * HF, 4 * C), (r(w), r("oe", 36, 72)))
-        act(r(wn, 0, 4 * HF), (r(w), r("oe", 0, 36)), ACT.Copy)
-        if first:
-            act(r("dl", 0, B), r("da"), bias=-MLO)
+        cp(r(wn, 4 * HF, 4 * C), (r(w), r("oe", HF // 4, 72)))
+        act(r(wn, 0, 4 * HF), (r(w), r("oe", 0, HF // 4)), ACT.Copy)
+        if not more:
+            relabel(t, 128, C)
         if more:
-            act(b1, col("e9", 3 + 2 * t), bias=col("base", t), scale=-GONE)
+            act(b1, col("e9", 3 + 2 * t), bias=col("kr", B - 1), scale=GONE - B)
+            act(sx, m2, bias=MLO + GONE)
             act(eg, dv_, ACT.Relu, bias=GONE, scale=-GONE / U)
-            act(b2_, col("e9", 4 + 2 * t), bias=b1, scale=-GONE)
-            act(col("base", t + 1), eg, bias=b2_)
+            act(b2_, col("e9", 4 + 2 * t), bias=b1, scale=sx)
+            act(col("base", t + 1), eg, bias=b2_, scale=-1.0)
 
     xa, xb = R * C, R * C + C
     w = "w%d" % (R % 2)
     quant("xq", "xs", xa + HF, xb, r(w, 4 * HF, 4 * C))
     quant("xq", "xs", xa, xa + HF, r(w, 0, 4 * HF))
-    relabel(R - 1, 128, C)
     act(r("oba"), r("src%d" % (R % 2)), bias=MHI, scale=1 / U)
     act(r("obo"), r("oba"), bias=-MHI)
     mm("pc", "vq", "vs", 0, "xq", "xs", xa + HF, xb)
     mm("pp", "vq", "vs", 0, "xq", "xs", xa, xa + HF)
     dma("y", "sc", T.oc[:], u8(r("xq", xa, xb)), [r("xq", xa, xb)], [])
-    cp(r("yo", HF, C), r("pc", 0, HF))
+    cp(r("yo", HF, C), r("pc", 0, C - HF))
     cp(r("yo", 0, HF), r("pp", 0, HF))
     for k in range(4):
         dma("y", "s%d" % k, T.osc[4 * k:4 * k + 4, :], T.xs[32 * k:32 * k + 4, xa:xb], [r("xs", xa, xb)], [])
-    dma("y", "sz", T.y[:, HF:C], T.yo[:, HF:C], [r("yo", HF, C)], [])
-    dma("y", "sy", T.y[:, 0:HF], T.yo[:, 0:HF], [r("yo", 0, HF)], [])
-    dma("s", "so", T.ob[:], T.obo[15:128:16, :], [r("obo")], [])
+    dma("y", "so", T.ob[:], T.obo[15:128:16, :], [r("obo")], [])
+    dma("s", "sz", T.y[:, HF:C], T.yo[:, HF:C], [r("yo", HF, C)], [])
+    dma("s", "sy", T.y[:, 0:HF], T.yo[:, 0:HF], [r("yo", 0, HF)], [])
 
     marked = {q: sorted({i for p in ops for o in ops[p] for s, i in o[1] if s == q}) for q in eng}
     for q in eng:

@@ -1,7 +1,8 @@
-from concourse.mybir import dt, AluOpType, AxisListType, ActivationFunctionType
+from concourse.mybir import dt, AluOpType, ActivationFunctionType
 
 C, B, K, R = 288, 96, 64, 3
 HF = 160
+TOP = 224
 NY, NH, ND = 288, 384, 448
 WW = 4 * (ND + C)
 U, EPS = 2.0 ** -8, 2.0 ** -17
@@ -11,9 +12,10 @@ GONE = 512.0
 BIG = 2.0 ** 93
 CT = [0, 288, 512, 672, 768]
 CW = [288, 224, 160, 128, 128]
-ORDER = [16, 15, 13, 12, 11, 9, 8, 7, 6, 5, 4, 3, 2, 1]
 ON_SCALAR = (17, 14, 10)
-QUANT_AFTER = {12: (0, 288), 8: (288, 512), 4: (512, 672)}
+PARTS = [(10, 18, "pc"), (6, 10, "py0"), (0, 6, "py1")]
+PLAN = [16, "hh", 15, 13, "dv", 12, 11, "q0", "dseg", "q1", 9, 8, "adj", 7, 6, 5, 4, "d0", "q2", 3, 2, 1,
+        "x0", "d1", "q3", "r0", "x1", "d2", "s0", "r1", "x2", "s1", "r2", "s2"]
 KT = [64, 48, 40]
 
 F32, BF, I32, U16, Q4, U8 = "float32", "bfloat16", "int32", "uint16", "float8_e4m3fn_x4", "uint8"
@@ -22,9 +24,9 @@ SIZES = {
              st=512, zer=192, lz=192, sd=C, dseg=C, ind=192, in2=192, pf=192, le=386, rl=386, lc=386, zc=C),
     Q4: dict(xq=4 * C, lq=R * C, uq=128, uq2=128, vq=128, wq=512, eq=512, bq=128, cq=896, tq=128, sq=128),
     U8: dict(xs=4 * C, ls=R * C, us=128, us2=128, vs=128, wp=512, es=512, bs=128, cs=896, ts=128, ss=128),
-    I32: dict(pi=2, ci=6, oui=8),
+    I32: dict(pi=1, ci=5, oui=8),
     U16: dict(ou=8, r16=18, o4=8 * R, op=8 * R, os16=16 * R, ol=16 * R, ot=24, oe=72),
-    F32: dict(n0=1, n1=1, n2=1, gj=128, ga=128, cf=6, cc=24, i16=C, i4=C, it16=72, it4=72, itd=72, ed=72, mx=C, hd=C, d1=C, d4=C, kk=18,
+    F32: dict(n0=1, n1=1, n2=1, gj=128, ga=128, cf=5, cc=24, i16=C, i4=C, it16=72, it4=72, itd=72, ed=72, mx=C, hd=C, d1=C, d4=C, kk=18,
               thr=8, jl=10, ju=10, e9=10, fl=10, flm=10, flu=10, pg=C, src0=C, src1=C, aa=C, hh=C, rs=18, adj=18, ext=C, zz=C + 64,
               kd=160, kr=160, kt=64, kb=64, ke=32, mm=64 * R, acc=2, d16=192, ex=192, er=12, ep=12, tx=B, tr=24, tp=24, zp=C,
               zx=C, th=1, ea=72, eb=72, ec=72, da=B, dl=C, kz=64, base=4, yo=C, oba=C, obo=C),
@@ -171,26 +173,24 @@ def rank_program(g, core, T, topo):
     dma("y", "lp", T.wp[:], T.ws[:], [], [r("wp")])
     dma("y", "lv", T.vt[:], T.v[:], [], [r("vt")])
 
-    q_, qm1, h_, r_, q4, g_ = (col("cf", j) for j in range(6))
+    q_, h_, r_, q4, g_ = (col("cf", j) for j in range(5))
     mq, z0, t0, ccs, ck, ku, ctl, cz0, cz, cth, t1, cu, c1, t3, t4, dv_, e2, fv, dl_, eg, b1, b2_, sx = (col("cc", j) for j in range(23))
     zer, zwr, zun = r("zer"), r("zz", 64, 64 + B), r("zz", 64 + B, 64 + C)
     fill(r("ones"), 1.0)
     fill(r("ff", 0, 520), 0.0)
-    iota(r("pi"), [[15, 2]], 0, 1)
-    iota(r("i16"), [[0, 18], [1, 16]], 0)
     iota(r("oui"), [[16, 8]], 0)
+    iota(r("pi"), [[0, 1]], 0, 1)
+    iota(r("i16"), [[0, 18], [1, 16]], 0)
     iota(r("gj"), [[1, 8], [0, 16]], 0)
     act(r("ff", 520, 1040), r("ff", 0, 520), ACT.Copy)
     ident(r("ff", 2, 514, 4))
     ident(r("ff", 523, 1035, 4))
     iota(r("it16"), [[16, 72]], 0)
     iota(r("jl"), [[1, 10]], 0)
-    iota(r("ct", 4 * 464, 4 * 512), [[0, 192]], 0)
+    iota(r("ct", 4 * 624, 4 * 672), [[0, 192]], 0)
 
     def late_rows():
         iota(r("sd"), [[0, 18], [1, 16]], 0)
-        iota(r("ct", 4 * 624, 4 * 672), [[0, 192]], 0)
-        iota(r("ct", 4 * 720, 4 * 896), [[0, 704]], 0)
         iota(r("pg"), [[1, C]], -144)
         iota(r("i4"), [[0, 72], [1, 4]], 0)
         iota(r("zz", 0, 63), [[0, 63]], 0)
@@ -200,53 +200,37 @@ def rank_program(g, core, T, topo):
         iota(r("ds", 192, 4 * 208, 208), [[0, 4]], 0)
         iota(r("zc", 0, B), [[1, B]], 1)
         iota(r("le", 192, 194), [[0, 2]], 0)
-        iota(r("tt", 4 * B, 512), [[0, 128]], 0)
-        iota(r("st", 4 * K, 512), [[0, 256]], 0)
+        iota(r("rl"), [[0, 386]], 0)
+        put("g", lambda: g.affine_select(T.rl[:, 0:386], T.rl[:, 0:386], [[0, 386]], A.is_gt, -1.0 / 256, 0, 0), [r("rl")], [r("rl")])
 
     def tile_e(b):
         a = (2, 522, 0, 520)[b]
         quant("eq", "es", 128 * b, 128 * b + 128, r("ff", a, a + 512))
 
-    ts(r("ci", 0, 2), r("pi"), 15, A.bitwise_and)
-    ts(col("ci", 2), col("pi", 0), 4, A.logical_shift_right, 1, A.bitwise_and)
-    ts(col("ci", 3), col("pi", 0), 2, A.logical_shift_right, 3, A.bitwise_and)
-    ts(col("ci", 4), col("pi", 0), 3, A.bitwise_and)
-    ts(col("ci", 5), col("pi", 0), 4, A.logical_shift_right)
-    fill(r("ct", 4 * 240, 4 * 288), 0.0)
-    cp(r("cf"), r("ci"))
-    fill(r("rl"), -1.0 / 256)
-    ts(ctl, q4, 4.0 * 144, A.add)
-    ts(t3, q_, B + 0.5, A.add)
-    ts(cz0, q4, S, A.mult, 4.0 * (NY - 1) * S - 6, A.add)
     cp(r("ou"), r("oui"))
-    ts(r("mx"), r("i16"), q_, A.not_equal, -BIG, A.mult)
-    act(r("hd"), r("i16"), bias=-0.5 * BIG, scale=BIG)
-    act(r("ga"), r("gj"), ACT.Abs, bias=g_, scale=-1.0)
-    act(z0, q_, ACT.Relu, bias=1.0, scale=-1.0)
-    act(t0, q_, bias=-7680.0, scale=512.0)
-    act(r("b2", 0, 512, 4), r("ga"), ACT.Relu, bias=1.0, scale=-1.0)
+    fill(r("ct", 4 * 240, 4 * 288), 0.0)
     fill(col("rs", 0), 0.0)
+    ts(col("ci", 0), r("pi"), 15, A.bitwise_and)
+    ts(col("ci", 1), r("pi"), 4, A.logical_shift_right, 1, A.bitwise_and)
+    ts(col("ci", 2), r("pi"), 2, A.logical_shift_right, 3, A.bitwise_and)
+    ts(col("ci", 3), r("pi"), 3, A.bitwise_and)
+    ts(col("ci", 4), r("pi"), 4, A.logical_shift_right)
+    fill(r("ct", 4 * 720, 4 * 896), 0.0)
+    cp(r("cf"), r("ci"))
     quant("uq", "us", 0, 128, r("ut"))
-    ts(c1, q_, U, A.mult, 1 - 15 * U, A.add)
-    ts(cth, q4, S, A.mult, (4.0 * (NH - 0.5) - 4 * MLO) * S, A.add)
-    ts(t4, q_, S, A.mult)
-    ts(cz, r_, 2.0, A.mult, cz0, A.add)
+    quant("cq", "cs", 768, 896, r("ct", 4 * 768, 4 * 896))
     put("v", lambda: g.vector.tensor_copy(T.uq2[:, 0:128].bitcast(dt.uint32), T.uq[:, 0:128].bitcast(dt.uint32).indirect(T.ou[:, 0:8])),
         [r("uq"), r("ou")], [r("uq2")])
+    quant("xq", "xs", HF, C, xhi)
+    ts(r("mx"), r("i16"), q_, A.not_equal, -BIG, A.mult)
+    act(r("hd"), r("i16"), bias=-0.5 * BIG, scale=BIG)
     put("s", lambda: g.scalar.activation(T.us2[:, 0:128], T.us[:, 0:128].indirect(T.ou[:, 0:8]), ACT.Copy), [r("us"), r("ou")], [r("us2")])
-    tile_e(0)
-    for b in range(1, 4):
-        act(r("b2", b, 512, 4), r("ga"), ACT.Relu, bias=1.0, scale=-1.0)
+    act(r("ga"), r("gj"), ACT.Abs, bias=g_, scale=-1.0)
+    act(z0, q_, ACT.Relu, bias=1.0, scale=-1.0)
     act(t1, q_, bias=15.0, scale=-1.0)
-    act(ccs, z0, bias=t0, scale=65024.0)
-    act(r("ju"), r("jl"), scale=U)
+    for b in range(4):
+        act(r("b2", b, 512, 4), r("ga"), ACT.Relu, bias=1.0, scale=-1.0)
     act(ck, z0, bias=t1, scale=-65024.0)
-    act(r("d16"), r("mx", 0, 192), bias=-34.0, scale=-36.0 / BIG)
-    act(ku, q_, ACT.Sign, bias=-2.5)
-    act(mq, q_, bias=-MLO, scale=-0.0625)
-    act(cu, q_, bias=15 * U, scale=-U)
-    act(r("kk"), r("it16", 0, 18), bias=ck)
-    act(col("base", 0), ku, bias=-MHI - (GONE + B) / 2, scale=-(GONE - B) / 2)
 
     pd = ["pd0", "pd1", "pd2", "pd3"]
     py = ["py0", "py1", "pp", "pc"]
@@ -270,11 +254,10 @@ def rank_program(g, core, T, topo):
         kt, la, lb = KT[t], 16 * t, 8 * t
         n4 = (kt + 15) // 16
 
-        def own_d(b, product=False, bank=None):
-            bank = bank or pd[b]
+        def own_d(b, product=False):
             if product:
-                mm(bank, "eq", "es", 128 * b, "xq", "xs", xa, xb)
-            act(r(w, 4 * ND + b, WW, 4), r(bank, 0, C), ACT.Copy)
+                mm(pd[b], "eq", "es", 128 * b, "xq", "xs", xa, xb)
+            act(r(w, 4 * ND + b, WW, 4), r(pd[b], 0, C), ACT.Copy)
 
         def far_d(b):
             mm(pd[b], "eq", "es", 128 * b, "lq", "ls", xa, xb)
@@ -286,11 +269,8 @@ def rank_program(g, core, T, topo):
         def pick_s(b, call):
             call(r("st", b, 64 * n4, 4), (r("ds", 208 * b, 208 * b + 193), r("op", lb, lb + n4)))
 
-        quant("xq", "xs", xa + HF, xb, r(w, 4 * HF, 4 * C))
-        if first:
-            ts(r("d1"), r("i16"), qm1, A.not_equal, 1.0 - 1.0 / 128, A.subtract)
-            ts(r("e9"), r("jl"), q_, A.is_equal)
-            act(r("d1"), r("d1"), scale=65536.0)
+        if not first:
+            quant("xq", "xs", xa + HF, xb, r(w, 4 * HF, 4 * C))
         quant("xq", "xs", xa, xa + HF, r(w, 0, 4 * HF))
         send(u8(r("lq", xa, xb)), u8(r("xq", xa, xb)), "ax%d" % t, [r("xq", xa, xb)])
         send(ap(r("ls", xa, xb)), ap(r("xs", xa, xb)), "ax%d" % t, [r("xs", xa, xb)])
@@ -302,82 +282,102 @@ def rank_program(g, core, T, topo):
         if not first:
             for b in range(4):
                 mm(pd[b], "eq", "es", 128 * b, "xq", "xs", xa, xb)
-        if not first:
-            relabel(t - 1, 128, C)
+            relabel(t - 1, 128, TOP)
         dv = r("ct", 0, 4 * C, 4)
-        tt(r("aa", HF, C), r("py1", 0, C - HF), r("mx", HF, C), A.add)
+        if first:
+            tile_e(0)
+            act(r("d1", 0, C - 1), r("mx", 1, C), bias=-65024.0, scale=-65536.0 / BIG)
+            act(r("kk"), r("it16", 0, 18), bias=ck)
+            act(r("ju"), r("jl"), scale=U)
+        for a, b in ((TOP, C), (HF, TOP)):
+            tt(r("aa", a, b), r("py1", a - HF, b - HF), r("mx", a, b), A.add)
         if first:
             tile_e(1)
-        scan(r("hh", HF, C), r("hd", HF, C), r("aa", HF, C), -BIG, A.min, A.max)
+            fill(r("ct", 4 * 464, 4 * 512), 0.0)
+        else:
+            relabel(t - 1, TOP, C)
+        for a, b in ((TOP, C), (HF, TOP)):
+            scan(r("hh", a, b), r("hd", a, b), r("aa", a, b), -BIG, A.min, A.max)
         tt(r("aa", 0, HF), r("pp", 0, HF), r("mx", 0, HF), A.add)
         for m in ON_SCALAR:
             act(jview(m), r("py0", 0, 16 * m), ACT.Sign, bias=col("hh", 16 * m + 15), scale=-1.0)
         for m in ON_SCALAR:
             act(cview(m), jview(m), ACT.Relu, acc=col("rs", m))
-        for m in ORDER:
-            ts(cview(m), r("pp", 0, 16 * m), col("hh", 16 * m + 15), A.is_lt)
-            act(jview(m), cview(m), acc=col("rs", m))
-            if m == 16:
+
+        def step(name):
+            if isinstance(name, int):
+                ts(cview(name), r("pp", 0, 16 * name), col("hh", 16 * name + 15), A.is_lt)
+                act(jview(name), cview(name), acc=col("rs", name))
+            elif name == "hh":
                 scan(r("hh", 0, HF), r("hd", 0, HF), r("aa", 0, HF), -BIG, A.min, A.max)
-            if first and m == 13:
-                quant("bq", "bs", 0, 128, r("b2"))
-            if m == 15:
+            elif name == "dv":
                 tt(dv, r("hh"), r("pp", 0, C), A.is_ge)
-            if m in QUANT_AFTER:
-                a, b = QUANT_AFTER[m]
-                quant("cq", "cs", a, b, r("ct", 4 * a, 4 * b))
-            if first and m == 8:
-                quant("cq", "cs", 768, 896, r("ct", 4 * 768, 4 * 896))
-            if first and m == ORDER[3]:
-                tt(r("fl"), r("e9"), r("ju"), A.add)
-            if m == 11:
+            elif name == "dseg":
                 scan(r("dseg"), r("sd"), dv, 0.0, A.min, A.add)
-            if m == 8:
+            elif name == "adj":
                 tt(r("adj"), r("kk"), r("dseg", 15, C, 16), A.subtract)
-        for k in (0, 1, 2):
-            mm("pc", "bq", "bs", 0, "cq", "cs", CT[k], CT[k] + CW[k], start=(k == 0), stop=(k == 2))
-            mm("py1", "bq", "bs", 0, "cq", "cs", CT[k], CT[k] + 128, start=(k == 0), stop=False)
+            elif name == "q3":
+                quant("cq", "cs", 672, 800, r("ct", 4 * 672, 4 * 800))
+                for k in (3, 4):
+                    mm("py1", "bq", "bs", 0, "cq", "cs", CT[k], CT[k] + 128, start=False, stop=(k == 4))
+            elif name[0] == "q":
+                k = int(name[1])
+                quant("cq", "cs", CT[k], CT[k + 1], r("ct", 4 * CT[k], 4 * CT[k + 1]))
+                if k < 2:
+                    mm("pc", "bq", "bs", 0, "cq", "cs", CT[k], CT[k] + CW[k], start=(k == 0), stop=(k == 1))
+                mm("py0", "bq", "bs", 0, "cq", "cs", CT[k], CT[k] + 160, start=(k == 0), stop=(k == 2))
+                mm("py1", "bq", "bs", 0, "cq", "cs", CT[k], CT[k] + 128, start=(k == 0), stop=False)
+            else:
+                a, b, bank = PARTS[int(name[1])]
+                if name[0] == "d":
+                    tt(r("d1", 16 * a + 15, 16 * b, 16), r("adj", a, b), r("rs", a, b), A.subtract)
+                if name[0] == "x":
+                    scan(r("ext", 16 * a, 16 * b), r(bank, 16 * a, 16 * b), r("d1", 16 * a, 16 * b), -65024.0, A.max, A.add)
+                if name[0] == "r":
+                    ts(r("r16", a, b), r("ext", 16 * a + 15, 16 * b, 16), ccs, A.add)
+                if name[0] == "s":
+                    cp((r("zz", 64, 64 + C), r("r16", a, b)), r(src, 16 * a, 16 * b))
+
+        behind = {}
         if first:
-            for b in (1, 2, 0):
-                act(r(src, B * b, B * b + B), r("pg", B * b, B * b + B), bias=col("fl", b), scale=EPS)
-            act(col("zz", 63), q_, bias=MHI, scale=0.0)
-            act(r("thr", 0, 4), r("it16", 0, 4), bias=t3)
-        else:
-            for b in range(4):
-                own_d(b)
-        tt(r("d1", B + 15, C, 16), r("adj", 6, 18), r("rs", 6, 18), A.subtract)
+            behind = {
+                15: lambda: ts(r("e9"), r("jl"), q_, A.is_equal),
+                13: lambda: quant("bq", "bs", 0, 128, r("b2")),
+                12: lambda: tt(r("fl"), r("e9"), r("ju"), A.add),
+                "q2": lambda: ts(t0, q_, 512.0, A.mult, -7680.0, A.add),
+                "d1": lambda: (ts(cu, q_, -U, A.mult, 15 * U, A.add), ts(ccs, z0, 65024.0, A.mult, t0, A.add)),
+                "r0": lambda: ts(r("kb", 32, 64), r("gj", 0, 32), h_, A.not_equal, -4096.0, A.mult),
+                "x1": lambda: ts(r("ke"), r("i16", 0, 32), q_, A.not_equal, cu, A.mult),
+                "d2": lambda: (ts(mq, q_, -0.0625, A.mult, -MLO, A.add), ts(t3, q_, B + 0.5, A.add)),
+                "x2": lambda: (tt(r("kb", 0, 32), r("kb", 32, 64), r("ke"), A.add), ts(t4, q_, S, A.mult)),
+                "r1": lambda: tile_e(2),
+                "r2": lambda: (ts(col("kd", B), col("kb", 0), mq, A.add), tt(r("kd", B + 1, 160), r("kb", 1, 64), r("kb", 0, 63), A.subtract)),
+                "s2": lambda: (tile_e(3), ts(r("flm"), r("fl"), MLO, A.add)),
+            }
+        for name in PLAN:
+            step(name)
+            if name in behind:
+                behind[name]()
+            if name == 1 and first:
+                for b in (2, 1, 0):
+                    act(r(src, B * b, B * b + B), r("pg", B * b, B * b + B), bias=col("fl", b), scale=EPS)
+                act(col("zz", 63), q_, bias=MHI, scale=0.0)
+                act(r("d16"), r("mx", 0, 192), bias=-34.0, scale=-36.0 / BIG)
+                act(ku, q_, ACT.Sign, bias=-2.5)
         if first:
-            tile_e(2)
-        quant("cq", "cs", 672, 800, r("ct", 4 * 672, 4 * 800))
-        for k in (3, 4):
-            mm("py1", "bq", "bs", 0, "cq", "cs", CT[k], CT[k] + 128, start=False, stop=(k == 4))
-        if not first:
-            for b in range(2):
-                far_d(b)
-        scan(r("ext", B, C), r("pc", B, C), r("d1", B, C), -65024.0, A.max, A.add)
-        if first:
-            ts(r("kb", 32, 64), r("gj", 0, 32), h_, A.not_equal, -4096.0, A.mult)
-            ts(r("ke"), r("i16", 0, 32), q_, A.not_equal, cu, A.mult)
-        tt(r("d1", 15, B, 16), r("adj", 0, 6), r("rs", 0, 6), A.subtract)
-        ts(r("r16", 6, 18), r("ext", B + 15, C, 16), ccs, A.add)
-        if first:
-            tt(r("kb", 0, 32), r("kb", 32, 64), r("ke"), A.add)
-            ts(r("flm"), r("fl"), MLO, A.add)
-        scan(r("ext", 0, B), r("py1", 0, B), r("d1", 0, B), -65024.0, A.max, A.add)
-        cp((r("zz", 64, 64 + C), r("r16", 6, 18)), r(src, B, C))
-        ts(r("r16", 0, 6), r("ext", 15, B, 16), ccs, A.add)
-        if first:
-            ts(col("kd", B), col("kb", 0), mq, A.add)
-            tt(r("kd", B + 1, 160), r("kb", 1, 64), r("kb", 0, 63), A.subtract)
             act(r("d4"), r("i4"), ACT.Abs, bias=r_, scale=-1.0)
+            act(col("base", 0), ku, bias=-MHI - (GONE + B) / 2, scale=-(GONE - B) / 2)
             own_d(0, True)
             act(r("d4"), r("d4"), ACT.Sign)
+            act(r("thr", 0, 4), r("it16", 0, 4), bias=t3)
             own_d(1, True)
             act(r("d4"), r("d4"), bias=-14.0, scale=16.0)
             own_d(2, True)
-        cp((r("zz", 64, 64 + C), r("r16", 0, 6)), r(src, 0, B))
-        if first:
-            tile_e(3)
+        else:
+            for b in range(4):
+                own_d(b)
+            for b in range(2):
+                far_d(b)
         act(r("lz"), zun, ACT.Relu, bias=15 * U, scale=-1.0)
         if first:
             act(r("it4"), r("it16"), bias=t4, scale=S)
@@ -391,18 +391,21 @@ def rank_program(g, core, T, topo):
         act(r("da"), zwr, bias=col("flm", 3 + 2 * t), scale=-1.0)
         for b in range(0 if first else 2, 3):
             far_d(b)
-        act(r("dl", 0, B), r("da"), bias=-MLO)
-        far_d(3)
-        if first:
-            mm("pd3", "eq", "es", 384, "xq", "xs", xa, xb)
+        if not first:
+            act(r("dl", 0, B), r("da"), bias=-MLO)
+            far_d(3)
         scan(r("mm", 64 * t, 64 * t + 64), r("kz"), r("kt"), 0.0, A.min, A.max)
         send(T["n%d" % t][:, 0:1], ap(m2), "an%d" % t, [m2])
         ts(r("tr"), r("tx", 3, B, 4), MLO, A.add, MLO, A.subtract)
         tt(r("ep"), r("ex", 15, 192, 16), r("er"), A.subtract)
+        if first:
+            ts(ctl, q4, 4.0 * 144, A.add)
         ts(r("ind"), r("lz"), m2, A.add, m1, A.is_equal)
         tt(r("tp"), r("tx", 3, B, 4), r("tr"), A.subtract)
         ts(r("os16", la, la + 12), r("ep"), 1 / EPS, A.mult, 144.0, A.add)
         send(ap(r("ol", la, la + 12)), ap(r("os16", la, la + 12)), "al%d" % t, [r("os16", la, la + 12)])
+        if first:
+            ts(cz0, q4, S, A.mult, 4.0 * (NY - 1) * S - 6, A.add)
         scan(r("pf"), r("ind"), zer, float(B), A.add, A.add)
         ns = n4 - 2
         for k, a in ((ns, 194), (ns + 1, 0)):
@@ -414,14 +417,24 @@ def rank_program(g, core, T, topo):
         put("v", lambda: g.vector.tensor_tensor_scan(T.lc[:, 0:386], T.rl[:, 0:386], T.le[:, 385::-1], 0.0, A.add, A.max),
             [r("rl"), r("le")], [r("lc")])
         scan(r("zc", B, C), r("pf"), r("in2"), 0.0, A.max, A.min)
-        ts(dv_, m1, m2, A.subtract)
+        if first:
+            ts(cz, r_, 2.0, A.mult, cz0, A.add)
         ts(r("o4", lb, lb + ns), r("acc", 0, ns), 192.0, A.add, 0.5, A.mult)
         ts(r("o4", lb + ns, lb + n4), r("lc", 191, 386, 194), -256.0, A.mult)
         send(ap(r("op", lb, lb + n4)), ap(r("o4", lb, lb + n4)), "ap%d" % t, [r("o4", lb, lb + n4)])
+        if first:
+            far_d(3)
+            mm("pd3", "eq", "es", 384, "xq", "xs", xa, xb)
         act(r("tt", 2 * B, 4 * B), (r(w, 0, 4 * C), r("ot", 12, 24)))
         act(r("zp"), (r("zc"), r("r16")), bias=cz, scale=4.0 * S)
-        ts(e2, dv_, 0.0, A.is_equal, c1, A.mult)
+        if first:
+            fill(r("tt", 4 * B, 512), 0.0)
+            fill(r("st", 4 * K, 512), 0.0)
+            ts(c1, q_, U, A.mult, 1 - 15 * U, A.add)
+            ts(cth, q4, S, A.mult, (4.0 * (NH - 0.5) - 4 * MLO) * S, A.add)
+        ts(dv_, m1, m2, A.subtract)
         cp(r("tt", 0, 2 * B), (r(w, 0, 4 * C), r("ot", 0, 12)))
+        ts(e2, dv_, 0.0, A.is_equal, c1, A.mult)
         if first:
             ts(r("flu"), r("fl"), 15 * U, A.subtract)
             ts(r("itd"), r("it4"), 4.0 * ND * S, A.add)
@@ -448,6 +461,8 @@ def rank_program(g, core, T, topo):
         tt(r("eb"), r("ea"), r("ec"), A.add)
         quant("sq", "ss", 0, 128, r("st"))
         act(r("dl", B, C), r("ind"), scale=dl_)
+        if first:
+            act(r("dl", 0, B), r("da"), bias=-MLO)
         for b in range(4):
             act(r(w, 4 * NY + b, 4 * NH, 4), r(py[b], 0, B), scale=0.03125)
         tt(r("ed"), r("eb"), r("itd"), A.min)
@@ -465,7 +480,7 @@ def rank_program(g, core, T, topo):
         act(r(wn, 0, 4 * HF), (r(w), r("oe", 0, HF // 4)), ACT.Copy)
         if not more:
             relabel(t, 128, C)
-        if more:
+        else:
             act(b1, col("e9", 3 + 2 * t), bias=col("kr", B - 1), scale=GONE - B)
             act(sx, m2, bias=MLO + GONE)
             act(eg, dv_, ACT.Relu, bias=GONE, scale=-GONE / U)

from concourse.mybir import dt, AluOpType, ActivationFunctionType

C, B, K, R = 288, 96, 64, 3
HF = 160
TOP = 224
NY, NH, ND = 288, 384, 448
WW = 4 * (ND + C)
U, EPS = 2.0 ** -8, 2.0 ** -17
S = 2.0 ** -12
MLO, MHI = 1.5 * 2.0 ** 15, 1.5 * 2.0 ** 23
GONE = 512.0
BIG = 2.0 ** 93
CT = [0, 288, 512, 672, 768]
CW = [288, 224, 160, 128, 128]
ON_SCALAR = (17, 14, 10)
PARTS = [(10, 18, "pc"), (6, 10, "py0"), (0, 6, "py1")]
PLAN = [16, "hh", 15, 13, "dv", 12, 11, "q0", "dseg", "q1", 9, 8, "adj", 7, 6, 5, 4, "d0", "q2", 3, 2, 1,
        "x0", "d1", "q3", "r0", "x1", "d2", "s0", "r1", "x2", "s1", "r2", "s2"]
KT = [64, 48, 40]

F32, BF, I32, U16, Q4, U8 = "float32", "bfloat16", "int32", "uint16", "float8_e4m3fn_x4", "uint8"
SIZES = {
    BF: dict(w0=WW, w1=WW, dd=4 * C, ds=4 * 208, ut=512, vt=512, ones=128, ff=1040, b2=512, ct=4 * 896, junk=2448, junk2=384, tt=512,
             st=512, zer=192, lz=192, sd=C, dseg=C, ind=192, in2=192, pf=192, le=386, rl=386, lc=386, zc=C),
    Q4: dict(xq=4 * C, lq=R * C, uq=128, uq2=128, vq=128, wq=512, eq=512, bq=128, cq=896, tq=128, sq=128),
    U8: dict(xs=4 * C, ls=R * C, us=128, us2=128, vs=128, wp=512, es=512, bs=128, cs=896, ts=128, ss=128),
    I32: dict(pi=1, ci=5, oui=8),
    U16: dict(ou=8, r16=18, o4=8 * R, op=8 * R, os16=16 * R, ol=16 * R, ot=24, oe=72),
    F32: dict(n0=1, n1=1, n2=1, gj=128, ga=128, cf=5, cc=24, i16=C, i4=C, it16=72, it4=72, itd=72, ed=72, mx=C, hd=C, d1=C, d4=C, kk=18,
              thr=8, jl=10, ju=10, e9=10, fl=10, flm=10, flu=10, pg=C, src0=C, src1=C, aa=C, hh=C, rs=18, adj=18, ext=C, zz=C + 64,
              kd=160, kr=160, kt=64, kb=64, ke=32, mm=64 * R, acc=2, d16=192, ex=192, er=12, ep=12, tx=B, tr=24, tp=24, zp=C,
              zx=C, th=1, ea=72, eb=72, ec=72, da=B, dl=C, kz=64, base=4, yo=C, oba=C, obo=C),
}
SCRATCH = {n: ("sbuf", [128, k], d) for d in SIZES for n, k in SIZES[d].items()}
SCRATCH.update({n: ("psum", [128, 512], F32) for n in ("pp", "pc", "pd0", "pd1", "pd2", "pd3", "py0", "py1")})
SEMAPHORES = ["qv", "qs", "qt", "qg", "sent", "lx", "ly", "lu", "lv", "lw", "lp", "so", "sc", "sy", "sz", "s0", "s1", "s2", "s3",
              "an0", "an1", "an2", "ax0", "ax1", "ax2", "al0", "al1", "al2", "ap0", "ap1", "ap2"]
A, ACT = AluOpType, ActivationFunctionType


def _meet(a, b):
    if a[0] != b[0] or a[2] <= b[1] or b[2] <= a[1]:
        return False
    return not (a[3] == b[3] and a[3] > 1 and (a[1] - b[1]) % a[3] != 0)


def rank_program(g, core, T, topo):
    rank = T.rank_of(core)
    if rank is None:
        return
    nxt = T.cores[(rank + 1) % len(T.cores)]
    rid, pid = topo.addr(nxt)[:2]
    lanes = topo.mask(core, nxt)
    nl = len(topo.engines(core, nxt))
    nin = len(topo.engines(T.cores[rank - 1], core))
    eng = {"v": g.vector, "s": g.scalar, "t": g.tensor, "g": g, "y": g.sync}

    ops = {q: [] for q in eng}
    known = {q: {} for q in eng}
    seen = {n: [] for n in SCRATCH}
    count = {}
    sends = []

    def r(name, lo=0, hi=None, step=1):
        return (name, lo, SCRATCH[name][1][1] if hi is None else hi, step)

    def col(name, j):
        return r(name, j, j + 1)

    def ap(x):
        if len(x) == 2:
            return ap(x[0]).indirect(ap(x[1]))
        return T[x[0]][:, x[1]:x[2]:x[3]] if x[3] > 1 else T[x[0]][:, x[1]:x[2]]

    def val(x):
        return ap(x) if isinstance(x, tuple) else x

    def u8(x):
        return ap(x).bitcast(dt.uint8)

    def put(q, call, reads, writes, own=None, chain=False):
        acc = []
        for x, w in [(x, False) for x in reads if isinstance(x, tuple)] + [(x, True) for x in writes]:
            acc += [(x[0], w), (x[1], False)] if len(x) == 2 else [(x, w)]
        need = {}
        for x, w in acc:
            bank = SCRATCH[x[0]][0] == "psum"
            for y, wy, s, i, clock in seen[x[0]]:
                if chain and bank and s == q:
                    continue
                if (bank and s != q) or ((w or wy) and _meet(x, y)):
                    if known[q].get(s, -1) < i and need.get(s, (-1, None))[0] < i:
                        need[s] = (i, clock)
        waits = []
        for s, (i, clock) in sorted(need.items(), key=lambda e: -len(e[1][1])):
            if known[q].get(s, -1) >= i:
                continue
            waits.append((s, i))
            known[q][s] = i
            for k2, i2 in clock.items():
                if known[q].get(k2, -1) < i2:
                    known[q][k2] = i2
        me = (q, len(ops[q])) if own is None else (own, 0)
        ops[q].append([call, waits, own])
        for x, w in acc:
            seen[x[0]].append((x, w, me[0], me[1], dict(known[q])))

    def arrives(name, n, views):
        count[name] = n
        for x in views:
            seen[x[0]].append((x, True, name, 0, {}))

    def dma(q, sem, out, in_, reads, writes):
        count[sem] = 16
        put(q, lambda: eng[q].dma_start(out, in_), reads, writes, own=sem)

    def send(out, in_, sem, reads):
        sends.append(sem)
        put("g", lambda: g.remote_dma(out, in_, T.sem[sem], T.sem.sent, pid, rid, lanes), reads, [], own="")

    def ts(out, in0, s1, op0, s2=None, op1=None):
        if op1 is None:
            put("v", lambda: g.vector.tensor_scalar(ap(out), ap(in0), val(s1), None, op0), [in0, s1], [out])
        else:
            put("v", lambda: g.vector.tensor_scalar(ap(out), ap(in0), val(s1), val(s2), op0, op1), [in0, s1, s2], [out])

    def tt(out, a, b, op):
        put("v", lambda: g.vector.tensor_tensor(ap(out), ap(a), ap(b), op), [a, b], [out])

    def cp(out, a):
        put("v", lambda: g.vector.tensor_copy(ap(out), ap(a)), [a], [out])

    def fill(out, c):
        put("v", lambda: g.vector.memset(ap(out), c), [], [out])

    def scan(out, d0, d1, init, op0, op1):
        put("v", lambda: g.vector.tensor_tensor_scan(ap(out), ap(d0), ap(d1), val(init), op0, op1), [d0, d1, init], [out])

    def quant(qn, sn, lo, hi, tile):
        put("v", lambda: g.vector.quantize_mx(ap(r(qn, lo, hi)), ap(r(sn, lo, hi)), ap(tile)), [tile], [r(qn, lo, hi), r(sn, lo, hi)])

    def act(out, a, func=ACT.Identity, bias=0.0, scale=1.0, acc=None):
        if acc is None:
            put("s", lambda: g.scalar.activation(ap(out), ap(a), func, bias=val(bias), scale=val(scale)), [a, bias, scale], [out])
        else:
            put("s", lambda: g.scalar.activation(ap(out), ap(a), func, bias=val(bias), scale=val(scale), accum_out=ap(acc)), [a, bias, scale], [out, acc])

    def mm(bank, wn, ws_, w0, xn, xs_, lo, hi, start=True, stop=True):
        a = [r(wn, w0, w0 + 128), r(ws_, w0, w0 + 128), r(xn, lo, hi), r(xs_, lo, hi)]
        o = r(bank, 0, hi - lo)
        put("t", lambda: g.tensor.matmul_mx(ap(o), ap(a[0]), ap(a[1]), ap(a[2]), ap(a[3]), start, stop), a, [o], chain=not start)

    def iota(out, pattern, base, cm=0):
        if SCRATCH[out[0]][2] == I32:
            put("g", lambda: g.iota(ap(out), pattern, base, cm), [], [out])
        else:
            put("g", lambda: g.iota(ap(out), pattern, base, cm, allow_small_or_imprecise_dtypes=True), [], [out])

    def ident(out):
        put("g", lambda: g.affine_select(ap(out), T.ones[:, 0:128], [[-1, 128]], A.is_equal, 0.0, 0, 1), [r("ones")], [out])

    for t in range(R):
        arrives("an%d" % t, nin, [r("n%d" % t)])
        arrives("ax%d" % t, 2 * nin, [r("lq", C * t, C * t + C), r("ls", C * t, C * t + C)])
        arrives("al%d" % t, nin, [r("ol", 16 * t, 16 * t + 16)])
        arrives("ap%d" % t, nin, [r("op", 8 * t, 8 * t + 8)])

    xhi, xlo = r("w0", 4 * HF, 4 * C), r("w0", 0, 4 * HF)
    dma("y", "lx", ap(xhi), T.x[:, 4 * HF:4 * C], [], [xhi])
    dma("s", "lu", T.ut[:], T.u[:], [], [r("ut")])
    dma("y", "ly", ap(xlo), T.x[:, 0:4 * HF], [], [xlo])
    dma("y", "lw", u8(r("wq")), T.wc[:], [xlo], [r("wq")])
    dma("y", "lp", T.wp[:], T.ws[:], [], [r("wp")])
    dma("y", "lv", T.vt[:], T.v[:], [], [r("vt")])

    q_, h_, r_, q4, g_ = (col("cf", j) for j in range(5))
    mq, z0, t0, ccs, ck, ku, ctl, cz0, cz, cth, t1, cu, c1, t3, t4, dv_, e2, fv, dl_, eg, b1, b2_, sx = (col("cc", j) for j in range(23))
    zer, zwr, zun = r("zer"), r("zz", 64, 64 + B), r("zz", 64 + B, 64 + C)
    fill(r("ones"), 1.0)
    fill(r("ff", 0, 520), 0.0)
    iota(r("oui"), [[16, 8]], 0)
    iota(r("pi"), [[0, 1]], 0, 1)
    iota(r("i16"), [[0, 18], [1, 16]], 0)
    iota(r("gj"), [[1, 8], [0, 16]], 0)
    act(r("ff", 520, 1040), r("ff", 0, 520), ACT.Copy)
    ident(r("ff", 2, 514, 4))
    ident(r("ff", 523, 1035, 4))
    iota(r("it16"), [[16, 72]], 0)
    iota(r("jl"), [[1, 10]], 0)
    iota(r("ct", 4 * 624, 4 * 672), [[0, 192]], 0)

    def late_rows():
        iota(r("sd"), [[0, 18], [1, 16]], 0)
        iota(r("pg"), [[1, C]], -144)
        iota(r("i4"), [[0, 72], [1, 4]], 0)
        iota(r("zz", 0, 63), [[0, 63]], 0)
        iota(r("kd", 0, B), [[0, B]], 0)
        iota(r("kz"), [[0, 2], [30000, 32]], -70000)
        iota(zer, [[0, 192]], 0)
        iota(r("ds", 192, 4 * 208, 208), [[0, 4]], 0)
        iota(r("zc", 0, B), [[1, B]], 1)
        iota(r("le", 192, 194), [[0, 2]], 0)
        iota(r("rl"), [[0, 386]], 0)
        put("g", lambda: g.affine_select(T.rl[:, 0:386], T.rl[:, 0:386], [[0, 386]], A.is_gt, -1.0 / 256, 0, 0), [r("rl")], [r("rl")])

    def tile_e(b):
        a = (2, 522, 0, 520)[b]
        quant("eq", "es", 128 * b, 128 * b + 128, r("ff", a, a + 512))

    cp(r("ou"), r("oui"))
    fill(r("ct", 4 * 240, 4 * 288), 0.0)
    fill(col("rs", 0), 0.0)
    ts(col("ci", 0), r("pi"), 15, A.bitwise_and)
    ts(col("ci", 1), r("pi"), 4, A.logical_shift_right, 1, A.bitwise_and)
    ts(col("ci", 2), r("pi"), 2, A.logical_shift_right, 3, A.bitwise_and)
    ts(col("ci", 3), r("pi"), 3, A.bitwise_and)
    ts(col("ci", 4), r("pi"), 4, A.logical_shift_right)
    fill(r("ct", 4 * 720, 4 * 896), 0.0)
    cp(r("cf"), r("ci"))
    quant("uq", "us", 0, 128, r("ut"))
    quant("cq", "cs", 768, 896, r("ct", 4 * 768, 4 * 896))
    put("v", lambda: g.vector.tensor_copy(T.uq2[:, 0:128].bitcast(dt.uint32), T.uq[:, 0:128].bitcast(dt.uint32).indirect(T.ou[:, 0:8])),
        [r("uq"), r("ou")], [r("uq2")])
    quant("xq", "xs", HF, C, xhi)
    ts(r("mx"), r("i16"), q_, A.not_equal, -BIG, A.mult)
    act(r("hd"), r("i16"), bias=-0.5 * BIG, scale=BIG)
    put("s", lambda: g.scalar.activation(T.us2[:, 0:128], T.us[:, 0:128].indirect(T.ou[:, 0:8]), ACT.Copy), [r("us"), r("ou")], [r("us2")])
    act(r("ga"), r("gj"), ACT.Abs, bias=g_, scale=-1.0)
    act(z0, q_, ACT.Relu, bias=1.0, scale=-1.0)
    act(t1, q_, bias=15.0, scale=-1.0)
    for b in range(4):
        act(r("b2", b, 512, 4), r("ga"), ACT.Relu, bias=1.0, scale=-1.0)
    act(ck, z0, bias=t1, scale=-65024.0)

    pd = ["pd0", "pd1", "pd2", "pd3"]
    py = ["py0", "py1", "pp", "pc"]

    def relabel(t, a, b):
        tt(r("src%d" % ((t + 1) % 2), a, b), (r("dl"), r("r16", a // 16, b // 16)), r("src%d" % (t % 2), a, b), A.add)

    def cview(m):
        k = (18 - m) // 4
        return r("ct", 4 * CT[k] + (18 - m) % 4, 4 * (CT[k] + 16 * m), 4)

    def jview(m):
        return r("junk", 8 * m * (m - 1), 8 * m * (m + 1))

    for t in range(R):
        w, wn = "w%d" % (t % 2), "w%d" % ((t + 1) % 2)
        src = "src%d" % (t % 2)
        more, first = t < R - 1, t == 0
        m1, m2 = col("mm", 64 * t + 31), col("mm", 64 * t + 63)
        xa, xb = C * t, C * t + C
        kt, la, lb = KT[t], 16 * t, 8 * t
        n4 = (kt + 15) // 16

        def own_d(b, product=False):
            if product:
                mm(pd[b], "eq", "es", 128 * b, "xq", "xs", xa, xb)
            act(r(w, 4 * ND + b, WW, 4), r(pd[b], 0, C), ACT.Copy)

        def far_d(b):
            mm(pd[b], "eq", "es", 128 * b, "lq", "ls", xa, xb)
            act(r("dd", C * b, C * b + C), r(pd[b], 0, C), ACT.Copy)

        def sort_d(b, call):
            call(r("ds", 208 * b, 208 * b + 192), (r("dd", C * b, C * b + C), r("ol", la, la + 12)))

        def pick_s(b, call):
            call(r("st", b, 64 * n4, 4), (r("ds", 208 * b, 208 * b + 193), r("op", lb, lb + n4)))

        if not first:
            quant("xq", "xs", xa + HF, xb, r(w, 4 * HF, 4 * C))
        quant("xq", "xs", xa, xa + HF, r(w, 0, 4 * HF))
        send(u8(r("lq", xa, xb)), u8(r("xq", xa, xb)), "ax%d" % t, [r("xq", xa, xb)])
        send(ap(r("ls", xa, xb)), ap(r("xs", xa, xb)), "ax%d" % t, [r("xs", xa, xb)])
        if first:
            late_rows()
        mm("py1", "uq2", "us2", 0, "xq", "xs", xa + HF, xb)
        mm("pp", "uq2", "us2", 0, "xq", "xs", xa, xb)
        mm("py0", "uq2", "us2", 0, "xq", "xs", xa, xb)
        if not first:
            for b in range(4):
                mm(pd[b], "eq", "es", 128 * b, "xq", "xs", xa, xb)
            relabel(t - 1, 128, TOP)
        dv = r("ct", 0, 4 * C, 4)
        if first:
            tile_e(0)
            act(r("d1", 0, C - 1), r("mx", 1, C), bias=-65024.0, scale=-65536.0 / BIG)
            act(r("kk"), r("it16", 0, 18), bias=ck)
            act(r("ju"), r("jl"), scale=U)
        for a, b in ((TOP, C), (HF, TOP)):
            tt(r("aa", a, b), r("py1", a - HF, b - HF), r("mx", a, b), A.add)
        if first:
            tile_e(1)
            fill(r("ct", 4 * 464, 4 * 512), 0.0)
        else:
            relabel(t - 1, TOP, C)
        for a, b in ((TOP, C), (HF, TOP)):
            scan(r("hh", a, b), r("hd", a, b), r("aa", a, b), -BIG, A.min, A.max)
        tt(r("aa", 0, HF), r("pp", 0, HF), r("mx", 0, HF), A.add)
        for m in ON_SCALAR:
            act(jview(m), r("py0", 0, 16 * m), ACT.Sign, bias=col("hh", 16 * m + 15), scale=-1.0)
        for m in ON_SCALAR:
            act(cview(m), jview(m), ACT.Relu, acc=col("rs", m))

        def step(name):
            if isinstance(name, int):
                ts(cview(name), r("pp", 0, 16 * name), col("hh", 16 * name + 15), A.is_lt)
                act(jview(name), cview(name), acc=col("rs", name))
            elif name == "hh":
                scan(r("hh", 0, HF), r("hd", 0, HF), r("aa", 0, HF), -BIG, A.min, A.max)
            elif name == "dv":
                tt(dv, r("hh"), r("pp", 0, C), A.is_ge)
            elif name == "dseg":
                scan(r("dseg"), r("sd"), dv, 0.0, A.min, A.add)
            elif name == "adj":
                tt(r("adj"), r("kk"), r("dseg", 15, C, 16), A.subtract)
            elif name == "q3":
                quant("cq", "cs", 672, 800, r("ct", 4 * 672, 4 * 800))
                for k in (3, 4):
                    mm("py1", "bq", "bs", 0, "cq", "cs", CT[k], CT[k] + 128, start=False, stop=(k == 4))
            elif name[0] == "q":
                k = int(name[1])
                quant("cq", "cs", CT[k], CT[k + 1], r("ct", 4 * CT[k], 4 * CT[k + 1]))
                if k < 2:
                    mm("pc", "bq", "bs", 0, "cq", "cs", CT[k], CT[k] + CW[k], start=(k == 0), stop=(k == 1))
                mm("py0", "bq", "bs", 0, "cq", "cs", CT[k], CT[k] + 160, start=(k == 0), stop=(k == 2))
                mm("py1", "bq", "bs", 0, "cq", "cs", CT[k], CT[k] + 128, start=(k == 0), stop=False)
            else:
                a, b, bank = PARTS[int(name[1])]
                if name[0] == "d":
                    tt(r("d1", 16 * a + 15, 16 * b, 16), r("adj", a, b), r("rs", a, b), A.subtract)
                if name[0] == "x":
                    scan(r("ext", 16 * a, 16 * b), r(bank, 16 * a, 16 * b), r("d1", 16 * a, 16 * b), -65024.0, A.max, A.add)
                if name[0] == "r":
                    ts(r("r16", a, b), r("ext", 16 * a + 15, 16 * b, 16), ccs, A.add)
                if name[0] == "s":
                    cp((r("zz", 64, 64 + C), r("r16", a, b)), r(src, 16 * a, 16 * b))

        behind = {}
        if first:
            behind = {
                15: lambda: ts(r("e9"), r("jl"), q_, A.is_equal),
                13: lambda: quant("bq", "bs", 0, 128, r("b2")),
                12: lambda: tt(r("fl"), r("e9"), r("ju"), A.add),
                "q2": lambda: ts(t0, q_, 512.0, A.mult, -7680.0, A.add),
                "d1": lambda: (ts(cu, q_, -U, A.mult, 15 * U, A.add), ts(ccs, z0, 65024.0, A.mult, t0, A.add)),
                "r0": lambda: ts(r("kb", 32, 64), r("gj", 0, 32), h_, A.not_equal, -4096.0, A.mult),
                "x1": lambda: ts(r("ke"), r("i16", 0, 32), q_, A.not_equal, cu, A.mult),
                "d2": lambda: (ts(mq, q_, -0.0625, A.mult, -MLO, A.add), ts(t3, q_, B + 0.5, A.add)),
                "x2": lambda: (tt(r("kb", 0, 32), r("kb", 32, 64), r("ke"), A.add), ts(t4, q_, S, A.mult)),
                "r1": lambda: tile_e(2),
                "r2": lambda: (ts(col("kd", B), col("kb", 0), mq, A.add), tt(r("kd", B + 1, 160), r("kb", 1, 64), r("kb", 0, 63), A.subtract)),
                "s2": lambda: (tile_e(3), ts(r("flm"), r("fl"), MLO, A.add)),
            }
        for name in PLAN:
            step(name)
            if name in behind:
                behind[name]()
            if name == 1 and first:
                for b in (2, 1, 0):
                    act(r(src, B * b, B * b + B), r("pg", B * b, B * b + B), bias=col("fl", b), scale=EPS)
                act(col("zz", 63), q_, bias=MHI, scale=0.0)
                act(r("d16"), r("mx", 0, 192), bias=-34.0, scale=-36.0 / BIG)
                act(ku, q_, ACT.Sign, bias=-2.5)
        if first:
            act(r("d4"), r("i4"), ACT.Abs, bias=r_, scale=-1.0)
            act(col("base", 0), ku, bias=-MHI - (GONE + B) / 2, scale=-(GONE - B) / 2)
            own_d(0, True)
            act(r("d4"), r("d4"), ACT.Sign)
            act(r("thr", 0, 4), r("it16", 0, 4), bias=t3)
            own_d(1, True)
            act(r("d4"), r("d4"), bias=-14.0, scale=16.0)
            own_d(2, True)
        else:
            for b in range(4):
                own_d(b)
            for b in range(2):
                far_d(b)
        act(r("lz"), zun, ACT.Relu, bias=15 * U, scale=-1.0)
        if first:
            act(r("it4"), r("it16"), bias=t4, scale=S)
            act(r("thr", 4, 8), r("thr", 0, 4), bias=B - 0.5, scale=-1.0)
        put("v", lambda t=t: g.vector.tensor_tensor_scan(T.kr[:, 0:160], T.zz[:, 159::-1], T.kd[:, 0:160], T.base[:, t:t + 1], A.add, A.add),
            [r("zz", 0, 160), r("kd"), col("base", t)], [r("kr")])
        scan(r("ex"), r("d16"), zun, 0.0, A.add, A.max)
        put("v", lambda: g.vector.transpose(T.kt[:, 0:64], T.kr[:, B:160]), [r("kr", B, 160)], [r("kt")])
        scan(r("tx"), r("d4", 0, B), zwr, 0.0, A.add, A.max)
        ts(r("er"), r("ex", 15, 192, 16), MLO, A.add, MLO, A.subtract)
        act(r("da"), zwr, bias=col("flm", 3 + 2 * t), scale=-1.0)
        for b in range(0 if first else 2, 3):
            far_d(b)
        if not first:
            act(r("dl", 0, B), r("da"), bias=-MLO)
            far_d(3)
        scan(r("mm", 64 * t, 64 * t + 64), r("kz"), r("kt"), 0.0, A.min, A.max)
        send(T["n%d" % t][:, 0:1], ap(m2), "an%d" % t, [m2])
        ts(r("tr"), r("tx", 3, B, 4), MLO, A.add, MLO, A.subtract)
        tt(r("ep"), r("ex", 15, 192, 16), r("er"), A.subtract)
        if first:
            ts(ctl, q4, 4.0 * 144, A.add)
        ts(r("ind"), r("lz"), m2, A.add, m1, A.is_equal)
        tt(r("tp"), r("tx", 3, B, 4), r("tr"), A.subtract)
        ts(r("os16", la, la + 12), r("ep"), 1 / EPS, A.mult, 144.0, A.add)
        send(ap(r("ol", la, la + 12)), ap(r("os16", la, la + 12)), "al%d" % t, [r("os16", la, la + 12)])
        if first:
            ts(cz0, q4, S, A.mult, 4.0 * (NY - 1) * S - 6, A.add)
        scan(r("pf"), r("ind"), zer, float(B), A.add, A.add)
        ns = n4 - 2
        for k, a in ((ns, 194), (ns + 1, 0)):
            scan(r("le", a, a + 192), r("ind"), zer, col("thr", 4 + k), A.add, A.min)
        for k in range(ns):
            act(r("junk2", 192 * k, 192 * k + 192), r("pf"), ACT.Sign, bias=col("thr", k), scale=-1.0, acc=col("acc", k))
        ts(r("ot"), r("tp"), 2.0 ** 19, A.mult, ctl, A.add)
        ts(r("in2"), r("ind"), 1024.0, A.mult, 512.0, A.subtract)
        put("v", lambda: g.vector.tensor_tensor_scan(T.lc[:, 0:386], T.rl[:, 0:386], T.le[:, 385::-1], 0.0, A.add, A.max),
            [r("rl"), r("le")], [r("lc")])
        scan(r("zc", B, C), r("pf"), r("in2"), 0.0, A.max, A.min)
        if first:
            ts(cz, r_, 2.0, A.mult, cz0, A.add)
        ts(r("o4", lb, lb + ns), r("acc", 0, ns), 192.0, A.add, 0.5, A.mult)
        ts(r("o4", lb + ns, lb + n4), r("lc", 191, 386, 194), -256.0, A.mult)
        send(ap(r("op", lb, lb + n4)), ap(r("o4", lb, lb + n4)), "ap%d" % t, [r("o4", lb, lb + n4)])
        if first:
            far_d(3)
            mm("pd3", "eq", "es", 384, "xq", "xs", xa, xb)
        act(r("tt", 2 * B, 4 * B), (r(w, 0, 4 * C), r("ot", 12, 24)))
        act(r("zp"), (r("zc"), r("r16")), bias=cz, scale=4.0 * S)
        if first:
            fill(r("tt", 4 * B, 512), 0.0)
            fill(r("st", 4 * K, 512), 0.0)
            ts(c1, q_, U, A.mult, 1 - 15 * U, A.add)
            ts(cth, q4, S, A.mult, (4.0 * (NH - 0.5) - 4 * MLO) * S, A.add)
        ts(dv_, m1, m2, A.subtract)
        cp(r("tt", 0, 2 * B), (r(w, 0, 4 * C), r("ot", 0, 12)))
        ts(e2, dv_, 0.0, A.is_equal, c1, A.mult)
        if first:
            ts(r("flu"), r("fl"), 15 * U, A.subtract)
            ts(r("itd"), r("it4"), 4.0 * ND * S, A.add)
        if not more:
            quant("vq", "vs", 0, 128, r("vt"))
        ts(fv, e2, dv_, A.subtract)
        quant("tq", "ts", 0, 128, r("tt"))
        for b in range(4):
            mm(py[b], "wq", "wp", 128 * b, "tq", "ts", 0, 128)
        ts(dl_, fv, -1.0, A.mult, col("flu", 4 + 2 * t), A.add)
        scan(r("zx"), r("d4"), r("zp"), 0.0, A.add, A.max)
        if first:
            own_d(3)
        for b in range(1, 4):
            sort_d(b, act)
        ts(r("th"), r("n%d" % t), -4.0 * S, A.mult, cth, A.add)
        sort_d(0, cp)
        x = r("zx", 3, C, 4)
        tt(r("ec"), x, r("it4"), A.max)
        ts(r("ea"), x, r("th"), A.is_gt)
        for b in (0, 1):
            pick_s(b, cp)
            pick_s(b + 2, act)
        tt(r("eb"), r("ea"), r("ec"), A.add)
        quant("sq", "ss", 0, 128, r("st"))
        act(r("dl", B, C), r("ind"), scale=dl_)
        if first:
            act(r("dl", 0, B), r("da"), bias=-MLO)
        for b in range(4):
            act(r(w, 4 * NY + b, 4 * NH, 4), r(py[b], 0, B), scale=0.03125)
        tt(r("ed"), r("eb"), r("itd"), A.min)
        relabel(t, 0, 128)
        ts(r("oe"), r("ed"), 1 / S, A.mult)
        for b in (0, 2, 1, 3):
            mm(pd[b], "wq", "wp", 128 * b, "sq", "ss", 0, 128)
        for b in (0, 2, 1, 3):
            o = r(w, 4 * NH + b, 4 * (NH + kt), 4)
            if b < 2:
                ts(o, r(pd[b], 0, kt), 0.03125, A.mult)
            else:
                act(o, r(pd[b], 0, kt), scale=0.03125)
        cp(r(wn, 4 * HF, 4 * C), (r(w), r("oe", HF // 4, 72)))
        act(r(wn, 0, 4 * HF), (r(w), r("oe", 0, HF // 4)), ACT.Copy)
        if not more:
            relabel(t, 128, C)
        else:
            act(b1, col("e9", 3 + 2 * t), bias=col("kr", B - 1), scale=GONE - B)
            act(sx, m2, bias=MLO + GONE)
            act(eg, dv_, ACT.Relu, bias=GONE, scale=-GONE / U)
            act(b2_, col("e9", 4 + 2 * t), bias=b1, scale=sx)
            act(col("base", t + 1), eg, bias=b2_, scale=-1.0)

    xa, xb = R * C, R * C + C
    w = "w%d" % (R % 2)
    quant("xq", "xs", xa + HF, xb, r(w, 4 * HF, 4 * C))
    quant("xq", "xs", xa, xa + HF, r(w, 0, 4 * HF))
    act(r("oba"), r("src%d" % (R % 2)), bias=MHI, scale=1 / U)
    act(r("obo"), r("oba"), bias=-MHI)
    mm("pc", "vq", "vs", 0, "xq", "xs", xa + HF, xb)
    mm("pp", "vq", "vs", 0, "xq", "xs", xa, xa + HF)
    dma("y", "sc", T.oc[:], u8(r("xq", xa, xb)), [r("xq", xa, xb)], [])
    cp(r("yo", HF, C), r("pc", 0, C - HF))
    cp(r("yo", 0, HF), r("pp", 0, HF))
    for k in range(4):
        dma("y", "s%d" % k, T.osc[4 * k:4 * k + 4, :], T.xs[32 * k:32 * k + 4, xa:xb], [r("xs", xa, xb)], [])
    dma("y", "so", T.ob[:], T.obo[15:128:16, :], [r("obo")], [])
    dma("s", "sz", T.y[:, HF:C], T.yo[:, HF:C], [r("yo", HF, C)], [])
    dma("s", "sy", T.y[:, 0:HF], T.yo[:, 0:HF], [r("yo", 0, HF)], [])

    marked = {q: sorted({i for p in ops for o in ops[p] for s, i in o[1] if s == q}) for q in eng}
    for q in eng:
        for i, (call, waits, own) in enumerate(ops[q]):
            for s, j in waits:
                if s in eng:
                    eng[q].wait_ge(T.sem["q" + s], marked[s].index(j) + 1)
                else:
                    eng[q].wait_ge(T.sem[s], count[s])
            ins = call()
            if own:
                ins.then_inc(T.sem[own], 16)
            elif own is None and i in marked[q]:
                ins.then_inc(T.sem["q" + q], 1)
    g.wait_ge(T.sem.sent, nl * len(sends))
    for s in ("so", "sc", "sy", "sz", "s0", "s1", "s2", "s3"):
        g.sync.wait_ge(T.sem[s], 16)
